import numpy as np
import ml_dtypes


def mxq(x, axis, fmt="e4m3"):
    dtype, down = {"e4m3": (ml_dtypes.float8_e4m3fn, 7), "e5m2": (ml_dtypes.float8_e5m2, 14)}[fmt]
    v = np.moveaxis(np.asarray(x, np.float32).astype(ml_dtypes.bfloat16).astype(np.float64), axis, -1)
    blocks = v.reshape(v.shape[:-1] + (-1, 32))
    amax = np.abs(blocks).max(-1, keepdims=True)
    byte = np.maximum(np.where(amax > 0, np.frexp(amax)[1] - 1 + 127, 0) - down, 1)
    scale = np.exp2(byte - 127.0)
    codes = (blocks / scale).astype(np.float32).astype(dtype).astype(np.float64)
    return np.moveaxis((codes * scale).reshape(v.shape), -1, axis)


WIDE = False


def mx_kscale(k):
    if not WIDE:
        return np.ones(k)
    levels = np.array([10, -10, 5, -5, 0])
    if k % 512:
        return np.exp2(np.random.permutation(np.resize(levels, k // 32))).repeat(32)
    a = np.empty((k // 512, 16))
    for p in range(k // 512):
        a[p, :8] = np.random.permutation(np.resize(levels, 8))
        for g in range(8):
            far = levels[np.abs(levels - a[p, g]) >= 10]
            a[p, g + 8] = far[np.random.randint(len(far))]
    return np.exp2(a.ravel()).repeat(32)


def f64(x):
    return np.asarray(x).astype(np.float64)


def striped(idx):
    return np.tile(idx.reshape(-1, 16).T, (8, 1)).astype(np.uint16)


def unstriped(offs):
    return offs[:16].T.reshape(-1).astype(np.int64)


E2M1 = np.array([0.0, 0.5, 1.0, 1.5, 2.0, 3.0, 4.0, 6.0, -0.0, -0.5, -1.0, -1.5, -2.0, -3.0, -4.0, -6.0])


def pack_weight(w, fmt):
    k, n = w.shape
    w = f64(np.asarray(w, np.float32).astype(ml_dtypes.bfloat16)).reshape(k // 32, 32, n)
    amax = np.abs(w).max(1)
    if fmt == "e4m3":
        byte = np.frexp(amax)[1] - 1 + 127 - 7
    else:
        mant, ex = np.frexp(amax / 6.0)
        byte = np.where(mant > 0.5, ex, ex - 1) + 127
    byte = np.clip(np.where(amax > 0, byte, 1), 1, 254)
    scaled = (w * np.exp2(127.0 - byte)[:, None, :]).reshape(k, n).astype(np.float32)
    by_word = np.ascontiguousarray(scaled.reshape(k // 512, 128, 4, n).transpose(0, 1, 3, 2))
    if fmt == "e4m3":
        words = by_word.astype(ml_dtypes.float8_e4m3fn).view(np.uint8)
    else:
        c = by_word.astype(ml_dtypes.float4_e2m1fn).view(np.uint8) & 0xF
        words = (c[..., 0::2] | (c[..., 1::2] << 4)).reshape(k // 512, 128, 2 * n)
    return np.ascontiguousarray(words), np.ascontiguousarray(byte.astype(np.uint8).reshape(k // 512, 16, n))


def unpack_weight(words, scales, fmt):
    g, _, n = scales.shape
    words = np.ascontiguousarray(words).reshape(g, 128, n, -1)
    if fmt == "e4m3":
        vals = words.view(ml_dtypes.float8_e4m3fn).astype(np.float64)
    else:
        nib = np.empty((g, 128, n, 4), np.uint8)
        nib[..., 0::2] = words & 0xF
        nib[..., 1::2] = words >> 4
        vals = E2M1[nib]
    vals = vals * np.repeat(np.exp2(scales.astype(np.float64) - 127.0), 8, axis=1)[..., None]
    return vals.transpose(0, 1, 3, 2).reshape(g * 512, n)


def gelu(v):
    return 0.5 * v * (1.0 + np.tanh(np.sqrt(2.0 / np.pi) * (v + 0.044715 * v**3)))


def bf(x):
    return np.asarray(x, np.float32).astype(ml_dtypes.bfloat16)

def planes(Y):
    n, m = Y.shape
    b = f64(bf(Y)).reshape(n // 32, 32, m)
    amax = np.abs(b).max(1)
    byte = np.clip(np.where(amax > 0, np.frexp(amax)[1] - 1 + 127 - 7, 1), 1, 254)
    codes = (b * np.exp2(127.0 - byte)[:, None, :]).reshape(n, m).astype(np.float32).astype(ml_dtypes.float8_e4m3fn).view(np.uint8)
    words = codes.reshape(n // 512, 128, 4, m).transpose(0, 1, 3, 2)
    return np.ascontiguousarray(words), np.ascontiguousarray(byte.astype(np.uint8).reshape(n // 512, 16, m))


K, T, S, P, H, N = 1024, 4096, 1024, 512, 1536, 1024

def setup_inputs():
    n = np.random.standard_normal
    s = mx_kscale(K)[:, None]
    u = mx_kscale(H)[:, None]
    tab_words, tab_scales = pack_weight(n((K, T)) * s, "e4m3")
    amp = np.exp(0.8 * n(N))
    w2_words, w2_scales = pack_weight(n((H, N)) * amp[None, :] / np.sqrt(H) / u, "e2m1")
    pairs = np.random.permutation(S)
    return {
        "tab_words": tab_words, "tab_scales": tab_scales,
        "offs": striped(np.random.permutation(T)[:S]),
        "pos1": striped(pairs[:P]),
        "pos2": striped(pairs[P:]),
        "w1": (0.7 * n((K, H)) / np.sqrt(K) / s).astype(np.float32),
        "gain": (np.exp(0.3 * n(H)) * u[:, 0]).astype(np.float32),
        "w2_words": w2_words, "w2_scales": w2_scales,
        "bias": (0.3 * amp * n(N)).astype(np.float32),
    }

def reference(tab_words, tab_scales, offs, pos1, pos2, w1, gain, w2_words, w2_scales, bias):
    v = unpack_weight(tab_words, tab_scales, "e4m3")[:, unstriped(offs)]
    h = mxq(f64(w1), 0, "e4m3").T @ v
    a = h[:, unstriped(pos1)]
    b = h[:, unstriped(pos2)]
    e = np.minimum(np.maximum(a - b, -1.0), 1.0)
    z = f64(gain)[:, None] * e
    w2 = unpack_weight(w2_words, w2_scales, "e2m1")
    y = (w2.T @ mxq(z, 0, "e4m3")) + f64(bias)[:, None]
    words, scales = planes(y)
    return y, words, scales

@@ -1,0 +1,416 @@
+from contextlib import ExitStack
+
+import concourse.mybir as mybir
+
+K, T, S, PAIRS, H, N = 1024, 4096, 1024, 512, 1536, 1024
+FLOPS = 2 * K * H * S + 2 * H * N * PAIRS
+
+F32 = mybir.dt.float32
+BF16 = mybir.dt.bfloat16
+I32 = mybir.dt.int32
+U32 = mybir.dt.uint32
+U16 = mybir.dt.uint16
+U8 = mybir.dt.uint8
+FP8X4 = mybir.dt.float8_e4m3fn_x4
+FP4X4 = mybir.dt.float4_e2m1fn_x4
+ALU = mybir.AluOpType
+ACT = mybir.ActivationFunctionType
+
+P = 128
+PACK = 4
+KP = P * PACK
+A_PASSES = K // KP
+B_PASSES = H // KP
+GROUPS = N // KP
+QUARTER = 128
+QUARTERS = PAIRS // QUARTER
+LAST_PIECES = ((0, 256), (256, 128), (384, 128))
+
+
+def tile_list_clamped_landmark_differences_kernel(
+    tc, tab_words, tab_scales, offs, pos1, pos2, w1, gain, w2_words, w2_scales, bias, out_0, out_1, out_2
+):
+    nc = tc.nc
+    with ExitStack() as ctx:
+        keep = ctx.enter_context(tc.tile_pool(name="keep", bufs=1))
+        ring = ctx.enter_context(tc.tile_pool(name="ring", bufs=2))
+        psum = ctx.enter_context(tc.psum_pool(name="psum", bufs=1))
+
+        offs_sb = keep.tile([P, S // 16], U16, name="offs_sb")
+        pos1_sb = keep.tile([P, PAIRS // 16], U16, name="pos1_sb")
+        pos2_sb = keep.tile([P, PAIRS // 16], U16, name="pos2_sb")
+        tabs = keep.tile([P, T], U8, name="tabs", tag="slot_c")
+        w2w_raw = keep.tile([P, B_PASSES * 2 * N], U8, name="w2w_raw")
+        w2s_raw = keep.tile([P, B_PASSES * N], U8, name="w2s_raw")
+        w2w = keep.tile([P, B_PASSES * 2 * N], U8, name="w2w", align_bytes=64)
+        w2s = keep.tile([P, B_PASSES * N], U8, name="w2s", align_bytes=64)
+        gain_sb = keep.tile([P, B_PASSES, PACK], F32, name="gain_sb")
+        bias_sb = keep.tile([P, GROUPS, PACK], F32, name="bias_sb")
+        vw = [keep.tile([P, S], U32, name="vw%d" % a, align_bytes=64) for a in range(A_PASSES)]
+        vs = keep.tile([P, S], U8, name="vs", align_bytes=64)
+        ys = keep.tile([P, GROUPS * PAIRS], U8, name="ys", align_bytes=64)
+
+        nc.vector.memset(w2s_raw[:].bitcast(I32), 0)
+        nc.vector.memset(tabs[:].bitcast(I32), 0)
+
+        w1_raw = {}
+        tabw = {}
+
+        def load_w1(b, a, tag):
+            raw = keep.tile([P, PACK, KP], F32, name="w1_raw", tag=tag)
+            nc.sync.dma_start(
+                out=raw[:],
+                in_=w1[KP * a : KP * (a + 1), KP * b : KP * (b + 1)].rearrange("(p j) c -> p j c", j=PACK),
+            )
+            w1_raw[b, a] = raw
+
+        def load_table(a, tag):
+            tabw[a] = keep.tile([P, T], I32, name="tabw", tag=tag)
+            nc.sync.dma_start(out=tabw[a][:], in_=tab_words[a].rearrange("p t i -> p (t i)").bitcast(I32))
+
+        nc.sync.dma_start(offs_sb[:], offs)
+        nc.sync.dma_start(
+            out=w2w_raw[:].bitcast(I32).rearrange("p (b c) -> p b c", b=B_PASSES),
+            in_=w2_words.bitcast(I32).rearrange("b p c -> p b c"),
+        )
+        for quad in range(4):
+            nc.sync.dma_start(
+                out=w2s_raw[32 * quad : 32 * quad + 4, :].bitcast(I32).rearrange("p (b c) -> p b c", b=B_PASSES),
+                in_=w2_scales[:, 4 * quad : 4 * quad + 4, :].bitcast(I32).rearrange("b r c -> r b c"),
+            )
+        load_table(0, "slot_b")
+        for quad in range(4):
+            nc.sync.dma_start(
+                out=tabs[32 * quad : 32 * quad + 4 * A_PASSES, :].bitcast(I32),
+                in_=tab_scales[:, 4 * quad : 4 * quad + 4, :].bitcast(I32),
+            )
+        load_table(1, "slot_a")
+        load_w1(0, 0, "slot_d")
+        load_w1(0, 1, "slot_e")
+        nc.sync.dma_start(pos2_sb[:], pos2)
+        nc.sync.dma_start(pos1_sb[:], pos1)
+
+        nc.vector.tensor_copy(
+            out=w2w[:].bitcast(U16).rearrange("p (r t m) -> p r m t", t=PACK, m=P),
+            in_=w2w_raw[:].bitcast(U16).rearrange("p (r m t) -> p r m t", t=PACK, m=P),
+        )
+        nc.vector.tensor_copy(
+            out=w2s[:].rearrange("p (r t m) -> p r m t", t=PACK, m=P),
+            in_=w2s_raw[:].rearrange("p (r m t) -> p r m t", t=PACK, m=P),
+        )
+        nc.vector.tensor_copy(out=vw[0][:], in_=tabw[0][:].bitcast(U32).indirect(offs_sb[:]))
+        load_w1(1, 0, "slot_b")
+        nc.vector.tensor_copy(out=vs[:], in_=tabs[:].indirect(offs_sb[:]))
+        load_w1(1, 1, "slot_c")
+        nc.vector.tensor_copy(out=vw[1][:], in_=tabw[1][:].bitcast(U32).indirect(offs_sb[:]))
+        nc.sync.dma_start(out=gain_sb[:], in_=gain.rearrange("(b p t) -> p b t", b=B_PASSES, t=PACK))
+        nc.sync.dma_start(out=bias_sb[:], in_=bias.rearrange("(g p t) -> p g t", g=GROUPS, t=PACK))
+
+        w1_bf = {}
+        w1c = {}
+        w1s = {}
+
+        def cast_w1(b, a, m0, m1, on_vector):
+            if (b, a) not in w1_bf:
+                w1_bf[b, a] = ring.tile([P, PACK * KP], BF16, name="w1_bf", align_bytes=64)
+            dst = w1_bf[b, a][:].rearrange("p (t m j) -> p m j t", t=PACK, j=PACK)[:, m0:m1]
+            src = w1_raw[b, a][:].rearrange("p j (m t) -> p m j t", t=PACK)[:, m0:m1]
+            if on_vector:
+                nc.vector.tensor_copy(out=dst, in_=src)
+            else:
+                nc.scalar.copy(out=dst, in_=src)
+
+        def quant_w1(b, a, t0=0, t1=PACK):
+            if (b, a) not in w1c:
+                w1c[b, a] = keep.tile([P, KP], U32, name="w1c%d%d" % (b, a), align_bytes=64)
+                w1s[b, a] = keep.tile([P, KP], U8, name="w1s%d%d" % (b, a), align_bytes=64)
+            nc.vector.quantize_mx(
+                out=w1c[b, a][:, P * t0 : P * t1].bitcast(FP8X4),
+                scales=w1s[b, a][:, P * t0 : P * t1],
+                in_=w1_bf[b, a][:, KP * t0 : KP * t1],
+            )
+
+        h = {}
+
+        def make_h(s, share=False):
+            b, t = divmod(s, PACK)
+            h[s] = ring.tile([P, S], F32, name="h", bufs=8)
+            cols = slice(P * t, P * (t + 1))
+            for half in range(2):
+                acc = psum.tile([P, 512], F32, name="acc", tag="bank%d" % (4 + 2 * (s % 2) + half))
+                ent = slice(512 * half, 512 * (half + 1))
+                for a in range(A_PASSES):
+                    nc.tensor.matmul_mx(
+                        out=acc[:],
+                        lhsT=w1c[b, a][:, cols].bitcast(FP8X4),
+                        lhsT_scale=w1s[b, a][:, cols],
+                        rhs=vw[a][:, ent].bitcast(FP8X4),
+                        rhs_scale=vs[4 * a : P, ent],
+                        start=(a == 0),
+                        stop=(a == A_PASSES - 1),
+                    )
+                if share and half == 1:
+                    nc.vector.tensor_copy(out=h[s][:, ent], in_=acc[:])
+                else:
+                    nc.scalar.copy(out=h[s][:, ent], in_=acc[:])
+
+        second = {}
+        after_z = {(2, 3, 0): (0, 0), (2, 1, 256): (1, 0), (2, 3, 256): (2, 0), (2, 2, 384): (2, 256)}
+        after_quant = {(0, 2): (1, 0), (0, 3): (1, 1), (1, 1): (2, 0), (1, 2): (2, 1)}
+        second_ring = [keep.tile([P, PAIRS], F32, name="second%d" % i) for i in range(3)]
+        diff = {}
+        zplane = {}
+        zword = {}
+        zc = {}
+        zs = {}
+
+        def pick_second(b, t, j0, n):
+            if (b, t) in after_quant:
+                g2 = w1_bf[after_quant[b, t]][:].bitcast(F32)[:, 0:n]
+            else:
+                if (b, t, j0) in after_z:
+                    second_ring[len(second) % 3] = zword[after_z[b, t, j0]][:].bitcast(F32)
+                g2 = second_ring[len(second) % 3][:, 0:n]
+            nc.vector.tensor_copy(out=g2, in_=h[PACK * b + t][:].indirect(pos2_sb[:, j0 // 16 : (j0 + n) // 16]))
+            second[b, t, j0] = g2
+
+        def pick_diff(b, t, j0, n):
+            if (b, j0) not in diff:
+                diff[b, j0] = ring.tile([P, PACK, n], F32, name="diff", tag="diff", bufs=3)
+            nc.vector.tensor_tensor(
+                out=diff[b, j0][:, t, :],
+                in0=h[PACK * b + t][:].indirect(pos1_sb[:, j0 // 16 : (j0 + n) // 16]),
+                in1=second[b, t, j0],
+                op=ALU.subtract,
+            )
+
+        def clamp(b, t0, t1, j0):
+            d = diff[b, j0][:, t0:t1, :]
+            nc.vector.tensor_scalar(out=d, in0=d, scalar1=-1.0, scalar2=1.0, op0=ALU.max, op1=ALU.min)
+
+        def weigh(b, t, j0, n):
+            if (b, j0) not in zplane:
+                zplane[b, j0] = ring.tile([P, PACK, n], BF16, name="zplane", tag="zplane")
+            nc.scalar.activation(
+                out=zplane[b, j0][:, t, :], in_=diff[b, j0][:, t, :], func=ACT.Copy, scale=gain_sb[:, b, t : t + 1]
+            )
+
+        def weave_z(b, j0, n, on_vector):
+            zword[b, j0] = keep.tile([P, n * PACK], BF16, name="zword%d_%d" % (b, j0), align_bytes=64)
+            dst = zword[b, j0][:].rearrange("p (c i t) -> p c t i", i=4, t=PACK)
+            src = zplane[b, j0][:].rearrange("p t (c i) -> p c t i", i=4)
+            if on_vector:
+                nc.vector.tensor_copy(out=dst, in_=src)
+            else:
+                nc.scalar.copy(out=dst, in_=src)
+
+        def weigh_weave(b, j0, n):
+            zword[b, j0] = keep.tile([P, n * PACK], BF16, name="zword%d_%d" % (b, j0), align_bytes=64)
+            nc.vector.tensor_tensor(
+                out=zword[b, j0][:].rearrange("p (j t) -> p j t", t=PACK),
+                in0=diff[b, j0][:].rearrange("p t j -> p j t"),
+                in1=gain_sb[:, b, :].unsqueeze(1).to_broadcast([P, n, PACK]),
+                op=ALU.mult,
+            )
+
+        def quant_z(b, j0, n):
+            codes = keep.tile([P, n], U32, name="zc%d_%d" % (b, j0), align_bytes=64)
+            scales = keep.tile([P, n], U8, name="zs%d_%d" % (b, j0), align_bytes=64)
+            nc.vector.quantize_mx(out=codes[:].bitcast(FP8X4), scales=scales[:], in_=zword[b, j0][:])
+            for q in range(j0 // QUARTER, (j0 + n) // QUARTER):
+                cols = slice(QUARTER * q - j0, QUARTER * (q + 1) - j0)
+                zc[b, q] = codes[:, cols]
+                zs[b, q] = scales[:, cols]
+
+        yacc = {}
+
+        def mul_z(b, q, g):
+            if (q, g) not in yacc:
+                yacc[q, g] = psum.tile([P, PACK, QUARTER], F32, name="yacc", tag="bank%d" % (2 * q + g))
+            for t in range(PACK):
+                col = (b * GROUPS + g) * KP + t * P
+                nc.tensor.matmul_mx(
+                    out=yacc[q, g][:, t, :],
+                    lhsT=w2w[:, 2 * col : 2 * (col + P)].bitcast(FP4X4),
+                    lhsT_scale=w2s[:, col : col + P],
+                    rhs=zc[b, q].bitcast(FP8X4),
+                    rhs_scale=zs[b, q],
+                    start=(b == 0 and t == 0),
+                    stop=(b == B_PASSES - 1 and t == PACK - 1),
+                )
+
+        y = {}
+        yword = {}
+        yc = {}
+
+        def add_bias(q, g, on_vector):
+            y[q, g] = ring.tile([P, PACK, QUARTER], F32, name="y", tag="y", bufs=8)
+            if on_vector:
+                nc.vector.tensor_tensor(
+                    out=y[q, g][:],
+                    in0=yacc[q, g][:],
+                    in1=bias_sb[:, g, :].unsqueeze(2).to_broadcast([P, PACK, QUARTER]),
+                    op=ALU.add,
+                )
+            else:
+                for t in range(PACK):
+                    nc.scalar.activation(
+                        out=y[q, g][:, t, :], in_=yacc[q, g][:, t, :], func=ACT.Identity, bias=bias_sb[:, g, t : t + 1]
+                    )
+            nc.sync.dma_start(
+                out=out_0[KP * g : KP * (g + 1), QUARTER * q : QUARTER * (q + 1)].rearrange("(p t) j -> p t j", t=PACK),
+                in_=y[q, g][:],
+            )
+
+        def weave_y(q, g, on_vector):
+            yword[q, g] = ring.tile([P, QUARTER * PACK], BF16, name="yword", tag="yword", bufs=8, align_bytes=64)
+            dst = yword[q, g][:].rearrange("p (c i t) -> p c t i", i=4, t=PACK)
+            src = y[q, g][:].rearrange("p t (c i) -> p c t i", i=4)
+            if on_vector:
+                nc.vector.tensor_copy(out=dst, in_=src)
+            else:
+                nc.scalar.copy(out=dst, in_=src)
+
+        def quant_y(q, g):
+            if q not in yc:
+                yc[q] = keep.tile([P, GROUPS * QUARTER], U32, name="yc%d" % q, align_bytes=64)
+            nc.vector.quantize_mx(
+                out=yc[q][:, QUARTER * g : QUARTER * (g + 1)].bitcast(FP8X4),
+                scales=ys[:, PAIRS * g + QUARTER * q : PAIRS * g + QUARTER * (q + 1)],
+                in_=yword[q, g][:],
+            )
+
+        def store_codes(q):
+            nc.sync.dma_start(
+                out=out_1[:, :, QUARTER * q : QUARTER * (q + 1), :].rearrange("g p m t -> p g (m t)").bitcast(I32),
+                in_=yc[q][:].bitcast(I32).rearrange("p (g m) -> p g m", g=GROUPS),
+            )
+
+        cast_w1(0, 0, 0, 44, False)
+        cast_w1(0, 0, 44, P, True)
+        load_w1(2, 0, "slot_d")
+        quant_w1(0, 0)
+        cast_w1(0, 1, 0, 44, False)
+        cast_w1(0, 1, 44, P, True)
+        load_w1(2, 1, "slot_e")
+        quant_w1(0, 1, 0, 1)
+        quant_w1(0, 1, 1, 2)
+        quant_w1(0, 1, 2, 4)
+        make_h(0, True)
+        make_h(1)
+
+        last = B_PASSES - 1
+        cast_w1(1, 0, 0, P, False)
+        make_h(2)
+        cast_w1(1, 1, 0, P, False)
+        make_h(3)
+        for s in range(2 * PACK):
+            b, t = divmod(s, PACK)
+            if (b, t) in after_quant:
+                quant_w1(*after_quant[b, t])
+            pick_second(b, t, 0, PAIRS)
+            if s > 0:
+                pick_diff((s - 1) // PACK, (s - 1) % PACK, 0, PAIRS)
+            if s == 3:
+                make_h(4)
+                cast_w1(2, 0, 0, P, False)
+                make_h(5)
+                cast_w1(2, 1, 0, P, False)
+                make_h(6)
+                make_h(7)
+            if s == 4:
+                clamp(0, 0, PACK, 0)
+                for u in range(PACK):
+                    weigh(0, u, 0, PAIRS)
+            if s == 6:
+                weave_z(0, 0, PAIRS, False)
+                for u in range(PACK):
+                    make_h(PACK * last + u)
+
+        (j0, n0), (j1, n1), (j2, n2) = LAST_PIECES
+        pick_second(last, 0, j0, n0)
+        pick_diff(1, 3, 0, PAIRS)
+        pick_second(last, 1, j0, n0)
+        clamp(1, 0, PACK, 0)
+        for t in range(PACK):
+            weigh(1, t, 0, PAIRS)
+        pick_diff(last, 0, j0, n0)
+        pick_second(last, 2, j0, n0)
+        quant_z(0, 0, PAIRS)
+        for q in range(QUARTERS):
+            for g in range(GROUPS):
+                mul_z(0, q, g)
+        pick_diff(last, 1, j0, n0)
+        pick_second(last, 3, j0, n0)
+        pick_diff(last, 2, j0, n0)
+        pick_second(last, 0, j1, n1)
+        pick_diff(last, 3, j0, n0)
+        weave_z(1, 0, PAIRS, True)
+        quant_z(1, 0, PAIRS)
+        for q in range(2):
+            for g in range(GROUPS):
+                mul_z(1, q, g)
+        clamp(last, 0, PACK, j0)
+        for t in range(PACK):
+            weigh(last, t, j0, n0)
+        pick_second(last, 1, j1, n1)
+        pick_diff(last, 0, j1, n1)
+        pick_second(last, 2, j1, n1)
+        pick_diff(last, 1, j1, n1)
+        weave_z(last, j0, n0, True)
+        pick_diff(last, 2, j1, n1)
+        quant_z(last, j0, n0)
+        for q in range(2):
+            for g in range(GROUPS):
+                mul_z(last, q, g)
+                add_bias(q, g, False)
+                weave_y(q, g, False)
+        for q in range(2, QUARTERS):
+            for g in range(GROUPS):
+                mul_z(1, q, g)
+        pick_second(last, 0, j2, n2)
+        pick_second(last, 3, j1, n1)
+        pick_second(last, 1, j2, n2)
+        pick_diff(last, 3, j1, n1)
+        pick_diff(last, 0, j2, n2)
+        clamp(last, 0, PACK, j1)
+        pick_diff(last, 1, j2, n2)
+        weigh_weave(last, j1, n1)
+        pick_second(last, 3, j2, n2)
+        quant_z(last, j1, n1)
+        for g in range(GROUPS):
+            mul_z(last, 2, g)
+        pick_diff(last, 3, j2, n2)
+        pick_second(last, 2, j2, n2)
+        quant_y(0, 0)
+        pick_diff(last, 2, j2, n2)
+        add_bias(2, 0, True)
+        clamp(last, 0, PACK, j2)
+        add_bias(2, 1, True)
+        weigh_weave(last, j2, n2)
+        quant_y(0, 1)
+        store_codes(0)
+        quant_z(last, j2, n2)
+        for g in range(GROUPS):
+            mul_z(last, 3, g)
+        weave_y(2, 0, True)
+        weave_y(2, 1, True)
+        quant_y(2, 0)
+        quant_y(2, 1)
+        store_codes(2)
+        add_bias(3, 0, True)
+        add_bias(3, 1, False)
+        quant_y(1, 0)
+        weave_y(3, 0, True)
+        weave_y(3, 1, False)
+        quant_y(1, 1)
+        store_codes(1)
+        quant_y(3, 0)
+        quant_y(3, 1)
+        store_codes(3)
+        for quad in range(4):
+            eng = nc.scalar if quad % 2 else nc.sync
+            eng.dma_start(
+                out=out_2[:, 4 * quad : 4 * quad + 4, :].bitcast(I32).rearrange("g r m -> r g m"),
+                in_=ys[32 * quad : 32 * quad + 4, :].bitcast(I32).rearrange("p (g m) -> p g m", g=GROUPS),
+            )

@@ -44,8 +44,6 @@ def tile_list_clamped_landmark_differences_kernel(
         w2s_raw = keep.tile([P, B_PASSES * N], U8, name="w2s_raw")
         w2w = keep.tile([P, B_PASSES * 2 * N], U8, name="w2w", align_bytes=64)
         w2s = keep.tile([P, B_PASSES * N], U8, name="w2s", align_bytes=64)
-        gain_sb = keep.tile([P, B_PASSES, PACK], F32, name="gain_sb")
-        bias_sb = keep.tile([P, GROUPS, PACK], F32, name="bias_sb")
         vw = [keep.tile([P, S], U32, name="vw%d" % a, align_bytes=64) for a in range(A_PASSES)]
         vs = keep.tile([P, S], U8, name="vs", align_bytes=64)
         ys = keep.tile([P, GROUPS * PAIRS], U8, name="ys", align_bytes=64)
@@ -91,20 +89,18 @@ def tile_list_clamped_landmark_differences_kernel(
         nc.sync.dma_start(pos1_sb[:], pos1)
 
         nc.vector.tensor_copy(
-            out=w2w[:].bitcast(U16).rearrange("p (r t m) -> p r m t", t=PACK, m=P),
-            in_=w2w_raw[:].bitcast(U16).rearrange("p (r m t) -> p r m t", t=PACK, m=P),
+            out=w2w[:].bitcast(U16).rearrange("p (r t c i) -> p r c t i", t=PACK, c=16, i=8),
+            in_=w2w_raw[:].bitcast(U16).rearrange("p (r c i t) -> p r c t i", t=PACK, c=16, i=8),
         )
         nc.vector.tensor_copy(
-            out=w2s[:].rearrange("p (r t m) -> p r m t", t=PACK, m=P),
-            in_=w2s_raw[:].rearrange("p (r m t) -> p r m t", t=PACK, m=P),
+            out=w2s[:].rearrange("p (r t c i) -> p r c t i", t=PACK, c=8, i=16),
+            in_=w2s_raw[:].rearrange("p (r c i t) -> p r c t i", t=PACK, c=8, i=16),
         )
         nc.vector.tensor_copy(out=vw[0][:], in_=tabw[0][:].bitcast(U32).indirect(offs_sb[:]))
         load_w1(1, 0, "slot_b")
         nc.vector.tensor_copy(out=vs[:], in_=tabs[:].indirect(offs_sb[:]))
         load_w1(1, 1, "slot_c")
         nc.vector.tensor_copy(out=vw[1][:], in_=tabw[1][:].bitcast(U32).indirect(offs_sb[:]))
-        nc.sync.dma_start(out=gain_sb[:], in_=gain.rearrange("(b p t) -> p b t", b=B_PASSES, t=PACK))
-        nc.sync.dma_start(out=bias_sb[:], in_=bias.rearrange("(g p t) -> p g t", g=GROUPS, t=PACK))
 
         w1_bf = {}
         w1c = {}
@@ -113,8 +109,8 @@ def tile_list_clamped_landmark_differences_kernel(
         def cast_w1(b, a, m0, m1, on_vector):
             if (b, a) not in w1_bf:
                 w1_bf[b, a] = ring.tile([P, PACK * KP], BF16, name="w1_bf", align_bytes=64)
-            dst = w1_bf[b, a][:].rearrange("p (t m j) -> p m j t", t=PACK, j=PACK)[:, m0:m1]
-            src = w1_raw[b, a][:].rearrange("p j (m t) -> p m j t", t=PACK)[:, m0:m1]
+            dst = w1_bf[b, a][:].rearrange("p (t m j) -> p m t j", t=PACK, j=PACK)[:, m0:m1]
+            src = w1_raw[b, a][:].rearrange("p j (m t) -> p m t j", t=PACK)[:, m0:m1]
             if on_vector:
                 nc.vector.tensor_copy(out=dst, in_=src)
             else:
@@ -171,29 +167,38 @@ def tile_list_clamped_landmark_differences_kernel(
                 if (b, t, j0) in after_z:
                     second_ring[len(second) % 3] = zword[after_z[b, t, j0]][:].bitcast(F32)
                 g2 = second_ring[len(second) % 3][:, 0:n]
-            nc.vector.tensor_copy(out=g2, in_=h[PACK * b + t][:].indirect(pos2_sb[:, j0 // 16 : (j0 + n) // 16]))
+            step = n // 2 if n > QUARTER else n
+            for c in range(0, n, step):
+                nc.vector.tensor_copy(
+                    out=g2[:, c : c + step],
+                    in_=h[PACK * b + t][:].indirect(pos2_sb[:, (j0 + c) // 16 : (j0 + c + step) // 16]),
+                )
             second[b, t, j0] = g2
 
         def pick_diff(b, t, j0, n):
             if (b, j0) not in diff:
                 diff[b, j0] = ring.tile([P, PACK, n], F32, name="diff", tag="diff", bufs=3)
-            nc.vector.tensor_tensor(
-                out=diff[b, j0][:, t, :],
-                in0=h[PACK * b + t][:].indirect(pos1_sb[:, j0 // 16 : (j0 + n) // 16]),
-                in1=second[b, t, j0],
-                op=ALU.subtract,
-            )
+            step = n // 2 if n > QUARTER else n
+            for c in range(0, n, step):
+                nc.vector.tensor_tensor(
+                    out=diff[b, j0][:, t, c : c + step],
+                    in0=h[PACK * b + t][:].indirect(pos1_sb[:, (j0 + c) // 16 : (j0 + c + step) // 16]),
+                    in1=second[b, t, j0][:, c : c + step],
+                    op=ALU.subtract,
+                )
 
         def clamp(b, t0, t1, j0):
             d = diff[b, j0][:, t0:t1, :]
             nc.vector.tensor_scalar(out=d, in0=d, scalar1=-1.0, scalar2=1.0, op0=ALU.max, op1=ALU.min)
 
-        def weigh(b, t, j0, n):
+        def weigh(b, t, j0, n, on_vector=False):
             if (b, j0) not in zplane:
                 zplane[b, j0] = ring.tile([P, PACK, n], BF16, name="zplane", tag="zplane")
-            nc.scalar.activation(
-                out=zplane[b, j0][:, t, :], in_=diff[b, j0][:, t, :], func=ACT.Copy, scale=gain_sb[:, b, t : t + 1]
-            )
+            dst, src, factor = zplane[b, j0][:, t, :], diff[b, j0][:, t, :], gain_sb[:, b, t : t + 1]
+            if on_vector:
+                nc.vector.tensor_scalar(out=dst, in0=src, scalar1=factor, scalar2=None, op0=ALU.mult)
+            else:
+                nc.scalar.activation(out=dst, in_=src, func=ACT.Copy, scale=factor)
 
         def weave_z(b, j0, n, on_vector):
             zword[b, j0] = keep.tile([P, n * PACK], BF16, name="zword%d_%d" % (b, j0), align_bytes=64)
@@ -203,15 +208,6 @@ def tile_list_clamped_landmark_differences_kernel(
                 nc.vector.tensor_copy(out=dst, in_=src)
             else:
                 nc.scalar.copy(out=dst, in_=src)
-
-        def weigh_weave(b, j0, n):
-            zword[b, j0] = keep.tile([P, n * PACK], BF16, name="zword%d_%d" % (b, j0), align_bytes=64)
-            nc.vector.tensor_tensor(
-                out=zword[b, j0][:].rearrange("p (j t) -> p j t", t=PACK),
-                in0=diff[b, j0][:].rearrange("p t j -> p j t"),
-                in1=gain_sb[:, b, :].unsqueeze(1).to_broadcast([P, n, PACK]),
-                op=ALU.mult,
-            )
 
         def quant_z(b, j0, n):
             codes = keep.tile([P, n], U32, name="zc%d_%d" % (b, j0), align_bytes=64)
@@ -303,6 +299,10 @@ def tile_list_clamped_landmark_differences_kernel(
         cast_w1(1, 0, 0, P, False)
         make_h(2)
         cast_w1(1, 1, 0, P, False)
+        gain_sb = keep.tile([P, B_PASSES, PACK], F32, name="gain_sb", tag="slot_b")
+        bias_sb = keep.tile([P, GROUPS, PACK], F32, name="bias_sb", tag="slot_c")
+        nc.sync.dma_start(out=gain_sb[:], in_=gain.rearrange("(b p t) -> p b t", b=B_PASSES, t=PACK))
+        nc.sync.dma_start(out=bias_sb[:], in_=bias.rearrange("(g p t) -> p g t", g=GROUPS, t=PACK))
         make_h(3)
         for s in range(2 * PACK):
             b, t = divmod(s, PACK)
@@ -375,19 +375,26 @@ def tile_list_clamped_landmark_differences_kernel(
         pick_diff(last, 0, j2, n2)
         clamp(last, 0, PACK, j1)
         pick_diff(last, 1, j2, n2)
-        weigh_weave(last, j1, n1)
+        for t in range(PACK):
+            weigh(last, t, j1, n1, True)
         pick_second(last, 3, j2, n2)
+        weave_z(last, j1, n1, True)
+        pick_diff(last, 3, j2, n2)
         quant_z(last, j1, n1)
         for g in range(GROUPS):
             mul_z(last, 2, g)
-        pick_diff(last, 3, j2, n2)
+        clamp(last, 0, 2, j2)
         pick_second(last, 2, j2, n2)
-        quant_y(0, 0)
+        clamp(last, 3, 4, j2)
+        for t in (0, 1, 3):
+            weigh(last, t, j2, n2, True)
         pick_diff(last, 2, j2, n2)
+        quant_y(0, 0)
+        clamp(last, 2, 3, j2)
         add_bias(2, 0, True)
-        clamp(last, 0, PACK, j2)
+        weigh(last, 2, j2, n2, True)
         add_bias(2, 1, True)
-        weigh_weave(last, j2, n2)
+        weave_z(last, j2, n2, True)
         quant_y(0, 1)
         store_codes(0)
         quant_z(last, j2, n2)

@@ -186,10 +186,12 @@ def tile_list_clamped_landmark_differences_kernel(
                     in1=second[b, t, j0][:, c : c + step],
                     op=ALU.subtract,
                 )
+            if n > QUARTER:
+                clamp(b, t, t + 1, j0, nc.gpsimd)
 
-        def clamp(b, t0, t1, j0):
+        def clamp(b, t0, t1, j0, engine=nc.vector):
             d = diff[b, j0][:, t0:t1, :]
-            nc.vector.tensor_scalar(out=d, in0=d, scalar1=-1.0, scalar2=1.0, op0=ALU.max, op1=ALU.min)
+            engine.tensor_scalar(out=d, in0=d, scalar1=1.0, scalar2=-1.0, op0=ALU.min, op1=ALU.max)
 
         def weigh(b, t, j0, n, on_vector=False):
             if (b, j0) not in zplane:
@@ -220,66 +222,75 @@ def tile_list_clamped_landmark_differences_kernel(
 
         yacc = {}
 
-        def mul_z(b, q, g):
-            if (q, g) not in yacc:
-                yacc[q, g] = psum.tile([P, PACK, QUARTER], F32, name="yacc", tag="bank%d" % (2 * q + g))
-            for t in range(PACK):
-                col = (b * GROUPS + g) * KP + t * P
-                nc.tensor.matmul_mx(
-                    out=yacc[q, g][:, t, :],
-                    lhsT=w2w[:, 2 * col : 2 * (col + P)].bitcast(FP4X4),
-                    lhsT_scale=w2s[:, col : col + P],
-                    rhs=zc[b, q].bitcast(FP8X4),
-                    rhs_scale=zs[b, q],
-                    start=(b == 0 and t == 0),
-                    stop=(b == B_PASSES - 1 and t == PACK - 1),
-                )
+        def mul_z(b, j0, n, g):
+            per_bank = KP // n
+            for u in range(PACK // per_bank):
+                if (j0, g, u) not in yacc:
+                    bank = 2 * (j0 // QUARTER) + g * (PACK // per_bank) + u
+                    yacc[j0, g, u] = psum.tile([P, per_bank, n], F32, name="yacc", tag="bank%d" % bank)
+                for i in range(per_bank):
+                    col = (b * GROUPS + g) * KP + (per_bank * u + i) * P
+                    for c in range(0, n, QUARTER):
+                        q = (j0 + c) // QUARTER
+                        nc.tensor.matmul_mx(
+                            out=yacc[j0, g, u][:, i, c : c + QUARTER],
+                            lhsT=w2w[:, 2 * col : 2 * (col + P)].bitcast(FP4X4),
+                            lhsT_scale=w2s[:, col : col + P],
+                            rhs=zc[b, q].bitcast(FP8X4),
+                            rhs_scale=zs[b, q],
+                            start=(b == 0 and i == 0 and c == 0),
+                            stop=(b == B_PASSES - 1 and i == per_bank - 1 and c == n - QUARTER),
+                        )
 
         y = {}
         yword = {}
         yc = {}
 
-        def add_bias(q, g, on_vector):
-            y[q, g] = ring.tile([P, PACK, QUARTER], F32, name="y", tag="y", bufs=8)
+        def add_bias(j0, n, g, on_vector):
+            y[j0, g] = keep.tile([P, PACK, n], F32, name="y%d_%d" % (j0, g))
+            per_bank = KP // n
             if on_vector:
                 nc.vector.tensor_tensor(
-                    out=y[q, g][:],
-                    in0=yacc[q, g][:],
-                    in1=bias_sb[:, g, :].unsqueeze(2).to_broadcast([P, PACK, QUARTER]),
+                    out=y[j0, g][:],
+                    in0=yacc[j0, g, 0][:],
+                    in1=bias_sb[:, g, :].unsqueeze(2).to_broadcast([P, PACK, n]),
                     op=ALU.add,
                 )
             else:
                 for t in range(PACK):
                     nc.scalar.activation(
-                        out=y[q, g][:, t, :], in_=yacc[q, g][:, t, :], func=ACT.Identity, bias=bias_sb[:, g, t : t + 1]
+                        out=y[j0, g][:, t, :],
+                        in_=yacc[j0, g, t // per_bank][:, t % per_bank, :],
+                        func=ACT.Identity,
+                        bias=bias_sb[:, g, t : t + 1],
                     )
             nc.sync.dma_start(
-                out=out_0[KP * g : KP * (g + 1), QUARTER * q : QUARTER * (q + 1)].rearrange("(p t) j -> p t j", t=PACK),
-                in_=y[q, g][:],
+                out=out_0[KP * g : KP * (g + 1), j0 : j0 + n].rearrange("(p t) j -> p t j", t=PACK),
+                in_=y[j0, g][:],
             )
 
-        def weave_y(q, g, on_vector):
-            yword[q, g] = ring.tile([P, QUARTER * PACK], BF16, name="yword", tag="yword", bufs=8, align_bytes=64)
-            dst = yword[q, g][:].rearrange("p (c i t) -> p c t i", i=4, t=PACK)
-            src = y[q, g][:].rearrange("p t (c i) -> p c t i", i=4)
+        def weave_y(j0, n, g, on_vector):
+            yword[j0, g] = keep.tile([P, n * PACK], BF16, name="yword%d_%d" % (j0, g), align_bytes=64)
+            dst = yword[j0, g][:].rearrange("p (c i t) -> p c t i", i=4, t=PACK)
+            src = y[j0, g][:].rearrange("p t (c i) -> p c t i", i=4)
             if on_vector:
                 nc.vector.tensor_copy(out=dst, in_=src)
             else:
                 nc.scalar.copy(out=dst, in_=src)
 
-        def quant_y(q, g):
-            if q not in yc:
-                yc[q] = keep.tile([P, GROUPS * QUARTER], U32, name="yc%d" % q, align_bytes=64)
+        def quant_y(j0, n, g):
+            if j0 not in yc:
+                yc[j0] = keep.tile([P, GROUPS * n], U32, name="yc%d" % j0, align_bytes=64)
             nc.vector.quantize_mx(
-                out=yc[q][:, QUARTER * g : QUARTER * (g + 1)].bitcast(FP8X4),
-                scales=ys[:, PAIRS * g + QUARTER * q : PAIRS * g + QUARTER * (q + 1)],
-                in_=yword[q, g][:],
+                out=yc[j0][:, n * g : n * (g + 1)].bitcast(FP8X4),
+                scales=ys[:, PAIRS * g + j0 : PAIRS * g + j0 + n],
+                in_=yword[j0, g][:],
             )
 
-        def store_codes(q):
+        def store_codes(j0, n):
             nc.sync.dma_start(
-                out=out_1[:, :, QUARTER * q : QUARTER * (q + 1), :].rearrange("g p m t -> p g (m t)").bitcast(I32),
-                in_=yc[q][:].bitcast(I32).rearrange("p (g m) -> p g m", g=GROUPS),
+                out=out_1[:, :, j0 : j0 + n, :].rearrange("g p m t -> p g (m t)").bitcast(I32),
+                in_=yc[j0][:].bitcast(I32).rearrange("p (g m) -> p g m", g=GROUPS),
             )
 
         cast_w1(0, 0, 0, 44, False)
@@ -319,7 +330,6 @@ def tile_list_clamped_landmark_differences_kernel(
                 make_h(6)
                 make_h(7)
             if s == 4:
-                clamp(0, 0, PACK, 0)
                 for u in range(PACK):
                     weigh(0, u, 0, PAIRS)
             if s == 6:
@@ -331,15 +341,14 @@ def tile_list_clamped_landmark_differences_kernel(
         pick_second(last, 0, j0, n0)
         pick_diff(1, 3, 0, PAIRS)
         pick_second(last, 1, j0, n0)
-        clamp(1, 0, PACK, 0)
         for t in range(PACK):
             weigh(1, t, 0, PAIRS)
         pick_diff(last, 0, j0, n0)
         pick_second(last, 2, j0, n0)
         quant_z(0, 0, PAIRS)
-        for q in range(QUARTERS):
+        for piece in LAST_PIECES:
             for g in range(GROUPS):
-                mul_z(0, q, g)
+                mul_z(0, *piece, g)
         pick_diff(last, 1, j0, n0)
         pick_second(last, 3, j0, n0)
         pick_diff(last, 2, j0, n0)
@@ -347,10 +356,8 @@ def tile_list_clamped_landmark_differences_kernel(
         pick_diff(last, 3, j0, n0)
         weave_z(1, 0, PAIRS, True)
         quant_z(1, 0, PAIRS)
-        for q in range(2):
-            for g in range(GROUPS):
-                mul_z(1, q, g)
-        clamp(last, 0, PACK, j0)
+        for g in range(GROUPS):
+            mul_z(1, j0, n0, g)
         for t in range(PACK):
             weigh(last, t, j0, n0)
         pick_second(last, 1, j1, n1)
@@ -360,14 +367,13 @@ def tile_list_clamped_landmark_differences_kernel(
         weave_z(last, j0, n0, True)
         pick_diff(last, 2, j1, n1)
         quant_z(last, j0, n0)
-        for q in range(2):
+        for g in range(GROUPS):
+            mul_z(last, j0, n0, g)
+            add_bias(j0, n0, g, False)
+            weave_y(j0, n0, g, False)
+        for piece in LAST_PIECES[1:]:
             for g in range(GROUPS):
-                mul_z(last, q, g)
-                add_bias(q, g, False)
-                weave_y(q, g, False)
-        for q in range(2, QUARTERS):
-            for g in range(GROUPS):
-                mul_z(1, q, g)
+                mul_z(1, *piece, g)
         pick_second(last, 0, j2, n2)
         pick_second(last, 3, j1, n1)
         pick_second(last, 1, j2, n2)
@@ -382,39 +388,36 @@ def tile_list_clamped_landmark_differences_kernel(
         pick_diff(last, 3, j2, n2)
         quant_z(last, j1, n1)
         for g in range(GROUPS):
-            mul_z(last, 2, g)
+            mul_z(last, j1, n1, g)
         clamp(last, 0, 2, j2)
         pick_second(last, 2, j2, n2)
         clamp(last, 3, 4, j2)
         for t in (0, 1, 3):
             weigh(last, t, j2, n2, True)
         pick_diff(last, 2, j2, n2)
-        quant_y(0, 0)
         clamp(last, 2, 3, j2)
-        add_bias(2, 0, True)
+        add_bias(j1, n1, 0, True)
         weigh(last, 2, j2, n2, True)
-        add_bias(2, 1, True)
+        add_bias(j1, n1, 1, True)
         weave_z(last, j2, n2, True)
-        quant_y(0, 1)
-        store_codes(0)
+        quant_y(j0, n0, 0)
         quant_z(last, j2, n2)
         for g in range(GROUPS):
-            mul_z(last, 3, g)
-        weave_y(2, 0, True)
-        weave_y(2, 1, True)
-        quant_y(2, 0)
-        quant_y(2, 1)
-        store_codes(2)
-        add_bias(3, 0, True)
-        add_bias(3, 1, False)
-        quant_y(1, 0)
-        weave_y(3, 0, True)
-        weave_y(3, 1, False)
-        quant_y(1, 1)
-        store_codes(1)
-        quant_y(3, 0)
-        quant_y(3, 1)
-        store_codes(3)
+            mul_z(last, j2, n2, g)
+        weave_y(j1, n1, 0, True)
+        weave_y(j1, n1, 1, True)
+        quant_y(j1, n1, 0)
+        quant_y(j1, n1, 1)
+        store_codes(j1, n1)
+        add_bias(j2, n2, 0, True)
+        add_bias(j2, n2, 1, False)
+        quant_y(j0, n0, 1)
+        store_codes(j0, n0)
+        weave_y(j2, n2, 0, True)
+        weave_y(j2, n2, 1, True)
+        quant_y(j2, n2, 0)
+        quant_y(j2, n2, 1)
+        store_codes(j2, n2)
         for quad in range(4):
             eng = nc.scalar if quad % 2 else nc.sync
             eng.dma_start(

@@ -39,7 +39,7 @@ def tile_list_clamped_landmark_differences_kernel(
         offs_sb = keep.tile([P, S // 16], U16, name="offs_sb")
         pos1_sb = keep.tile([P, PAIRS // 16], U16, name="pos1_sb")
         pos2_sb = keep.tile([P, PAIRS // 16], U16, name="pos2_sb")
-        tabs = keep.tile([P, T], U8, name="tabs", tag="slot_c")
+        tabs = keep.tile([P, T], U8, name="tabs")
         w2w_raw = keep.tile([P, B_PASSES * 2 * N], U8, name="w2w_raw")
         w2s_raw = keep.tile([P, B_PASSES * N], U8, name="w2s_raw")
         w2w = keep.tile([P, B_PASSES * 2 * N], U8, name="w2w", align_bytes=64)
@@ -71,22 +71,23 @@ def tile_list_clamped_landmark_differences_kernel(
             out=w2w_raw[:].bitcast(I32).rearrange("p (b c) -> p b c", b=B_PASSES),
             in_=w2_words.bitcast(I32).rearrange("b p c -> p b c"),
         )
-        for quad in range(4):
-            nc.sync.dma_start(
-                out=w2s_raw[32 * quad : 32 * quad + 4, :].bitcast(I32).rearrange("p (b c) -> p b c", b=B_PASSES),
-                in_=w2_scales[:, 4 * quad : 4 * quad + 4, :].bitcast(I32).rearrange("b r c -> r b c"),
-            )
         load_table(0, "slot_b")
-        for quad in range(4):
-            nc.sync.dma_start(
-                out=tabs[32 * quad : 32 * quad + 4 * A_PASSES, :].bitcast(I32),
-                in_=tab_scales[:, 4 * quad : 4 * quad + 4, :].bitcast(I32),
-            )
         load_table(1, "slot_a")
         load_w1(0, 0, "slot_d")
         load_w1(0, 1, "slot_e")
         nc.sync.dma_start(pos2_sb[:], pos2)
         nc.sync.dma_start(pos1_sb[:], pos1)
+        load_w1(1, 0, "slot_f")
+        for quad in range(4):
+            nc.gpsimd.dma_start(
+                out=w2s_raw[32 * quad : 32 * quad + 4, :].bitcast(I32).rearrange("p (b c) -> p b c", b=B_PASSES),
+                in_=w2_scales[:, 4 * quad : 4 * quad + 4, :].bitcast(I32).rearrange("b r c -> r b c"),
+            )
+        for quad in range(4):
+            nc.gpsimd.dma_start(
+                out=tabs[32 * quad : 32 * quad + 4 * A_PASSES, :].bitcast(I32),
+                in_=tab_scales[:, 4 * quad : 4 * quad + 4, :].bitcast(I32),
+            )
 
         nc.vector.tensor_copy(
             out=w2w[:].bitcast(U16).rearrange("p (r t c i) -> p r c t i", t=PACK, c=16, i=8),
@@ -97,9 +98,8 @@ def tile_list_clamped_landmark_differences_kernel(
             in_=w2s_raw[:].rearrange("p (r c i t) -> p r c t i", t=PACK, c=8, i=16),
         )
         nc.vector.tensor_copy(out=vw[0][:], in_=tabw[0][:].bitcast(U32).indirect(offs_sb[:]))
-        load_w1(1, 0, "slot_b")
         nc.vector.tensor_copy(out=vs[:], in_=tabs[:].indirect(offs_sb[:]))
-        load_w1(1, 1, "slot_c")
+        load_w1(1, 1, "slot_b")
         nc.vector.tensor_copy(out=vw[1][:], in_=tabw[1][:].bitcast(U32).indirect(offs_sb[:]))
 
         w1_bf = {}
@@ -108,7 +108,7 @@ def tile_list_clamped_landmark_differences_kernel(
 
         def cast_w1(b, a, m0, m1, on_vector):
             if (b, a) not in w1_bf:
-                w1_bf[b, a] = ring.tile([P, PACK * KP], BF16, name="w1_bf", align_bytes=64)
+                w1_bf[b, a] = ring.tile([P, PACK * KP], BF16, name="w1_bf", bufs=3, align_bytes=64)
             dst = w1_bf[b, a][:].rearrange("p (t m j) -> p m t j", t=PACK, j=PACK)[:, m0:m1]
             src = w1_raw[b, a][:].rearrange("p j (m t) -> p m t j", t=PACK)[:, m0:m1]
             if on_vector:
@@ -151,7 +151,17 @@ def tile_list_clamped_landmark_differences_kernel(
                     nc.scalar.copy(out=h[s][:, ent], in_=acc[:])
 
         second = {}
-        after_z = {(2, 3, 0): (0, 0), (2, 1, 256): (1, 0), (2, 3, 256): (2, 0), (2, 2, 384): (2, 256)}
+        after_z = {
+            (3, 0): ((0, 0), 0),
+            (0, 256): ((0, 0), 0),
+            (1, 256): ((0, 0), 128),
+            (2, 256): ((1, 0), 0),
+            (3, 256): ((2, 0), 0),
+            (0, 384): ((2, 0), 128),
+            (1, 384): ((1, 256), 0),
+            (2, 384): ((1, 256), 128),
+            (3, 384): ((1, 256), 256),
+        }
         after_quant = {(0, 2): (1, 0), (0, 3): (1, 1), (1, 1): (2, 0), (1, 2): (2, 1)}
         second_ring = [keep.tile([P, PAIRS], F32, name="second%d" % i) for i in range(3)]
         diff = {}
@@ -163,9 +173,10 @@ def tile_list_clamped_landmark_differences_kernel(
         def pick_second(b, t, j0, n):
             if (b, t) in after_quant:
                 g2 = w1_bf[after_quant[b, t]][:].bitcast(F32)[:, 0:n]
+            elif b == B_PASSES - 1 and (t, j0) in after_z:
+                key, c0 = after_z[t, j0]
+                g2 = zword[key][:].bitcast(F32)[:, c0 : c0 + n]
             else:
-                if (b, t, j0) in after_z:
-                    second_ring[len(second) % 3] = zword[after_z[b, t, j0]][:].bitcast(F32)
                 g2 = second_ring[len(second) % 3][:, 0:n]
             step = n // 2 if n > QUARTER else n
             for c in range(0, n, step):
@@ -195,17 +206,21 @@ def tile_list_clamped_landmark_differences_kernel(
 
         def weigh(b, t, j0, n, on_vector=False):
             if (b, j0) not in zplane:
-                zplane[b, j0] = ring.tile([P, PACK, n], BF16, name="zplane", tag="zplane")
+                zplane[b, j0] = keep.tile([P, PACK, n], BF16, name="zplane%d_%d" % (b, j0), align_bytes=64)
             dst, src, factor = zplane[b, j0][:, t, :], diff[b, j0][:, t, :], gain_sb[:, b, t : t + 1]
             if on_vector:
                 nc.vector.tensor_scalar(out=dst, in0=src, scalar1=factor, scalar2=None, op0=ALU.mult)
             else:
                 nc.scalar.activation(out=dst, in_=src, func=ACT.Copy, scale=factor)
 
-        def weave_z(b, j0, n, on_vector):
-            zword[b, j0] = keep.tile([P, n * PACK], BF16, name="zword%d_%d" % (b, j0), align_bytes=64)
+        def weave_z(b, j0, n, on_vector, base=None):
+            if base is None:
+                base = j0
+                zword[b, j0] = keep.tile([P, n * PACK], BF16, name="zword%d_%d" % (b, j0), align_bytes=64)
+            else:
+                zword[b, j0] = zplane[B_PASSES - 1, 0][:].rearrange("p t j -> p (t j)")
             dst = zword[b, j0][:].rearrange("p (c i t) -> p c t i", i=4, t=PACK)
-            src = zplane[b, j0][:].rearrange("p t (c i) -> p c t i", i=4)
+            src = zplane[b, base][:, :, j0 - base : j0 - base + n].rearrange("p t (c i) -> p c t i", i=4)
             if on_vector:
                 nc.vector.tensor_copy(out=dst, in_=src)
             else:
@@ -293,10 +308,11 @@ def tile_list_clamped_landmark_differences_kernel(
                 in_=yc[j0][:].bitcast(I32).rearrange("p (g m) -> p g m", g=GROUPS),
             )
 
-        cast_w1(0, 0, 0, 44, False)
-        cast_w1(0, 0, 44, P, True)
+        cast_w1(0, 0, 0, 64, False)
+        cast_w1(0, 0, 64, P, True)
         load_w1(2, 0, "slot_d")
         quant_w1(0, 0)
+        w1_bf[0, 1] = w1_bf[0, 0]
         cast_w1(0, 1, 0, 44, False)
         cast_w1(0, 1, 44, P, True)
         load_w1(2, 1, "slot_e")
@@ -310,8 +326,8 @@ def tile_list_clamped_landmark_differences_kernel(
         cast_w1(1, 0, 0, P, False)
         make_h(2)
         cast_w1(1, 1, 0, P, False)
-        gain_sb = keep.tile([P, B_PASSES, PACK], F32, name="gain_sb", tag="slot_b")
-        bias_sb = keep.tile([P, GROUPS, PACK], F32, name="bias_sb", tag="slot_c")
+        gain_sb = keep.tile([P, B_PASSES, PACK], F32, name="gain_sb", tag="slot_f")
+        bias_sb = keep.tile([P, GROUPS, PACK], F32, name="bias_sb", tag="slot_b")
         nc.sync.dma_start(out=gain_sb[:], in_=gain.rearrange("(b p t) -> p b t", b=B_PASSES, t=PACK))
         nc.sync.dma_start(out=bias_sb[:], in_=bias.rearrange("(g p t) -> p g t", g=GROUPS, t=PACK))
         make_h(3)
@@ -334,85 +350,89 @@ def tile_list_clamped_landmark_differences_kernel(
                     weigh(0, u, 0, PAIRS)
             if s == 6:
                 weave_z(0, 0, PAIRS, False)
-                for u in range(PACK):
-                    make_h(PACK * last + u)
+                make_h(PACK * last)
+                make_h(PACK * last + 1)
 
         (j0, n0), (j1, n1), (j2, n2) = LAST_PIECES
         pick_second(last, 0, j0, n0)
         pick_diff(1, 3, 0, PAIRS)
-        pick_second(last, 1, j0, n0)
-        for t in range(PACK):
+        for t in range(3):
             weigh(1, t, 0, PAIRS)
-        pick_diff(last, 0, j0, n0)
-        pick_second(last, 2, j0, n0)
+        make_h(PACK * last + 2)
+        make_h(PACK * last + 3)
+        weigh(1, 3, 0, PAIRS)
+        weave_z(1, j0, n0, False)
         quant_z(0, 0, PAIRS)
-        for piece in LAST_PIECES:
-            for g in range(GROUPS):
-                mul_z(0, *piece, g)
-        pick_diff(last, 1, j0, n0)
-        pick_second(last, 3, j0, n0)
-        pick_diff(last, 2, j0, n0)
-        pick_second(last, 0, j1, n1)
-        pick_diff(last, 3, j0, n0)
-        weave_z(1, 0, PAIRS, True)
-        quant_z(1, 0, PAIRS)
         for g in range(GROUPS):
-            mul_z(1, j0, n0, g)
+            mul_z(0, j0, n0, g)
+        pick_diff(last, 0, j0, n0)
+        for t in range(1, PACK):
+            pick_second(last, t, j0, n0)
+            pick_diff(last, t, j0, n0)
         for t in range(PACK):
             weigh(last, t, j0, n0)
+        weave_z(last, j0, n0, False)
+        weave_z(1, j1, PAIRS - j1, False, 0)
+        for piece in LAST_PIECES[1:]:
+            for g in range(GROUPS):
+                mul_z(0, *piece, g)
+        pick_second(last, 0, j1, n1)
         pick_second(last, 1, j1, n1)
+        quant_z(1, j0, n0)
+        for g in range(GROUPS):
+            mul_z(1, j0, n0, g)
         pick_diff(last, 0, j1, n1)
-        pick_second(last, 2, j1, n1)
         pick_diff(last, 1, j1, n1)
-        weave_z(last, j0, n0, True)
-        pick_diff(last, 2, j1, n1)
+        pick_second(last, 2, j1, n1)
         quant_z(last, j0, n0)
         for g in range(GROUPS):
             mul_z(last, j0, n0, g)
             add_bias(j0, n0, g, False)
             weave_y(j0, n0, g, False)
+        pick_diff(last, 2, j1, n1)
+        pick_second(last, 3, j1, n1)
+        pick_second(last, 0, j2, n2)
+        quant_z(1, j1, PAIRS - j1)
         for piece in LAST_PIECES[1:]:
             for g in range(GROUPS):
                 mul_z(1, *piece, g)
-        pick_second(last, 0, j2, n2)
-        pick_second(last, 3, j1, n1)
-        pick_second(last, 1, j2, n2)
         pick_diff(last, 3, j1, n1)
-        pick_diff(last, 0, j2, n2)
+        pick_second(last, 1, j2, n2)
         clamp(last, 0, PACK, j1)
-        pick_diff(last, 1, j2, n2)
+        pick_diff(last, 0, j2, n2)
         for t in range(PACK):
             weigh(last, t, j1, n1, True)
-        pick_second(last, 3, j2, n2)
+        pick_diff(last, 1, j2, n2)
         weave_z(last, j1, n1, True)
-        pick_diff(last, 3, j2, n2)
+        pick_second(last, 2, j2, n2)
         quant_z(last, j1, n1)
         for g in range(GROUPS):
             mul_z(last, j1, n1, g)
+        pick_second(last, 3, j2, n2)
         clamp(last, 0, 2, j2)
-        pick_second(last, 2, j2, n2)
-        clamp(last, 3, 4, j2)
-        for t in (0, 1, 3):
-            weigh(last, t, j2, n2, True)
         pick_diff(last, 2, j2, n2)
-        clamp(last, 2, 3, j2)
+        weigh(last, 0, j2, n2, True)
+        weigh(last, 1, j2, n2, True)
+        pick_diff(last, 3, j2, n2)
         add_bias(j1, n1, 0, True)
+        clamp(last, 2, PACK, j2)
+        add_bias(j1, n1, 1, False)
         weigh(last, 2, j2, n2, True)
-        add_bias(j1, n1, 1, True)
-        weave_z(last, j2, n2, True)
+        weigh(last, 3, j2, n2, True)
         quant_y(j0, n0, 0)
+        weave_z(last, j2, n2, True)
+        weave_y(j1, n1, 0, True)
         quant_z(last, j2, n2)
         for g in range(GROUPS):
             mul_z(last, j2, n2, g)
-        weave_y(j1, n1, 0, True)
-        weave_y(j1, n1, 1, True)
+        weave_y(j1, n1, 1, False)
         quant_y(j1, n1, 0)
         quant_y(j1, n1, 1)
         store_codes(j1, n1)
-        add_bias(j2, n2, 0, True)
-        add_bias(j2, n2, 1, False)
         quant_y(j0, n0, 1)
         store_codes(j0, n0)
+        add_bias(j2, n2, 0, True)
+        add_bias(j2, n2, 1, False)
         weave_y(j2, n2, 0, True)
         weave_y(j2, n2, 1, True)
         quant_y(j2, n2, 0)

@@ -22,9 +22,13 @@ KP = P * PACK
 A_PASSES = K // KP
 B_PASSES = H // KP
 GROUPS = N // KP
-QUARTER = 128
-QUARTERS = PAIRS // QUARTER
-LAST_PIECES = ((0, 256), (256, 128), (384, 128))
+BANK = 512
+PIECE = 128
+PIECES = PAIRS // PIECE
+SCALAR_SHARE = 44
+AT_SCALES = 4 * PACK * KP - 64
+AT_TABLE = AT_SCALES + T - 64
+AT_FIRST = AT_TABLE + 4 * T
 
 
 def tile_list_clamped_landmark_differences_kernel(
@@ -33,411 +37,399 @@ def tile_list_clamped_landmark_differences_kernel(
     nc = tc.nc
     with ExitStack() as ctx:
         keep = ctx.enter_context(tc.tile_pool(name="keep", bufs=1))
-        ring = ctx.enter_context(tc.tile_pool(name="ring", bufs=2))
+        shared = ctx.enter_context(tc.tile_pool(name="shared", bufs=1))
         psum = ctx.enter_context(tc.psum_pool(name="psum", bufs=1))
 
         offs_sb = keep.tile([P, S // 16], U16, name="offs_sb")
         pos1_sb = keep.tile([P, PAIRS // 16], U16, name="pos1_sb")
         pos2_sb = keep.tile([P, PAIRS // 16], U16, name="pos2_sb")
-        tabs = keep.tile([P, T], U8, name="tabs")
-        w2w_raw = keep.tile([P, B_PASSES * 2 * N], U8, name="w2w_raw")
-        w2s_raw = keep.tile([P, B_PASSES * N], U8, name="w2s_raw")
-        w2w = keep.tile([P, B_PASSES * 2 * N], U8, name="w2w", align_bytes=64)
-        w2s = keep.tile([P, B_PASSES * N], U8, name="w2s", align_bytes=64)
-        vw = [keep.tile([P, S], U32, name="vw%d" % a, align_bytes=64) for a in range(A_PASSES)]
-        vs = keep.tile([P, S], U8, name="vs", align_bytes=64)
+        tabs = shared.tile([P, T], U8, name="tabs", offset=AT_SCALES, align_bytes=64)
+        w2w_raw = [keep.tile([P, 2 * N], U8, name="w2w_raw", tag=tag, align_bytes=64) for tag in ("slot_g", "slot_c", "slot_e")]
+        w2s_raw = keep.tile([P, N], U8, name="w2s_raw")
+        planes = keep.tile([P, B_PASSES * N], U8, name="planes", align_bytes=64)
+        w2s = planes[:].rearrange("p (u b c) -> p u b c", b=B_PASSES, c=2 * P)
         ys = keep.tile([P, GROUPS * PAIRS], U8, name="ys", align_bytes=64)
+        gain_sb = keep.tile([P, B_PASSES, PACK], F32, name="gain_sb")
+        bias_sb = keep.tile([P, GROUPS, PACK], F32, name="bias_sb")
 
-        nc.vector.memset(w2s_raw[:].bitcast(I32), 0)
-        nc.vector.memset(tabs[:].bitcast(I32), 0)
+        for tile in (tabs, w2s_raw, planes):
+            nc.vector.memset(tile[:].bitcast(I32), 0)
 
         w1_raw = {}
         tabw = {}
 
-        def load_w1(b, a, tag):
-            raw = keep.tile([P, PACK, KP], F32, name="w1_raw", tag=tag)
+        def load_w1(b, a, tag=None, offset=None):
+            if tag:
+                raw = keep.tile([P, PACK, KP], F32, name="w1_raw", tag=tag, align_bytes=64)
+            else:
+                raw = shared.tile([P, PACK, KP], F32, name="w1_raw%d%d" % (b, a), offset=offset, align_bytes=64)
             nc.sync.dma_start(
                 out=raw[:],
                 in_=w1[KP * a : KP * (a + 1), KP * b : KP * (b + 1)].rearrange("(p j) c -> p j c", j=PACK),
             )
             w1_raw[b, a] = raw
 
-        def load_table(a, tag):
-            tabw[a] = keep.tile([P, T], I32, name="tabw", tag=tag)
+        def load_table(a, tile):
+            tabw[a] = tile
             nc.sync.dma_start(out=tabw[a][:], in_=tab_words[a].rearrange("p t i -> p (t i)").bitcast(I32))
 
         nc.sync.dma_start(offs_sb[:], offs)
-        nc.sync.dma_start(
-            out=w2w_raw[:].bitcast(I32).rearrange("p (b c) -> p b c", b=B_PASSES),
-            in_=w2_words.bitcast(I32).rearrange("b p c -> p b c"),
-        )
-        load_table(0, "slot_b")
-        load_table(1, "slot_a")
-        load_w1(0, 0, "slot_d")
-        load_w1(0, 1, "slot_e")
         nc.sync.dma_start(pos2_sb[:], pos2)
         nc.sync.dma_start(pos1_sb[:], pos1)
-        load_w1(1, 0, "slot_f")
-        for quad in range(4):
-            nc.gpsimd.dma_start(
-                out=w2s_raw[32 * quad : 32 * quad + 4, :].bitcast(I32).rearrange("p (b c) -> p b c", b=B_PASSES),
-                in_=w2_scales[:, 4 * quad : 4 * quad + 4, :].bitcast(I32).rearrange("b r c -> r b c"),
-            )
-        for quad in range(4):
-            nc.gpsimd.dma_start(
-                out=tabs[32 * quad : 32 * quad + 4 * A_PASSES, :].bitcast(I32),
-                in_=tab_scales[:, 4 * quad : 4 * quad + 4, :].bitcast(I32),
-            )
+        for b in range(B_PASSES):
+            nc.sync.dma_start(out=w2w_raw[b][:].bitcast(I32), in_=w2_words[b].bitcast(I32))
+        nc.sync.dma_start(out=gain_sb[:], in_=gain.rearrange("(b p t) -> p b t", b=B_PASSES, t=PACK))
+        nc.sync.dma_start(out=bias_sb[:], in_=bias.rearrange("(g p t) -> p g t", g=GROUPS, t=PACK))
+        nc.sync.dma_start(out=tabs[0:P:4, :].bitcast(I32), in_=tab_scales.rearrange("a q t -> (a q) t").bitcast(I32))
+        nc.sync.dma_start(out=w2s_raw[0:96:2, :].bitcast(I32), in_=w2_scales.rearrange("b q c -> (b q) c").bitcast(I32))
+        load_table(0, shared.tile([P, T], I32, name="tabw0", offset=AT_FIRST, align_bytes=64))
+        load_w1(0, 0, "slot_d")
 
+        w2w = {}
+
+        def deal_w2_words(b, tile):
+            w2w[b] = tile
+            nc.vector.tensor_copy(
+                out=tile[:].bitcast(U16).rearrange("p (r t c i) -> p r c t i", t=PACK, c=16, i=8),
+                in_=w2w_raw[b][:].bitcast(U16).rearrange("p (r c i t) -> p r c t i", t=PACK, c=16, i=8),
+            )
+        deal_w2_words(0, keep.tile([P, 2 * N], U8, name="w2w0", align_bytes=64))
+        vs_picked = keep.tile([P, S], U8, name="vs_picked")
+        nc.vector.tensor_copy(out=vs_picked[:], in_=tabs[:].indirect(offs_sb[:]))
+
+        def move_table_scales(a):
+            for r in range(4):
+                nc.sync.dma_start(
+                    out=planes[r:P:32, S * a : S * (a + 1)].bitcast(I32),
+                    in_=vs_picked[64 * a + 4 * r : 64 * (a + 1) : 16, :].bitcast(I32),
+                )
+
+        move_table_scales(0)
+        load_table(1, shared.tile([P, T], I32, name="tabw1", offset=AT_TABLE, align_bytes=64))
+        move_table_scales(1)
+        load_w1(0, 1, offset=0)
+        deal_w2_words(1, shared.tile([P, 2 * N], U8, name="w2w1", offset=AT_SCALES + 64, align_bytes=64))
+        w2s_dealt = shared.tile([P, N], U8, name="w2s_dealt", offset=AT_SCALES + 64 + 2 * N, align_bytes=64)
         nc.vector.tensor_copy(
-            out=w2w[:].bitcast(U16).rearrange("p (r t c i) -> p r c t i", t=PACK, c=16, i=8),
-            in_=w2w_raw[:].bitcast(U16).rearrange("p (r c i t) -> p r c t i", t=PACK, c=16, i=8),
-        )
-        nc.vector.tensor_copy(
-            out=w2s[:].rearrange("p (r t c i) -> p r c t i", t=PACK, c=8, i=16),
+            out=w2s_dealt[:].rearrange("p (r t c i) -> p r c t i", t=PACK, c=8, i=16),
             in_=w2s_raw[:].rearrange("p (r c i t) -> p r c t i", t=PACK, c=8, i=16),
         )
+        deal_w2_words(2, keep.tile([P, 2 * N], U8, name="w2w2", tag="slot_c", align_bytes=64))
+        vw = [keep.tile([P, S], U32, name="vw0", align_bytes=64)]
         nc.vector.tensor_copy(out=vw[0][:], in_=tabw[0][:].bitcast(U32).indirect(offs_sb[:]))
-        nc.vector.tensor_copy(out=vs[:], in_=tabs[:].indirect(offs_sb[:]))
-        load_w1(1, 1, "slot_b")
-        nc.vector.tensor_copy(out=vw[1][:], in_=tabw[1][:].bitcast(U32).indirect(offs_sb[:]))
 
         w1_bf = {}
         w1c = {}
         w1s = {}
 
-        def cast_w1(b, a, m0, m1, on_vector):
-            if (b, a) not in w1_bf:
-                w1_bf[b, a] = ring.tile([P, PACK * KP], BF16, name="w1_bf", bufs=3, align_bytes=64)
+        def copy_on(engine, dst, src):
+            if engine is nc.scalar:
+                nc.scalar.copy(out=dst, in_=src)
+            else:
+                engine.tensor_copy(out=dst, in_=src)
+
+        def take_bf(b, a, tag):
+            w1_bf[b, a] = keep.tile([P, PACK * KP], BF16, name="w1_bf", tag=tag, align_bytes=64)
+
+        def cast_w1(b, a, engine, m0=0, m1=P):
             dst = w1_bf[b, a][:].rearrange("p (t m j) -> p m t j", t=PACK, j=PACK)[:, m0:m1]
             src = w1_raw[b, a][:].rearrange("p j (m t) -> p m t j", t=PACK)[:, m0:m1]
-            if on_vector:
-                nc.vector.tensor_copy(out=dst, in_=src)
-            else:
-                nc.scalar.copy(out=dst, in_=src)
+            copy_on(engine, dst, src)
 
-        def quant_w1(b, a, t0=0, t1=PACK):
-            if (b, a) not in w1c:
-                w1c[b, a] = keep.tile([P, KP], U32, name="w1c%d%d" % (b, a), align_bytes=64)
+        def quant_w1(b, a, t0=0, t1=PACK, at=None):
+            if (b, a) not in w1s:
                 w1s[b, a] = keep.tile([P, KP], U8, name="w1s%d%d" % (b, a), align_bytes=64)
+            if at is None:
+                codes = keep.tile([P, P * (t1 - t0)], U32, name="w1c", tag="codes%d%d%d" % (b, a, t0), align_bytes=64)
+            else:
+                codes = shared.tile([P, P * (t1 - t0)], U32, name="w1c%d%d" % (b, a), offset=at, align_bytes=64)
+            for t in range(t0, t1):
+                w1c[b, a, t] = codes[:, P * (t - t0) : P * (t - t0 + 1)]
             nc.vector.quantize_mx(
-                out=w1c[b, a][:, P * t0 : P * t1].bitcast(FP8X4),
+                out=codes[:].bitcast(FP8X4),
                 scales=w1s[b, a][:, P * t0 : P * t1],
                 in_=w1_bf[b, a][:, KP * t0 : KP * t1],
             )
 
         h = {}
 
-        def make_h(s, share=False):
+        def make_h(s, second_engine=nc.scalar):
             b, t = divmod(s, PACK)
-            h[s] = ring.tile([P, S], F32, name="h", bufs=8)
+            h[s] = keep.tile([P, S], F32, name="h%d" % s)
             cols = slice(P * t, P * (t + 1))
             for half in range(2):
-                acc = psum.tile([P, 512], F32, name="acc", tag="bank%d" % (4 + 2 * (s % 2) + half))
-                ent = slice(512 * half, 512 * (half + 1))
+                acc = psum.tile([P, BANK], F32, name="acc", tag="bank%d" % (2 * t + half))
+                ent = slice(BANK * half, BANK * (half + 1))
                 for a in range(A_PASSES):
                     nc.tensor.matmul_mx(
                         out=acc[:],
-                        lhsT=w1c[b, a][:, cols].bitcast(FP8X4),
+                        lhsT=w1c[b, a, t].bitcast(FP8X4),
                         lhsT_scale=w1s[b, a][:, cols],
                         rhs=vw[a][:, ent].bitcast(FP8X4),
-                        rhs_scale=vs[4 * a : P, ent],
+                        rhs_scale=planes[:, S * a + BANK * half : S * a + BANK * (half + 1)],
                         start=(a == 0),
                         stop=(a == A_PASSES - 1),
                     )
-                if share and half == 1:
-                    nc.vector.tensor_copy(out=h[s][:, ent], in_=acc[:])
-                else:
-                    nc.scalar.copy(out=h[s][:, ent], in_=acc[:])
+                copy_on(second_engine if half else nc.scalar, h[s][:, ent], acc[:])
 
-        second = {}
-        after_z = {
-            (3, 0): ((0, 0), 0),
-            (0, 256): ((0, 0), 0),
-            (1, 256): ((0, 0), 128),
-            (2, 256): ((1, 0), 0),
-            (3, 256): ((2, 0), 0),
-            (0, 384): ((2, 0), 128),
-            (1, 384): ((1, 256), 0),
-            (2, 384): ((1, 256), 128),
-            (3, 384): ((1, 256), 256),
-        }
-        after_quant = {(0, 2): (1, 0), (0, 3): (1, 1), (1, 1): (2, 0), (1, 2): (2, 1)}
-        second_ring = [keep.tile([P, PAIRS], F32, name="second%d" % i) for i in range(3)]
-        diff = {}
-        zplane = {}
-        zword = {}
+        def pick_second(s, dst, j0, n):
+            nc.vector.tensor_copy(out=dst, in_=h[s][:].indirect(pos2_sb[:, j0 // 16 : (j0 + n) // 16]))
+
+        def pick_diff(s, dst, second, j0, n):
+            nc.vector.tensor_tensor(
+                out=dst,
+                in0=h[s][:].indirect(pos1_sb[:, j0 // 16 : (j0 + n) // 16]),
+                in1=second,
+                op=ALU.subtract,
+            )
+
+        def clamp(engine, dst, src):
+            engine.tensor_scalar(out=dst, in0=src, scalar1=1.0, scalar2=-1.0, op0=ALU.min, op1=ALU.max)
+
+        def weigh(b, t, dst, src):
+            nc.scalar.activation(out=dst, in_=src, func=ACT.Copy, scale=gain_sb[:, b, t : t + 1])
+
+        def weave(engine, dst, src):
+            copy_on(
+                engine,
+                dst.rearrange("p (c i t) -> p c t i", i=4, t=PACK),
+                src.rearrange("p t (c i) -> p c t i", i=4),
+            )
+
         zc = {}
         zs = {}
 
-        def pick_second(b, t, j0, n):
-            if (b, t) in after_quant:
-                g2 = w1_bf[after_quant[b, t]][:].bitcast(F32)[:, 0:n]
-            elif b == B_PASSES - 1 and (t, j0) in after_z:
-                key, c0 = after_z[t, j0]
-                g2 = zword[key][:].bitcast(F32)[:, c0 : c0 + n]
-            else:
-                g2 = second_ring[len(second) % 3][:, 0:n]
-            step = n // 2 if n > QUARTER else n
-            for c in range(0, n, step):
-                nc.vector.tensor_copy(
-                    out=g2[:, c : c + step],
-                    in_=h[PACK * b + t][:].indirect(pos2_sb[:, (j0 + c) // 16 : (j0 + c + step) // 16]),
-                )
-            second[b, t, j0] = g2
-
-        def pick_diff(b, t, j0, n):
-            if (b, j0) not in diff:
-                diff[b, j0] = ring.tile([P, PACK, n], F32, name="diff", tag="diff", bufs=3)
-            step = n // 2 if n > QUARTER else n
-            for c in range(0, n, step):
-                nc.vector.tensor_tensor(
-                    out=diff[b, j0][:, t, c : c + step],
-                    in0=h[PACK * b + t][:].indirect(pos1_sb[:, (j0 + c) // 16 : (j0 + c + step) // 16]),
-                    in1=second[b, t, j0][:, c : c + step],
-                    op=ALU.subtract,
-                )
-            if n > QUARTER:
-                clamp(b, t, t + 1, j0, nc.gpsimd)
-
-        def clamp(b, t0, t1, j0, engine=nc.vector):
-            d = diff[b, j0][:, t0:t1, :]
-            engine.tensor_scalar(out=d, in0=d, scalar1=1.0, scalar2=-1.0, op0=ALU.min, op1=ALU.max)
-
-        def weigh(b, t, j0, n, on_vector=False):
-            if (b, j0) not in zplane:
-                zplane[b, j0] = keep.tile([P, PACK, n], BF16, name="zplane%d_%d" % (b, j0), align_bytes=64)
-            dst, src, factor = zplane[b, j0][:, t, :], diff[b, j0][:, t, :], gain_sb[:, b, t : t + 1]
-            if on_vector:
-                nc.vector.tensor_scalar(out=dst, in0=src, scalar1=factor, scalar2=None, op0=ALU.mult)
-            else:
-                nc.scalar.activation(out=dst, in_=src, func=ACT.Copy, scale=factor)
-
-        def weave_z(b, j0, n, on_vector, base=None):
-            if base is None:
-                base = j0
-                zword[b, j0] = keep.tile([P, n * PACK], BF16, name="zword%d_%d" % (b, j0), align_bytes=64)
-            else:
-                zword[b, j0] = zplane[B_PASSES - 1, 0][:].rearrange("p t j -> p (t j)")
-            dst = zword[b, j0][:].rearrange("p (c i t) -> p c t i", i=4, t=PACK)
-            src = zplane[b, base][:, :, j0 - base : j0 - base + n].rearrange("p t (c i) -> p c t i", i=4)
-            if on_vector:
-                nc.vector.tensor_copy(out=dst, in_=src)
-            else:
-                nc.scalar.copy(out=dst, in_=src)
-
-        def quant_z(b, j0, n):
-            codes = keep.tile([P, n], U32, name="zc%d_%d" % (b, j0), align_bytes=64)
-            scales = keep.tile([P, n], U8, name="zs%d_%d" % (b, j0), align_bytes=64)
-            nc.vector.quantize_mx(out=codes[:].bitcast(FP8X4), scales=scales[:], in_=zword[b, j0][:])
-            for q in range(j0 // QUARTER, (j0 + n) // QUARTER):
-                cols = slice(QUARTER * q - j0, QUARTER * (q + 1) - j0)
+        def quant_z(b0, b1, q, words):
+            n = PIECE * (b1 - b0)
+            codes = keep.tile([P, n], U32, name="zc%d_%d" % (b0, q), align_bytes=64)
+            scales = keep.tile([P, n], U8, name="zs%d_%d" % (b0, q), align_bytes=64)
+            nc.vector.quantize_mx(out=codes[:].bitcast(FP8X4), scales=scales[:], in_=words)
+            for b in range(b0, b1):
+                cols = slice(PIECE * (b - b0), PIECE * (b - b0 + 1))
                 zc[b, q] = codes[:, cols]
                 zs[b, q] = scales[:, cols]
 
         yacc = {}
 
-        def mul_z(b, j0, n, g):
-            per_bank = KP // n
-            for u in range(PACK // per_bank):
-                if (j0, g, u) not in yacc:
-                    bank = 2 * (j0 // QUARTER) + g * (PACK // per_bank) + u
-                    yacc[j0, g, u] = psum.tile([P, per_bank, n], F32, name="yacc", tag="bank%d" % bank)
-                for i in range(per_bank):
-                    col = (b * GROUPS + g) * KP + (per_bank * u + i) * P
-                    for c in range(0, n, QUARTER):
-                        q = (j0 + c) // QUARTER
-                        nc.tensor.matmul_mx(
-                            out=yacc[j0, g, u][:, i, c : c + QUARTER],
-                            lhsT=w2w[:, 2 * col : 2 * (col + P)].bitcast(FP4X4),
-                            lhsT_scale=w2s[:, col : col + P],
-                            rhs=zc[b, q].bitcast(FP8X4),
-                            rhs_scale=zs[b, q],
-                            start=(b == 0 and i == 0 and c == 0),
-                            stop=(b == B_PASSES - 1 and i == per_bank - 1 and c == n - QUARTER),
-                        )
+        def mul_z(b, q):
+            for g in range(GROUPS):
+                if b == 0:
+                    yacc[q, g] = psum.tile([P, PACK, PIECE], F32, name="yacc", tag="bank%d" % (GROUPS * q + g))
+                for t in range(PACK):
+                    col = g * KP + t * P
+                    nc.tensor.matmul_mx(
+                        out=yacc[q, g][:, t, :],
+                        lhsT=w2w[b][:, 2 * col : 2 * (col + P)].bitcast(FP4X4),
+                        lhsT_scale=w2s[:, 2 * g + t // 2, b, P * (t % 2) : P * (t % 2 + 1)],
+                        rhs=zc[b, q].bitcast(FP8X4),
+                        rhs_scale=zs[b, q],
+                        start=(b == 0 and t == 0),
+                        stop=(b == B_PASSES - 1 and t == PACK - 1),
+                    )
 
         y = {}
         yword = {}
         yc = {}
 
-        def add_bias(j0, n, g, on_vector):
-            y[j0, g] = keep.tile([P, PACK, n], F32, name="y%d_%d" % (j0, g))
-            per_bank = KP // n
-            if on_vector:
+        def add_bias(q, g, engine):
+            y[q, g] = keep.tile([P, PACK, PIECE], F32, name="y%d_%d" % (q, g))
+            if engine is nc.vector:
                 nc.vector.tensor_tensor(
-                    out=y[j0, g][:],
-                    in0=yacc[j0, g, 0][:],
-                    in1=bias_sb[:, g, :].unsqueeze(2).to_broadcast([P, PACK, n]),
+                    out=y[q, g][:],
+                    in0=yacc[q, g][:],
+                    in1=bias_sb[:, g, :].unsqueeze(2).to_broadcast([P, PACK, PIECE]),
                     op=ALU.add,
                 )
             else:
                 for t in range(PACK):
                     nc.scalar.activation(
-                        out=y[j0, g][:, t, :],
-                        in_=yacc[j0, g, t // per_bank][:, t % per_bank, :],
-                        func=ACT.Identity,
-                        bias=bias_sb[:, g, t : t + 1],
+                        out=y[q, g][:, t, :], in_=yacc[q, g][:, t, :], func=ACT.Identity, bias=bias_sb[:, g, t : t + 1]
                     )
             nc.sync.dma_start(
-                out=out_0[KP * g : KP * (g + 1), j0 : j0 + n].rearrange("(p t) j -> p t j", t=PACK),
-                in_=y[j0, g][:],
+                out=out_0[KP * g : KP * (g + 1), PIECE * q : PIECE * (q + 1)].rearrange("(p t) j -> p t j", t=PACK),
+                in_=y[q, g][:],
             )
 
-        def weave_y(j0, n, g, on_vector):
-            yword[j0, g] = keep.tile([P, n * PACK], BF16, name="yword%d_%d" % (j0, g), align_bytes=64)
-            dst = yword[j0, g][:].rearrange("p (c i t) -> p c t i", i=4, t=PACK)
-            src = y[j0, g][:].rearrange("p t (c i) -> p c t i", i=4)
-            if on_vector:
-                nc.vector.tensor_copy(out=dst, in_=src)
-            else:
-                nc.scalar.copy(out=dst, in_=src)
+        def weave_y(q, g, engine):
+            yword[q, g] = keep.tile([P, PIECE * PACK], BF16, name="yword%d_%d" % (q, g), align_bytes=64)
+            weave(engine, yword[q, g][:], y[q, g][:])
 
-        def quant_y(j0, n, g):
-            if j0 not in yc:
-                yc[j0] = keep.tile([P, GROUPS * n], U32, name="yc%d" % j0, align_bytes=64)
-            nc.vector.quantize_mx(
-                out=yc[j0][:, n * g : n * (g + 1)].bitcast(FP8X4),
-                scales=ys[:, PAIRS * g + j0 : PAIRS * g + j0 + n],
-                in_=yword[j0, g][:],
-            )
-
-        def store_codes(j0, n):
+        def quant_y(q):
+            yc[q] = keep.tile([P, GROUPS * PIECE], U32, name="yc%d" % q, align_bytes=64)
+            for g in range(GROUPS):
+                nc.vector.quantize_mx(
+                    out=yc[q][:, PIECE * g : PIECE * (g + 1)].bitcast(FP8X4),
+                    scales=ys[:, PAIRS * g + PIECE * q : PAIRS * g + PIECE * (q + 1)],
+                    in_=yword[q, g][:],
+                )
             nc.sync.dma_start(
-                out=out_1[:, :, j0 : j0 + n, :].rearrange("g p m t -> p g (m t)").bitcast(I32),
-                in_=yc[j0][:].bitcast(I32).rearrange("p (g m) -> p g m", g=GROUPS),
+                out=out_1[:, :, PIECE * q : PIECE * (q + 1), :].rearrange("g p m t -> p g (m t)").bitcast(I32),
+                in_=yc[q][:].bitcast(I32).rearrange("p (g m) -> p g m", g=GROUPS),
             )
 
-        cast_w1(0, 0, 0, 64, False)
-        cast_w1(0, 0, 64, P, True)
-        load_w1(2, 0, "slot_d")
+        take_bf(0, 0, "bf00")
+        cast_w1(0, 0, nc.scalar)
+        load_w1(1, 0, offset=AT_FIRST)
+        load_w1(1, 1, "slot_d")
         quant_w1(0, 0)
-        w1_bf[0, 1] = w1_bf[0, 0]
-        cast_w1(0, 1, 0, 44, False)
-        cast_w1(0, 1, 44, P, True)
-        load_w1(2, 1, "slot_e")
+        vw.append(keep.tile([P, S], U32, name="vw1", tag="bf00", align_bytes=64))
+        nc.vector.tensor_copy(out=vw[1][:], in_=tabw[1][:].bitcast(U32).indirect(offs_sb[:]))
+        load_w1(2, 0, offset=AT_TABLE + 2 * T)
+        w1_bf[0, 1] = shared.tile([P, PACK * KP], BF16, name="w1_bf01", offset=AT_TABLE, align_bytes=64)
+        cast_w1(0, 1, nc.scalar, 0, SCALAR_SHARE)
+        cast_w1(0, 1, nc.vector, SCALAR_SHARE, P)
         quant_w1(0, 1, 0, 1)
         quant_w1(0, 1, 1, 2)
         quant_w1(0, 1, 2, 4)
-        make_h(0, True)
+        load_w1(2, 1, offset=AT_TABLE)
+        make_h(0, nc.vector)
         make_h(1)
-
-        last = B_PASSES - 1
-        cast_w1(1, 0, 0, P, False)
+        take_bf(1, 0, "codes011")
+        cast_w1(1, 0, nc.scalar)
         make_h(2)
-        cast_w1(1, 1, 0, P, False)
-        gain_sb = keep.tile([P, B_PASSES, PACK], F32, name="gain_sb", tag="slot_f")
-        bias_sb = keep.tile([P, GROUPS, PACK], F32, name="bias_sb", tag="slot_b")
-        nc.sync.dma_start(out=gain_sb[:], in_=gain.rearrange("(b p t) -> p b t", b=B_PASSES, t=PACK))
-        nc.sync.dma_start(out=bias_sb[:], in_=bias.rearrange("(g p t) -> p g t", g=GROUPS, t=PACK))
+        take_bf(2, 0, "bf20")
+        cast_w1(2, 0, nc.scalar)
         make_h(3)
-        for s in range(2 * PACK):
-            b, t = divmod(s, PACK)
-            if (b, t) in after_quant:
-                quant_w1(*after_quant[b, t])
-            pick_second(b, t, 0, PAIRS)
-            if s > 0:
-                pick_diff((s - 1) // PACK, (s - 1) % PACK, 0, PAIRS)
-            if s == 3:
-                make_h(4)
-                cast_w1(2, 0, 0, P, False)
-                make_h(5)
-                cast_w1(2, 1, 0, P, False)
-                make_h(6)
-                make_h(7)
-            if s == 4:
-                for u in range(PACK):
-                    weigh(0, u, 0, PAIRS)
-            if s == 6:
-                weave_z(0, 0, PAIRS, False)
-                make_h(PACK * last)
-                make_h(PACK * last + 1)
 
-        (j0, n0), (j1, n1), (j2, n2) = LAST_PIECES
-        pick_second(last, 0, j0, n0)
-        pick_diff(1, 3, 0, PAIRS)
-        for t in range(3):
-            weigh(1, t, 0, PAIRS)
-        make_h(PACK * last + 2)
-        make_h(PACK * last + 3)
-        weigh(1, 3, 0, PAIRS)
-        weave_z(1, j0, n0, False)
-        quant_z(0, 0, PAIRS)
-        for g in range(GROUPS):
-            mul_z(0, j0, n0, g)
-        pick_diff(last, 0, j0, n0)
-        for t in range(1, PACK):
-            pick_second(last, t, j0, n0)
-            pick_diff(last, t, j0, n0)
-        for t in range(PACK):
-            weigh(last, t, j0, n0)
-        weave_z(last, j0, n0, False)
-        weave_z(1, j1, PAIRS - j1, False, 0)
-        for piece in LAST_PIECES[1:]:
-            for g in range(GROUPS):
-                mul_z(0, *piece, g)
-        pick_second(last, 0, j1, n1)
-        pick_second(last, 1, j1, n1)
-        quant_z(1, j0, n0)
-        for g in range(GROUPS):
-            mul_z(1, j0, n0, g)
-        pick_diff(last, 0, j1, n1)
-        pick_diff(last, 1, j1, n1)
-        pick_second(last, 2, j1, n1)
-        quant_z(last, j0, n0)
-        for g in range(GROUPS):
-            mul_z(last, j0, n0, g)
-            add_bias(j0, n0, g, False)
-            weave_y(j0, n0, g, False)
-        pick_diff(last, 2, j1, n1)
-        pick_second(last, 3, j1, n1)
-        pick_second(last, 0, j2, n2)
-        quant_z(1, j1, PAIRS - j1)
-        for piece in LAST_PIECES[1:]:
-            for g in range(GROUPS):
-                mul_z(1, *piece, g)
-        pick_diff(last, 3, j1, n1)
-        pick_second(last, 1, j2, n2)
-        clamp(last, 0, PACK, j1)
-        pick_diff(last, 0, j2, n2)
-        for t in range(PACK):
-            weigh(last, t, j1, n1, True)
-        pick_diff(last, 1, j2, n2)
-        weave_z(last, j1, n1, True)
-        pick_second(last, 2, j2, n2)
-        quant_z(last, j1, n1)
-        for g in range(GROUPS):
-            mul_z(last, j1, n1, g)
-        pick_second(last, 3, j2, n2)
-        clamp(last, 0, 2, j2)
-        pick_diff(last, 2, j2, n2)
-        weigh(last, 0, j2, n2, True)
-        weigh(last, 1, j2, n2, True)
-        pick_diff(last, 3, j2, n2)
-        add_bias(j1, n1, 0, True)
-        clamp(last, 2, PACK, j2)
-        add_bias(j1, n1, 1, False)
-        weigh(last, 2, j2, n2, True)
-        weigh(last, 3, j2, n2, True)
-        quant_y(j0, n0, 0)
-        weave_z(last, j2, n2, True)
-        weave_y(j1, n1, 0, True)
-        quant_z(last, j2, n2)
-        for g in range(GROUPS):
-            mul_z(last, j2, n2, g)
-        weave_y(j1, n1, 1, False)
-        quant_y(j1, n1, 0)
-        quant_y(j1, n1, 1)
-        store_codes(j1, n1)
-        quant_y(j0, n0, 1)
-        store_codes(j0, n0)
-        add_bias(j2, n2, 0, True)
-        add_bias(j2, n2, 1, False)
-        weave_y(j2, n2, 0, True)
-        weave_y(j2, n2, 1, True)
-        quant_y(j2, n2, 0)
-        quant_y(j2, n2, 1)
-        store_codes(j2, n2)
+        diff0 = shared.tile([P, PACK, PAIRS], F32, name="diff0", offset=0, align_bytes=64)
+        zplane0 = keep.tile([P, PIECES, PACK, PIECE], BF16, name="zplane0", align_bytes=64)
+        zfirst = [keep.tile([P, 2, KP], BF16, name="zfirst%d" % q, align_bytes=64) for q in range(PIECES)]
+        half = PAIRS // 2
+
+        def first_pass(t, seconds, between=None):
+            for u in range(2):
+                pick_second(t, seconds[u], half * u, half)
+            if between:
+                between()
+            for u in range(2):
+                pick_diff(t, diff0[:, t, half * u : half * (u + 1)], seconds[u], half * u, half)
+            clamp(nc.gpsimd, diff0[:, t, :], diff0[:, t, :])
+
+        def weigh0(t):
+            weigh(0, t, zplane0[:, :, t, :], diff0[:, t, :].rearrange("p (q j) -> p q j", q=PIECES))
+
+        def weave0(q):
+            weave(nc.scalar, zfirst[q][:, 0, :], zplane0[:, q])
+
+        def lent(offset):
+            tile = shared.tile([P, PAIRS], F32, name="lent%d" % offset, offset=offset, align_bytes=64)
+            return tile[:]
+
+        def halves(words):
+            return words[:, 0:half], words[:, half:PAIRS]
+
+        spare = keep.tile([P, 5 * half], F32, name="spare", align_bytes=64)
+        first_pass(0, (spare[:, 0:half], spare[:, 4 * half : 5 * half]))
+        w1_bf[1, 1] = spare[:, 0 : 4 * half].bitcast(BF16)
+        cast_w1(1, 1, nc.vector)
+        spare = shared.tile([P, 5 * half], F32, name="spare_first", offset=AT_FIRST, align_bytes=64)
+        first_pass(
+            1,
+            (spare[:, 0:half], spare[:, 4 * half : 5 * half]),
+            lambda: (quant_w1(1, 0), quant_w1(1, 1, at=AT_FIRST + 20 * half)),
+        )
+        w1_bf[2, 1] = spare[:, 0 : 4 * half].bitcast(BF16)
+        cast_w1(2, 1, nc.vector)
+        second = halves(lent(AT_TABLE + 2 * T))
+        first_pass(2, second, lambda: (quant_w1(2, 0), quant_w1(2, 1, at=AT_TABLE + 2 * T + 4 * PAIRS)))
+        first_pass(3, second)
+        for s in range(PACK, 2 * PACK):
+            make_h(s)
+        weigh0(0)
+        for s in range(2 * PACK, 3 * PACK - 1):
+            make_h(s)
+        weigh0(1)
+        make_h(3 * PACK - 1)
+        for b in range(B_PASSES):
+            for r in range(4):
+                nc.sync.dma_start(
+                    out=w2s[r:P:32, :, b, :].bitcast(I32),
+                    in_=w2s_dealt[32 * b + 2 * r : 32 * (b + 1) : 8, :].rearrange("p (u c) -> p u c", c=2 * P).bitcast(I32),
+                )
+
+        ring = keep.tile([P, 3, PACK, PIECE], F32, name="ring")
+        seconds = [diff0[:, 0, :], diff0[:, 1, :]]
+        diff = {}
+        plane = {}
+        zlast = {}
+
+        def pick_unit(b, q, between=None):
+            k = 2 * q + b - 1
+            second = seconds[min(k, 1)].rearrange("p (t j) -> p t j", t=PACK)
+            diff[b, q] = ring[:, k % 3]
+            plane[b, q] = ring[:, (k + 2) % 3].bitcast(BF16)[:, :, 0:PIECE]
+            for t in range(PACK):
+                pick_second(PACK * b + t, second[:, t, :], PIECE * q, PIECE)
+            if between:
+                between()
+            for t in range(PACK):
+                pick_diff(PACK * b + t, diff[b, q][:, t, :], second[:, t, :], PIECE * q, PIECE)
+
+        def finish_unit(b, q, words, between=None):
+            clamp(nc.gpsimd, diff[b, q], diff[b, q])
+            for t in range(PACK):
+                weigh(b, t, plane[b, q][:, t, :], diff[b, q][:, t, :])
+            if between:
+                between()
+            weave(nc.scalar, words, plane[b, q])
+
+        def multiply_first(q):
+            quant_z(0, 2, q, zfirst[q][:].rearrange("p b c -> p (b c)"))
+            mul_z(0, q)
+            mul_z(1, q)
+
+        def multiply_last(q):
+            quant_z(2, 3, q, zlast[q][:])
+            mul_z(2, q)
+
+        def between_second(q):
+            if q >= 1:
+                multiply_first(q - 1)
+            if q >= 2:
+                quant_y(q - 2)
+
+        def between_third(q):
+            if q >= 1:
+                multiply_last(q - 1)
+                for g in range(GROUPS):
+                    add_bias(q - 1, g, nc.scalar)
+
+        for q in range(PIECES):
+            zlast[q] = keep.tile([P, KP], BF16, name="zlast%d" % q, align_bytes=64)
+            pick_unit(1, q, lambda: between_second(q))
+            finish_unit(1, q, zfirst[q][:, 1, :], (lambda: weave0(q)) if q else None)
+            if q == 0:
+                weigh0(2)
+                weigh0(3)
+                weave0(0)
+            pick_unit(2, q, lambda: between_third(q))
+            if q < PIECES - 1:
+                finish_unit(2, q, zlast[q][:])
+            if q >= 1:
+                for g in range(GROUPS):
+                    weave_y(q - 1, g, nc.scalar)
+
+        q = PIECES - 1
+        woven = ring[:, (2 * q + 2) % 3].rearrange("p t j -> p (t j)").rearrange("p (j t) -> p j t", t=PACK)
+        multiply_first(q)
+        clamp(
+            nc.vector,
+            woven.rearrange("p (c i) t -> p c t i", i=4),
+            diff[2, q].rearrange("p t (c i) -> p c t i", i=4),
+        )
+        nc.vector.tensor_tensor(
+            out=zlast[q][:].rearrange("p (j t) -> p j t", t=PACK),
+            in0=woven,
+            in1=gain_sb[:, 2, :].unsqueeze(1).to_broadcast([P, PIECE, PACK]),
+            op=ALU.mult,
+        )
+        multiply_last(q)
+        quant_y(q - 1)
+        add_bias(q, 0, nc.vector)
+        add_bias(q, 1, nc.scalar)
+        weave_y(q, 0, nc.vector)
+        weave_y(q, 1, nc.vector)
+        quant_y(q)
         for quad in range(4):
             eng = nc.scalar if quad % 2 else nc.sync
             eng.dma_start(

@@ -26,6 +26,7 @@ BANK = 512
 PIECE = 128
 PIECES = PAIRS // PIECE
 SCALAR_SHARE = 44
+VECTOR_SHARE = 320
 AT_SCALES = 4 * PACK * KP - 64
 AT_TABLE = AT_SCALES + T - 64
 AT_FIRST = AT_TABLE + 4 * T
@@ -196,76 +197,29 @@ def tile_list_clamped_landmark_differences_kernel(
                 src.rearrange("p t (c i) -> p c t i", i=4),
             )
 
-        zc = {}
-        zs = {}
+        zc = [keep.tile([P, PAIRS], U32, name="zc%d" % b, align_bytes=64) for b in range(B_PASSES)]
+        zs = [keep.tile([P, PAIRS], U8, name="zs%d" % b, align_bytes=64) for b in range(B_PASSES)]
 
-        def quant_z(b0, b1, q, words):
-            n = PIECE * (b1 - b0)
-            codes = keep.tile([P, n], U32, name="zc%d_%d" % (b0, q), align_bytes=64)
-            scales = keep.tile([P, n], U8, name="zs%d_%d" % (b0, q), align_bytes=64)
-            nc.vector.quantize_mx(out=codes[:].bitcast(FP8X4), scales=scales[:], in_=words)
-            for b in range(b0, b1):
-                cols = slice(PIECE * (b - b0), PIECE * (b - b0 + 1))
-                zc[b, q] = codes[:, cols]
-                zs[b, q] = scales[:, cols]
+        def quant_z(b, j0, n, words):
+            nc.vector.quantize_mx(out=zc[b][:, j0 : j0 + n].bitcast(FP8X4), scales=zs[b][:, j0 : j0 + n], in_=words)
 
         yacc = {}
 
-        def mul_z(b, q):
+        def mul_z(b):
             for g in range(GROUPS):
-                if b == 0:
-                    yacc[q, g] = psum.tile([P, PACK, PIECE], F32, name="yacc", tag="bank%d" % (GROUPS * q + g))
                 for t in range(PACK):
+                    if b == 0:
+                        yacc[g, t] = psum.tile([P, PAIRS], F32, name="yacc", tag="bank%d" % (PACK * g + t))
                     col = g * KP + t * P
                     nc.tensor.matmul_mx(
-                        out=yacc[q, g][:, t, :],
+                        out=yacc[g, t][:],
                         lhsT=w2w[b][:, 2 * col : 2 * (col + P)].bitcast(FP4X4),
                         lhsT_scale=w2s[:, 2 * g + t // 2, b, P * (t % 2) : P * (t % 2 + 1)],
-                        rhs=zc[b, q].bitcast(FP8X4),
-                        rhs_scale=zs[b, q],
-                        start=(b == 0 and t == 0),
-                        stop=(b == B_PASSES - 1 and t == PACK - 1),
+                        rhs=zc[b][:].bitcast(FP8X4),
+                        rhs_scale=zs[b][:],
+                        start=(b == 0),
+                        stop=(b == B_PASSES - 1),
                     )
-
-        y = {}
-        yword = {}
-        yc = {}
-
-        def add_bias(q, g, engine):
-            y[q, g] = keep.tile([P, PACK, PIECE], F32, name="y%d_%d" % (q, g))
-            if engine is nc.vector:
-                nc.vector.tensor_tensor(
-                    out=y[q, g][:],
-                    in0=yacc[q, g][:],
-                    in1=bias_sb[:, g, :].unsqueeze(2).to_broadcast([P, PACK, PIECE]),
-                    op=ALU.add,
-                )
-            else:
-                for t in range(PACK):
-                    nc.scalar.activation(
-                        out=y[q, g][:, t, :], in_=yacc[q, g][:, t, :], func=ACT.Identity, bias=bias_sb[:, g, t : t + 1]
-                    )
-            nc.sync.dma_start(
-                out=out_0[KP * g : KP * (g + 1), PIECE * q : PIECE * (q + 1)].rearrange("(p t) j -> p t j", t=PACK),
-                in_=y[q, g][:],
-            )
-
-        def weave_y(q, g, engine):
-            yword[q, g] = keep.tile([P, PIECE * PACK], BF16, name="yword%d_%d" % (q, g), align_bytes=64)
-            weave(engine, yword[q, g][:], y[q, g][:])
-
-        def quant_y(q):
-            yc[q] = keep.tile([P, GROUPS * PIECE], U32, name="yc%d" % q, align_bytes=64)
-            for g in range(GROUPS):
-                nc.vector.quantize_mx(
-                    out=yc[q][:, PIECE * g : PIECE * (g + 1)].bitcast(FP8X4),
-                    scales=ys[:, PAIRS * g + PIECE * q : PAIRS * g + PIECE * (q + 1)],
-                    in_=yword[q, g][:],
-                )
-            nc.sync.dma_start(
-                out=out_1[:, :, PIECE * q : PIECE * (q + 1), :].rearrange("g p m t -> p g (m t)").bitcast(I32),
-                in_=yc[q][:].bitcast(I32).rearrange("p (g m) -> p g m", g=GROUPS),
-            )
 
         take_bf(0, 0, "bf00")
         cast_w1(0, 0, nc.scalar)
@@ -287,149 +241,144 @@ def tile_list_clamped_landmark_differences_kernel(
         take_bf(1, 0, "codes011")
         cast_w1(1, 0, nc.scalar)
         make_h(2)
-        take_bf(2, 0, "bf20")
-        cast_w1(2, 0, nc.scalar)
         make_h(3)
+        take_bf(1, 1, "codes012")
+        cast_w1(1, 1, nc.scalar)
+        take_bf(2, 0, "codes000")
+        cast_w1(2, 0, nc.scalar)
 
-        diff0 = shared.tile([P, PACK, PAIRS], F32, name="diff0", offset=0, align_bytes=64)
-        zplane0 = keep.tile([P, PIECES, PACK, PIECE], BF16, name="zplane0", align_bytes=64)
-        zfirst = [keep.tile([P, 2, KP], BF16, name="zfirst%d" % q, align_bytes=64) for q in range(PIECES)]
         half = PAIRS // 2
+        diff = [
+            shared.tile([P, PACK, PAIRS], F32, name="diff0", offset=0, align_bytes=64),
+            keep.tile([P, PACK, PAIRS], F32, name="diff1"),
+        ]
+        zplane = [keep.tile([P, PACK, PAIRS], BF16, name="zplane%d" % b) for b in range(2)]
+        zword = [keep.tile([P, PACK * PAIRS], BF16, name="zword%d" % b, align_bytes=64) for b in range(B_PASSES)]
 
-        def first_pass(t, seconds, between=None):
-            for u in range(2):
-                pick_second(t, seconds[u], half * u, half)
+        def pick_slice(s, second, between=None):
+            b, t = divmod(s, PACK)
+            for j0 in (0, half):
+                pick_second(s, second[:, j0 : j0 + half], j0, half)
             if between:
                 between()
-            for u in range(2):
-                pick_diff(t, diff0[:, t, half * u : half * (u + 1)], seconds[u], half * u, half)
-            clamp(nc.gpsimd, diff0[:, t, :], diff0[:, t, :])
+            for j0 in (0, half):
+                pick_diff(s, diff[b][:, t, j0 : j0 + half], second[:, j0 : j0 + half], j0, half)
+            clamp(nc.gpsimd, diff[b][:, t, :], diff[b][:, t, :])
 
-        def weigh0(t):
-            weigh(0, t, zplane0[:, :, t, :], diff0[:, t, :].rearrange("p (q j) -> p q j", q=PIECES))
+        def finish_pass(b):
+            for t in range(PACK):
+                weigh(b, t, zplane[b][:, t, :], diff[b][:, t, :])
+            weave(nc.scalar, zword[b][:], zplane[b][:])
 
-        def weave0(q):
-            weave(nc.scalar, zfirst[q][:, 0, :], zplane0[:, q])
-
-        def lent(offset):
-            tile = shared.tile([P, PAIRS], F32, name="lent%d" % offset, offset=offset, align_bytes=64)
-            return tile[:]
-
-        def halves(words):
-            return words[:, 0:half], words[:, half:PAIRS]
-
-        spare = keep.tile([P, 5 * half], F32, name="spare", align_bytes=64)
-        first_pass(0, (spare[:, 0:half], spare[:, 4 * half : 5 * half]))
-        w1_bf[1, 1] = spare[:, 0 : 4 * half].bitcast(BF16)
-        cast_w1(1, 1, nc.vector)
-        spare = shared.tile([P, 5 * half], F32, name="spare_first", offset=AT_FIRST, align_bytes=64)
-        first_pass(
-            1,
-            (spare[:, 0:half], spare[:, 4 * half : 5 * half]),
-            lambda: (quant_w1(1, 0), quant_w1(1, 1, at=AT_FIRST + 20 * half)),
-        )
-        w1_bf[2, 1] = spare[:, 0 : 4 * half].bitcast(BF16)
-        cast_w1(2, 1, nc.vector)
-        second = halves(lent(AT_TABLE + 2 * T))
-        first_pass(2, second, lambda: (quant_w1(2, 0), quant_w1(2, 1, at=AT_TABLE + 2 * T + 4 * PAIRS)))
-        first_pass(3, second)
-        for s in range(PACK, 2 * PACK):
+        spare = keep.tile([P, PAIRS], F32, name="spare")
+        pick_slice(0, spare[:])
+        pick_slice(1, spare[:])
+        pick_slice(2, w1_raw[1, 0][:, 0, :], lambda: quant_w1(1, 0))
+        pick_slice(3, w1_raw[1, 1][:, 0, :], lambda: quant_w1(1, 1))
+        quant_w1(2, 0)
+        make_h(4)
+        make_h(5)
+        take_bf(2, 1, "codes011")
+        cast_w1(2, 1, nc.scalar)
+        make_h(6)
+        make_h(7)
+        pick_slice(4, spare[:])
+        pick_slice(5, w1_raw[2, 1][:, 0, :], lambda: quant_w1(2, 1))
+        pick_slice(6, spare[:])
+        pick_slice(7, spare[:])
+        for s in range(2 * PACK, 3 * PACK):
             make_h(s)
-        weigh0(0)
-        for s in range(2 * PACK, 3 * PACK - 1):
-            make_h(s)
-        weigh0(1)
-        make_h(3 * PACK - 1)
         for b in range(B_PASSES):
             for r in range(4):
                 nc.sync.dma_start(
                     out=w2s[r:P:32, :, b, :].bitcast(I32),
                     in_=w2s_dealt[32 * b + 2 * r : 32 * (b + 1) : 8, :].rearrange("p (u c) -> p u c", c=2 * P).bitcast(I32),
                 )
+        finish_pass(0)
+        finish_pass(1)
 
-        ring = keep.tile([P, 3, PACK, PIECE], F32, name="ring")
-        seconds = [diff0[:, 0, :], diff0[:, 1, :]]
-        diff = {}
-        plane = {}
-        zlast = {}
+        last = B_PASSES - 1
+        second = diff[0][:, 0, :]
+        wide = keep.tile([P, PACK, half], F32, name="wide")
+        wide_plane = keep.tile([P, PACK, half], BF16, name="wide_plane")
+        for t0 in (0, 2):
+            for u in range(2):
+                pick_second(PACK * last + t0 + u, second[:, half * u : half * (u + 1)], 0, half)
+            for u in range(2):
+                pick_diff(PACK * last + t0 + u, wide[:, t0 + u, :], second[:, half * u : half * (u + 1)], 0, half)
+            clamp(nc.gpsimd, wide[:, t0 : t0 + 2, :], wide[:, t0 : t0 + 2, :])
+        for t in range(PACK):
+            weigh(last, t, wide_plane[:, t, :], wide[:, t, :])
+        weave(nc.scalar, zword[last][:, 0 : PACK * half], wide_plane[:])
 
-        def pick_unit(b, q, between=None):
-            k = 2 * q + b - 1
-            second = seconds[min(k, 1)].rearrange("p (t j) -> p t j", t=PACK)
-            diff[b, q] = ring[:, k % 3]
-            plane[b, q] = ring[:, (k + 2) % 3].bitcast(BF16)[:, :, 0:PIECE]
+        def pick_piece(b, j0):
+            narrow = zplane[b][:].bitcast(F32)[:, :, 0:PIECE]
             for t in range(PACK):
-                pick_second(PACK * b + t, second[:, t, :], PIECE * q, PIECE)
-            if between:
-                between()
+                pick_second(PACK * last + t, second[:, PIECE * t : PIECE * (t + 1)], j0, PIECE)
+            quant_z(b, 0, PAIRS, zword[b][:])
+            mul_z(b)
             for t in range(PACK):
-                pick_diff(PACK * b + t, diff[b, q][:, t, :], second[:, t, :], PIECE * q, PIECE)
+                pick_diff(PACK * last + t, narrow[:, t, :], second[:, PIECE * t : PIECE * (t + 1)], j0, PIECE)
+            return narrow
 
-        def finish_unit(b, q, words, between=None):
-            clamp(nc.gpsimd, diff[b, q], diff[b, q])
-            for t in range(PACK):
-                weigh(b, t, plane[b, q][:, t, :], diff[b, q][:, t, :])
-            if between:
-                between()
-            weave(nc.scalar, words, plane[b, q])
+        narrow = pick_piece(0, half)
+        narrow_plane = keep.tile([P, PACK, PIECE], BF16, name="narrow_plane")
+        clamp(nc.gpsimd, narrow, narrow)
+        for t in range(PACK):
+            weigh(last, t, narrow_plane[:, t, :], narrow[:, t, :])
+        weave(nc.scalar, zword[last][:, PACK * half : PACK * (half + PIECE)], narrow_plane[:])
 
-        def multiply_first(q):
-            quant_z(0, 2, q, zfirst[q][:].rearrange("p b c -> p (b c)"))
-            mul_z(0, q)
-            mul_z(1, q)
-
-        def multiply_last(q):
-            quant_z(2, 3, q, zlast[q][:])
-            mul_z(2, q)
-
-        def between_second(q):
-            if q >= 1:
-                multiply_first(q - 1)
-            if q >= 2:
-                quant_y(q - 2)
-
-        def between_third(q):
-            if q >= 1:
-                multiply_last(q - 1)
-                for g in range(GROUPS):
-                    add_bias(q - 1, g, nc.scalar)
-
-        for q in range(PIECES):
-            zlast[q] = keep.tile([P, KP], BF16, name="zlast%d" % q, align_bytes=64)
-            pick_unit(1, q, lambda: between_second(q))
-            finish_unit(1, q, zfirst[q][:, 1, :], (lambda: weave0(q)) if q else None)
-            if q == 0:
-                weigh0(2)
-                weigh0(3)
-                weave0(0)
-            pick_unit(2, q, lambda: between_third(q))
-            if q < PIECES - 1:
-                finish_unit(2, q, zlast[q][:])
-            if q >= 1:
-                for g in range(GROUPS):
-                    weave_y(q - 1, g, nc.scalar)
-
-        q = PIECES - 1
-        woven = ring[:, (2 * q + 2) % 3].rearrange("p t j -> p (t j)").rearrange("p (j t) -> p j t", t=PACK)
-        multiply_first(q)
+        narrow = pick_piece(1, half + PIECE)
+        woven = wide_plane[:].rearrange("p t j -> p (t j)").bitcast(F32).rearrange("p (j t) -> p j t", t=PACK)
+        quant_z(last, 0, half, zword[last][:, 0 : PACK * half])
         clamp(
             nc.vector,
             woven.rearrange("p (c i) t -> p c t i", i=4),
-            diff[2, q].rearrange("p t (c i) -> p c t i", i=4),
+            narrow.rearrange("p t (c i) -> p c t i", i=4),
         )
         nc.vector.tensor_tensor(
-            out=zlast[q][:].rearrange("p (j t) -> p j t", t=PACK),
+            out=zword[last][:, PACK * (half + PIECE) :].rearrange("p (j t) -> p j t", t=PACK),
             in0=woven,
-            in1=gain_sb[:, 2, :].unsqueeze(1).to_broadcast([P, PIECE, PACK]),
+            in1=gain_sb[:, last, :].unsqueeze(1).to_broadcast([P, PIECE, PACK]),
             op=ALU.mult,
         )
-        multiply_last(q)
-        quant_y(q - 1)
-        add_bias(q, 0, nc.vector)
-        add_bias(q, 1, nc.scalar)
-        weave_y(q, 0, nc.vector)
-        weave_y(q, 1, nc.vector)
-        quant_y(q)
+        quant_z(last, half, half, zword[last][:, PACK * half :])
+        mul_z(last)
+
+        y = [keep.tile([P, PACK, PAIRS], F32, name="y%d" % g) for g in range(GROUPS)]
+        yword = [keep.tile([P, PACK * PAIRS], BF16, name="yword%d" % g, align_bytes=64) for g in range(GROUPS)]
+        yc = [keep.tile([P, PAIRS], U32, name="yc%d" % g, align_bytes=64) for g in range(GROUPS)]
+
+        def add_bias(g, t, engine):
+            if engine is nc.vector:
+                nc.vector.tensor_scalar(
+                    out=y[g][:, t, :], in0=yacc[g, t][:], scalar1=bias_sb[:, g, t : t + 1], scalar2=None, op0=ALU.add
+                )
+            else:
+                nc.scalar.activation(
+                    out=y[g][:, t, :], in_=yacc[g, t][:], func=ACT.Identity, bias=bias_sb[:, g, t : t + 1]
+                )
+            if t % 2:
+                nc.sync.dma_start(
+                    out=out_0[KP * g : KP * (g + 1), :].rearrange("(p t) j -> p t j", t=PACK)[:, t - 1 : t + 1, :],
+                    in_=y[g][:, t - 1 : t + 1, :],
+                )
+
+        def quant_y(g):
+            nc.vector.quantize_mx(
+                out=yc[g][:].bitcast(FP8X4), scales=ys[:, PAIRS * g : PAIRS * (g + 1)], in_=yword[g][:]
+            )
+            nc.sync.dma_start(out=out_1[g].rearrange("p m t -> p (m t)").bitcast(I32), in_=yc[g][:].bitcast(I32))
+
+        for t in range(PACK):
+            add_bias(0, t, nc.scalar if t % 2 else nc.vector)
+        weave(nc.vector, yword[0][:], y[0][:])
+        for t in range(PACK):
+            add_bias(1, t, nc.scalar)
+        quant_y(0)
+        weave(nc.vector, yword[1][:, 0 : PACK * VECTOR_SHARE], y[1][:, :, 0:VECTOR_SHARE])
+        weave(nc.scalar, yword[1][:, PACK * VECTOR_SHARE :], y[1][:, :, VECTOR_SHARE:])
+        quant_y(1)
         for quad in range(4):
             eng = nc.scalar if quad % 2 else nc.sync
             eng.dma_start(

@@ -191,11 +191,7 @@ def tile_list_clamped_landmark_differences_kernel(
             nc.scalar.activation(out=dst, in_=src, func=ACT.Copy, scale=gain_sb[:, b, t : t + 1])
 
         def weave(engine, dst, src):
-            copy_on(
-                engine,
-                dst.rearrange("p (c i t) -> p c t i", i=4, t=PACK),
-                src.rearrange("p t (c i) -> p c t i", i=4),
-            )
+            copy_on(engine, dst.rearrange("p (j t) -> p j t", t=PACK), src.rearrange("p t j -> p j t"))
 
         zc = [keep.tile([P, PAIRS], U32, name="zc%d" % b, align_bytes=64) for b in range(B_PASSES)]
         zs = [keep.tile([P, PAIRS], U8, name="zs%d" % b, align_bytes=64) for b in range(B_PASSES)]
@@ -331,11 +327,7 @@ def tile_list_clamped_landmark_differences_kernel(
         narrow = pick_piece(1, half + PIECE)
         woven = wide_plane[:].rearrange("p t j -> p (t j)").bitcast(F32).rearrange("p (j t) -> p j t", t=PACK)
         quant_z(last, 0, half, zword[last][:, 0 : PACK * half])
-        clamp(
-            nc.vector,
-            woven.rearrange("p (c i) t -> p c t i", i=4),
-            narrow.rearrange("p t (c i) -> p c t i", i=4),
-        )
+        clamp(nc.vector, woven, narrow.rearrange("p t j -> p j t"))
         nc.vector.tensor_tensor(
             out=zword[last][:, PACK * (half + PIECE) :].rearrange("p (j t) -> p j t", t=PACK),
             in0=woven,

@@ -25,8 +25,9 @@ GROUPS = N // KP
 BANK = 512
 PIECE = 128
 PIECES = PAIRS // PIECE
-SCALAR_SHARE = 44
-VECTOR_SHARE = 320
+SCALAR_SHARE = 52
+VECTOR_SHARE = 256
+LATER_SHARE = 104
 AT_SCALES = 4 * PACK * KP - 64
 AT_TABLE = AT_SCALES + T - 64
 AT_FIRST = AT_TABLE + 4 * T
@@ -190,8 +191,13 @@ def tile_list_clamped_landmark_differences_kernel(
         def weigh(b, t, dst, src):
             nc.scalar.activation(out=dst, in_=src, func=ACT.Copy, scale=gain_sb[:, b, t : t + 1])
 
-        def weave(engine, dst, src):
-            copy_on(engine, dst.rearrange("p (j t) -> p j t", t=PACK), src.rearrange("p t j -> p j t"))
+        def weave(engine, dst, src, width):
+            run = 8 // width
+            copy_on(
+                engine,
+                dst.rearrange("p (c i t) -> p c t i", i=run, t=PACK),
+                src.rearrange("p t (c i) -> p c t i", i=run),
+            )
 
         zc = [keep.tile([P, PAIRS], U32, name="zc%d" % b, align_bytes=64) for b in range(B_PASSES)]
         zs = [keep.tile([P, PAIRS], U8, name="zs%d" % b, align_bytes=64) for b in range(B_PASSES)]
@@ -237,11 +243,7 @@ def tile_list_clamped_landmark_differences_kernel(
         take_bf(1, 0, "codes011")
         cast_w1(1, 0, nc.scalar)
         make_h(2)
-        make_h(3)
-        take_bf(1, 1, "codes012")
-        cast_w1(1, 1, nc.scalar)
-        take_bf(2, 0, "codes000")
-        cast_w1(2, 0, nc.scalar)
+        take_bf(1, 1, "bf11")
 
         half = PAIRS // 2
         diff = [
@@ -253,24 +255,36 @@ def tile_list_clamped_landmark_differences_kernel(
 
         def pick_slice(s, second, between=None):
             b, t = divmod(s, PACK)
-            for j0 in (0, half):
-                pick_second(s, second[:, j0 : j0 + half], j0, half)
+            for u in range(2):
+                pick_second(s, second[u], half * u, half)
             if between:
                 between()
-            for j0 in (0, half):
-                pick_diff(s, diff[b][:, t, j0 : j0 + half], second[:, j0 : j0 + half], j0, half)
+            for u in range(2):
+                pick_diff(s, diff[b][:, t, half * u : half * (u + 1)], second[u], half * u, half)
             clamp(nc.gpsimd, diff[b][:, t, :], diff[b][:, t, :])
 
-        def finish_pass(b):
-            for t in range(PACK):
-                weigh(b, t, zplane[b][:, t, :], diff[b][:, t, :])
-            weave(nc.scalar, zword[b][:], zplane[b][:])
+        def halves(words):
+            return words[:, 0:half], words[:, half:PAIRS]
+
+        def weigh_slice(b, t):
+            weigh(b, t, zplane[b][:, t, :], diff[b][:, t, :])
+
+        def finish_pass(b, t0):
+            for t in range(t0, PACK):
+                weigh_slice(b, t)
+            weave(nc.scalar, zword[b][:], zplane[b][:], 2)
 
         spare = keep.tile([P, PAIRS], F32, name="spare")
-        pick_slice(0, spare[:])
-        pick_slice(1, spare[:])
-        pick_slice(2, w1_raw[1, 0][:, 0, :], lambda: quant_w1(1, 0))
-        pick_slice(3, w1_raw[1, 1][:, 0, :], lambda: quant_w1(1, 1))
+        pick_slice(0, (w1_bf[1, 1][:].bitcast(F32)[:, 0:half], spare[:, half:PAIRS]))
+        cast_w1(1, 1, nc.vector, LATER_SHARE, P)
+        cast_w1(1, 1, nc.scalar, 0, LATER_SHARE)
+        make_h(3)
+        take_bf(2, 0, "codes000")
+        cast_w1(2, 0, nc.scalar)
+        pick_slice(1, halves(spare[:]))
+        pick_slice(2, halves(w1_raw[1, 0][:, 0, :]), lambda: quant_w1(1, 0))
+        quant_w1(1, 1)
+        pick_slice(3, halves(spare[:]))
         quant_w1(2, 0)
         make_h(4)
         make_h(5)
@@ -278,26 +292,32 @@ def tile_list_clamped_landmark_differences_kernel(
         cast_w1(2, 1, nc.scalar)
         make_h(6)
         make_h(7)
-        pick_slice(4, spare[:])
-        pick_slice(5, w1_raw[2, 1][:, 0, :], lambda: quant_w1(2, 1))
-        pick_slice(6, spare[:])
-        pick_slice(7, spare[:])
-        for s in range(2 * PACK, 3 * PACK):
-            make_h(s)
+        pick_slice(4, halves(spare[:]))
+        pick_slice(5, halves(spare[:]))
+        pick_slice(6, halves(w1_raw[2, 1][:, 0, :]), lambda: quant_w1(2, 1))
+        pick_slice(7, halves(spare[:]))
+        for t in range(1, PACK):
+            weigh_slice(0, t)
+        make_h(8)
+        make_h(9)
+        weigh_slice(0, 0)
+        make_h(10)
+        make_h(11)
+        weigh_slice(1, 0)
         for b in range(B_PASSES):
             for r in range(4):
                 nc.sync.dma_start(
                     out=w2s[r:P:32, :, b, :].bitcast(I32),
                     in_=w2s_dealt[32 * b + 2 * r : 32 * (b + 1) : 8, :].rearrange("p (u c) -> p u c", c=2 * P).bitcast(I32),
                 )
-        finish_pass(0)
-        finish_pass(1)
+        finish_pass(0, PACK)
+        finish_pass(1, 1)
 
         last = B_PASSES - 1
-        second = diff[0][:, 0, :]
         wide = keep.tile([P, PACK, half], F32, name="wide")
         wide_plane = keep.tile([P, PACK, half], BF16, name="wide_plane")
         for t0 in (0, 2):
+            second = diff[t0 // 2][:, 0, :]
             for u in range(2):
                 pick_second(PACK * last + t0 + u, second[:, half * u : half * (u + 1)], 0, half)
             for u in range(2):
@@ -305,7 +325,7 @@ def tile_list_clamped_landmark_differences_kernel(
             clamp(nc.gpsimd, wide[:, t0 : t0 + 2, :], wide[:, t0 : t0 + 2, :])
         for t in range(PACK):
             weigh(last, t, wide_plane[:, t, :], wide[:, t, :])
-        weave(nc.scalar, zword[last][:, 0 : PACK * half], wide_plane[:])
+        weave(nc.scalar, zword[last][:, 0 : PACK * half], wide_plane[:], 2)
 
         def pick_piece(b, j0):
             narrow = zplane[b][:].bitcast(F32)[:, :, 0:PIECE]
@@ -322,19 +342,20 @@ def tile_list_clamped_landmark_differences_kernel(
         clamp(nc.gpsimd, narrow, narrow)
         for t in range(PACK):
             weigh(last, t, narrow_plane[:, t, :], narrow[:, t, :])
-        weave(nc.scalar, zword[last][:, PACK * half : PACK * (half + PIECE)], narrow_plane[:])
+        weave(nc.scalar, zword[last][:, PACK * half : PACK * (half + PIECE)], narrow_plane[:], 2)
 
         narrow = pick_piece(1, half + PIECE)
         woven = wide_plane[:].rearrange("p t j -> p (t j)").bitcast(F32).rearrange("p (j t) -> p j t", t=PACK)
         quant_z(last, 0, half, zword[last][:, 0 : PACK * half])
         clamp(nc.vector, woven, narrow.rearrange("p t j -> p j t"))
+        quant_z(last, half, PIECE, zword[last][:, PACK * half : PACK * (half + PIECE)])
         nc.vector.tensor_tensor(
             out=zword[last][:, PACK * (half + PIECE) :].rearrange("p (j t) -> p j t", t=PACK),
             in0=woven,
             in1=gain_sb[:, last, :].unsqueeze(1).to_broadcast([P, PIECE, PACK]),
             op=ALU.mult,
         )
-        quant_z(last, half, half, zword[last][:, PACK * half :])
+        quant_z(last, half + PIECE, PIECE, zword[last][:, PACK * (half + PIECE) :])
         mul_z(last)
 
         y = [keep.tile([P, PACK, PAIRS], F32, name="y%d" % g) for g in range(GROUPS)]
@@ -350,11 +371,12 @@ def tile_list_clamped_landmark_differences_kernel(
                 nc.scalar.activation(
                     out=y[g][:, t, :], in_=yacc[g, t][:], func=ACT.Identity, bias=bias_sb[:, g, t : t + 1]
                 )
-            if t % 2:
-                nc.sync.dma_start(
-                    out=out_0[KP * g : KP * (g + 1), :].rearrange("(p t) j -> p t j", t=PACK)[:, t - 1 : t + 1, :],
-                    in_=y[g][:, t - 1 : t + 1, :],
-                )
+
+        def store_y(g, t0, t1):
+            nc.sync.dma_start(
+                out=out_0[KP * g : KP * (g + 1), :].rearrange("(p t) j -> p t j", t=PACK)[:, t0:t1, :],
+                in_=y[g][:, t0:t1, :],
+            )
 
         def quant_y(g):
             nc.vector.quantize_mx(
@@ -364,16 +386,20 @@ def tile_list_clamped_landmark_differences_kernel(
 
         for t in range(PACK):
             add_bias(0, t, nc.scalar if t % 2 else nc.vector)
-        weave(nc.vector, yword[0][:], y[0][:])
-        for t in range(PACK):
+            if t != 2:
+                store_y(0, t if t < 2 else 2, t + 1)
+        add_bias(1, 0, nc.vector)
+        weave(nc.vector, yword[0][:], y[0][:], 4)
+        for t in range(1, PACK):
             add_bias(1, t, nc.scalar)
+            if t % 2:
+                store_y(1, t - 1, t + 1)
         quant_y(0)
-        weave(nc.vector, yword[1][:, 0 : PACK * VECTOR_SHARE], y[1][:, :, 0:VECTOR_SHARE])
-        weave(nc.scalar, yword[1][:, PACK * VECTOR_SHARE :], y[1][:, :, VECTOR_SHARE:])
+        weave(nc.vector, yword[1][:, 0 : PACK * VECTOR_SHARE], y[1][:, :, 0:VECTOR_SHARE], 4)
+        weave(nc.scalar, yword[1][:, PACK * VECTOR_SHARE :], y[1][:, :, VECTOR_SHARE:], 4)
         quant_y(1)
         for quad in range(4):
-            eng = nc.scalar if quad % 2 else nc.sync
-            eng.dma_start(
+            nc.scalar.dma_start(
                 out=out_2[:, 4 * quad : 4 * quad + 4, :].bitcast(I32).rearrange("g r m -> r g m"),
                 in_=ys[32 * quad : 32 * quad + 4, :].bitcast(I32).rearrange("p (g m) -> p g m", g=GROUPS),
             )

@@ -23,14 +23,17 @@ A_PASSES = K // KP
 B_PASSES = H // KP
 GROUPS = N // KP
 BANK = 512
+HALF = PAIRS // 2
 PIECE = 128
-PIECES = PAIRS // PIECE
-SCALAR_SHARE = 52
-VECTOR_SHARE = 256
-LATER_SHARE = 104
-AT_SCALES = 4 * PACK * KP - 64
-AT_TABLE = AT_SCALES + T - 64
-AT_FIRST = AT_TABLE + 4 * T
+RAW_PITCH = KP + 9
+LONG = 384
+PIECE_PITCH = PIECE + 1
+HEAD_SHARE = 48
+Y_SHARE = 256
+RAW_BYTES = 8384
+AT_SCALES = RAW_BYTES - 128
+AT_TABLE1 = AT_SCALES + T - 64
+AT_TABLE0 = AT_TABLE1 + 4 * T
 
 
 def tile_list_clamped_landmark_differences_kernel(
@@ -46,77 +49,87 @@ def tile_list_clamped_landmark_differences_kernel(
         pos1_sb = keep.tile([P, PAIRS // 16], U16, name="pos1_sb")
         pos2_sb = keep.tile([P, PAIRS // 16], U16, name="pos2_sb")
         tabs = shared.tile([P, T], U8, name="tabs", offset=AT_SCALES, align_bytes=64)
-        w2w_raw = [keep.tile([P, 2 * N], U8, name="w2w_raw", tag=tag, align_bytes=64) for tag in ("slot_g", "slot_c", "slot_e")]
+        w2w_raw = keep.tile([P, B_PASSES * 2 * N], U8, name="w2w_raw", align_bytes=64)
         w2s_raw = keep.tile([P, N], U8, name="w2s_raw")
         planes = keep.tile([P, B_PASSES * N], U8, name="planes", align_bytes=64)
         w2s = planes[:].rearrange("p (u b c) -> p u b c", b=B_PASSES, c=2 * P)
+        first_plane = keep.tile([P, S], U8, name="first_plane", align_bytes=64)
+        vs = [first_plane[:], planes[:, 0:S]]
         ys = keep.tile([P, GROUPS * PAIRS], U8, name="ys", align_bytes=64)
         gain_sb = keep.tile([P, B_PASSES, PACK], F32, name="gain_sb")
         bias_sb = keep.tile([P, GROUPS, PACK], F32, name="bias_sb")
 
-        for tile in (tabs, w2s_raw, planes):
-            nc.vector.memset(tile[:].bitcast(I32), 0)
+        nc.vector.memset(w2s_raw[:].bitcast(I32), 0)
+        nc.vector.memset(tabs[32:64, :].bitcast(I32), 0)
+        nc.vector.memset(tabs[64:P, :].bitcast(I32), 0)
+        nc.vector.memset(first_plane[:].bitcast(I32), 0)
+        nc.vector.memset(planes[:].bitcast(I32), 0)
 
         w1_raw = {}
         tabw = {}
 
-        def load_w1(b, a, tag=None, offset=None):
-            if tag:
-                raw = keep.tile([P, PACK, KP], F32, name="w1_raw", tag=tag, align_bytes=64)
+        def load_w1(b, a, offset=None):
+            if offset is None:
+                raw = keep.tile([P, PACK, RAW_PITCH], F32, name="w1_raw", tag="first_raw", align_bytes=64)
             else:
-                raw = shared.tile([P, PACK, KP], F32, name="w1_raw%d%d" % (b, a), offset=offset, align_bytes=64)
+                raw = shared.tile([P, PACK, RAW_PITCH], F32, name="w1_raw%d%d" % (b, a), offset=offset, align_bytes=64)
             nc.sync.dma_start(
-                out=raw[:],
+                out=raw[:, :, 0:KP],
                 in_=w1[KP * a : KP * (a + 1), KP * b : KP * (b + 1)].rearrange("(p j) c -> p j c", j=PACK),
             )
             w1_raw[b, a] = raw
 
-        def load_table(a, tile):
-            tabw[a] = tile
+        def load_table(a, offset):
+            tabw[a] = shared.tile([P, T], I32, name="tabw%d" % a, offset=offset, align_bytes=64)
             nc.sync.dma_start(out=tabw[a][:], in_=tab_words[a].rearrange("p t i -> p (t i)").bitcast(I32))
 
         nc.sync.dma_start(offs_sb[:], offs)
+        nc.sync.dma_start(out=tabs[0:32, :].bitcast(I32), in_=tab_scales.rearrange("a q t -> (a q) t").bitcast(I32))
         nc.sync.dma_start(pos2_sb[:], pos2)
         nc.sync.dma_start(pos1_sb[:], pos1)
-        for b in range(B_PASSES):
-            nc.sync.dma_start(out=w2w_raw[b][:].bitcast(I32), in_=w2_words[b].bitcast(I32))
-        nc.sync.dma_start(out=gain_sb[:], in_=gain.rearrange("(b p t) -> p b t", b=B_PASSES, t=PACK))
-        nc.sync.dma_start(out=bias_sb[:], in_=bias.rearrange("(g p t) -> p g t", g=GROUPS, t=PACK))
-        nc.sync.dma_start(out=tabs[0:P:4, :].bitcast(I32), in_=tab_scales.rearrange("a q t -> (a q) t").bitcast(I32))
-        nc.sync.dma_start(out=w2s_raw[0:96:2, :].bitcast(I32), in_=w2_scales.rearrange("b q c -> (b q) c").bitcast(I32))
-        load_table(0, shared.tile([P, T], I32, name="tabw0", offset=AT_FIRST, align_bytes=64))
-        load_w1(0, 0, "slot_d")
+        nc.sync.dma_start(
+            out=w2w_raw[:].bitcast(I32).rearrange("p (b c) -> p b c", b=B_PASSES),
+            in_=w2_words.bitcast(I32).rearrange("b p c -> p b c"),
+        )
+        load_table(0, AT_TABLE0)
+        load_w1(0, 0)
+        nc.scalar.dma_start(out=gain_sb[:], in_=gain.rearrange("(b p t) -> p b t", b=B_PASSES, t=PACK))
+        nc.scalar.dma_start(out=bias_sb[:], in_=bias.rearrange("(g p t) -> p g t", g=GROUPS, t=PACK))
+        nc.scalar.dma_start(out=w2s_raw[0:96:2, :].bitcast(I32), in_=w2_scales.rearrange("b q c -> (b q) c").bitcast(I32))
 
-        w2w = {}
-
-        def deal_w2_words(b, tile):
-            w2w[b] = tile
-            nc.vector.tensor_copy(
-                out=tile[:].bitcast(U16).rearrange("p (r t c i) -> p r c t i", t=PACK, c=16, i=8),
-                in_=w2w_raw[b][:].bitcast(U16).rearrange("p (r c i t) -> p r c t i", t=PACK, c=16, i=8),
-            )
-        deal_w2_words(0, keep.tile([P, 2 * N], U8, name="w2w0", align_bytes=64))
         vs_picked = keep.tile([P, S], U8, name="vs_picked")
         nc.vector.tensor_copy(out=vs_picked[:], in_=tabs[:].indirect(offs_sb[:]))
 
         def move_table_scales(a):
             for r in range(4):
                 nc.sync.dma_start(
-                    out=planes[r:P:32, S * a : S * (a + 1)].bitcast(I32),
-                    in_=vs_picked[64 * a + 4 * r : 64 * (a + 1) : 16, :].bitcast(I32),
+                    out=vs[a][r:P:32, :].bitcast(I32),
+                    in_=vs_picked[16 * a + r : 16 * (a + 1) : 4, :].bitcast(I32),
                 )
 
         move_table_scales(0)
-        load_table(1, shared.tile([P, T], I32, name="tabw1", offset=AT_TABLE, align_bytes=64))
+        load_table(1, AT_TABLE1)
         move_table_scales(1)
         load_w1(0, 1, offset=0)
-        deal_w2_words(1, shared.tile([P, 2 * N], U8, name="w2w1", offset=AT_SCALES + 64, align_bytes=64))
-        w2s_dealt = shared.tile([P, N], U8, name="w2s_dealt", offset=AT_SCALES + 64 + 2 * N, align_bytes=64)
+
+        w2w = {}
+
+        def deal_w2_words(b, dealt):
+            w2w[b] = dealt
+            nc.vector.tensor_copy(
+                out=dealt.bitcast(U16).rearrange("p (r t c i) -> p r c t i", t=PACK, c=16, i=8),
+                in_=w2w_raw[:, 2 * N * b : 2 * N * (b + 1)].bitcast(U16).rearrange("p (r c i t) -> p r c t i", t=PACK, c=16, i=8),
+            )
+
+        w2w_first = shared.tile([P, 2 * N], U8, name="w2w_first", offset=RAW_BYTES, align_bytes=64)
+        deal_w2_words(0, w2w_first[:])
+        w2s_dealt = shared.tile([P, N], U8, name="w2s_dealt", offset=RAW_BYTES + 2 * N, align_bytes=64)
         nc.vector.tensor_copy(
             out=w2s_dealt[:].rearrange("p (r t c i) -> p r c t i", t=PACK, c=8, i=16),
             in_=w2s_raw[:].rearrange("p (r c i t) -> p r c t i", t=PACK, c=8, i=16),
         )
-        deal_w2_words(2, keep.tile([P, 2 * N], U8, name="w2w2", tag="slot_c", align_bytes=64))
+        for b in range(1, B_PASSES):
+            deal_w2_words(b, w2w_raw[:, 2 * N * (b - 1) : 2 * N * b])
         vw = [keep.tile([P, S], U32, name="vw0", align_bytes=64)]
         nc.vector.tensor_copy(out=vw[0][:], in_=tabw[0][:].bitcast(U32).indirect(offs_sb[:]))
 
@@ -130,21 +143,17 @@ def tile_list_clamped_landmark_differences_kernel(
             else:
                 engine.tensor_copy(out=dst, in_=src)
 
-        def take_bf(b, a, tag):
-            w1_bf[b, a] = keep.tile([P, PACK * KP], BF16, name="w1_bf", tag=tag, align_bytes=64)
-
         def cast_w1(b, a, engine, m0=0, m1=P):
+            if (b, a) not in w1_bf:
+                w1_bf[b, a] = keep.tile([P, PACK * KP], BF16, name="w1_bf", tag="bf%d%d" % (b, a), align_bytes=64)
             dst = w1_bf[b, a][:].rearrange("p (t m j) -> p m t j", t=PACK, j=PACK)[:, m0:m1]
-            src = w1_raw[b, a][:].rearrange("p j (m t) -> p m t j", t=PACK)[:, m0:m1]
+            src = w1_raw[b, a][:, :, 0:KP].rearrange("p j (m t) -> p m t j", t=PACK)[:, m0:m1]
             copy_on(engine, dst, src)
 
-        def quant_w1(b, a, t0=0, t1=PACK, at=None):
+        def quant_w1(b, a, t0=0, t1=PACK):
             if (b, a) not in w1s:
                 w1s[b, a] = keep.tile([P, KP], U8, name="w1s%d%d" % (b, a), align_bytes=64)
-            if at is None:
-                codes = keep.tile([P, P * (t1 - t0)], U32, name="w1c", tag="codes%d%d%d" % (b, a, t0), align_bytes=64)
-            else:
-                codes = shared.tile([P, P * (t1 - t0)], U32, name="w1c%d%d" % (b, a), offset=at, align_bytes=64)
+            codes = keep.tile([P, P * (t1 - t0)], U32, name="w1c%d%d%d" % (b, a, t0), align_bytes=64)
             for t in range(t0, t1):
                 w1c[b, a, t] = codes[:, P * (t - t0) : P * (t - t0 + 1)]
             nc.vector.quantize_mx(
@@ -154,25 +163,32 @@ def tile_list_clamped_landmark_differences_kernel(
             )
 
         h = {}
+        hacc = {}
 
-        def make_h(s, second_engine=nc.scalar):
+        def mul_h(s, a):
             b, t = divmod(s, PACK)
-            h[s] = keep.tile([P, S], F32, name="h%d" % s)
-            cols = slice(P * t, P * (t + 1))
             for half in range(2):
-                acc = psum.tile([P, BANK], F32, name="acc", tag="bank%d" % (2 * t + half))
-                ent = slice(BANK * half, BANK * (half + 1))
-                for a in range(A_PASSES):
-                    nc.tensor.matmul_mx(
-                        out=acc[:],
-                        lhsT=w1c[b, a, t].bitcast(FP8X4),
-                        lhsT_scale=w1s[b, a][:, cols],
-                        rhs=vw[a][:, ent].bitcast(FP8X4),
-                        rhs_scale=planes[:, S * a + BANK * half : S * a + BANK * (half + 1)],
-                        start=(a == 0),
-                        stop=(a == A_PASSES - 1),
-                    )
-                copy_on(second_engine if half else nc.scalar, h[s][:, ent], acc[:])
+                if a == 0:
+                    hacc[s, half] = psum.tile([P, BANK], F32, name="hacc", tag="bank%d" % (2 * t + half))
+                nc.tensor.matmul_mx(
+                    out=hacc[s, half][:],
+                    lhsT=w1c[b, a, t].bitcast(FP8X4),
+                    lhsT_scale=w1s[b, a][:, P * t : P * (t + 1)],
+                    rhs=vw[a][:, BANK * half : BANK * (half + 1)].bitcast(FP8X4),
+                    rhs_scale=vs[a][:, BANK * half : BANK * (half + 1)],
+                    start=(a == 0),
+                    stop=(a == A_PASSES - 1),
+                )
+
+        def empty_h(s, second_engine=nc.scalar):
+            h[s] = keep.tile([P, S], F32, name="h%d" % s)
+            for half in range(2):
+                copy_on(second_engine if half else nc.scalar, h[s][:, BANK * half : BANK * (half + 1)], hacc[s, half][:])
+
+        def make_h(s):
+            for a in range(A_PASSES):
+                mul_h(s, a)
+            empty_h(s)
 
         def pick_second(s, dst, j0, n):
             nc.vector.tensor_copy(out=dst, in_=h[s][:].indirect(pos2_sb[:, j0 // 16 : (j0 + n) // 16]))
@@ -191,8 +207,7 @@ def tile_list_clamped_landmark_differences_kernel(
         def weigh(b, t, dst, src):
             nc.scalar.activation(out=dst, in_=src, func=ACT.Copy, scale=gain_sb[:, b, t : t + 1])
 
-        def weave(engine, dst, src, width):
-            run = 8 // width
+        def weave(engine, dst, src, run):
             copy_on(
                 engine,
                 dst.rearrange("p (c i t) -> p c t i", i=run, t=PACK),
@@ -201,9 +216,14 @@ def tile_list_clamped_landmark_differences_kernel(
 
         zc = [keep.tile([P, PAIRS], U32, name="zc%d" % b, align_bytes=64) for b in range(B_PASSES)]
         zs = [keep.tile([P, PAIRS], U8, name="zs%d" % b, align_bytes=64) for b in range(B_PASSES)]
+        zword = [keep.tile([P, PACK * PAIRS], BF16, name="zword%d" % b, align_bytes=64) for b in range(B_PASSES)]
 
-        def quant_z(b, j0, n, words):
-            nc.vector.quantize_mx(out=zc[b][:, j0 : j0 + n].bitcast(FP8X4), scales=zs[b][:, j0 : j0 + n], in_=words)
+        def quant_z(b, j0, n):
+            nc.vector.quantize_mx(
+                out=zc[b][:, j0 : j0 + n].bitcast(FP8X4),
+                scales=zs[b][:, j0 : j0 + n],
+                in_=zword[b][:, PACK * j0 : PACK * (j0 + n)],
+            )
 
         yacc = {}
 
@@ -223,143 +243,152 @@ def tile_list_clamped_landmark_differences_kernel(
                         stop=(b == B_PASSES - 1),
                     )
 
-        take_bf(0, 0, "bf00")
         cast_w1(0, 0, nc.scalar)
-        load_w1(1, 0, offset=AT_FIRST)
-        load_w1(1, 1, "slot_d")
+        load_w1(1, 0, offset=AT_TABLE0 + 512)
+        load_w1(1, 1)
         quant_w1(0, 0)
         vw.append(keep.tile([P, S], U32, name="vw1", tag="bf00", align_bytes=64))
         nc.vector.tensor_copy(out=vw[1][:], in_=tabw[1][:].bitcast(U32).indirect(offs_sb[:]))
-        load_w1(2, 0, offset=AT_TABLE + 2 * T)
-        w1_bf[0, 1] = shared.tile([P, PACK * KP], BF16, name="w1_bf01", offset=AT_TABLE, align_bytes=64)
-        cast_w1(0, 1, nc.scalar, 0, SCALAR_SHARE)
-        cast_w1(0, 1, nc.vector, SCALAR_SHARE, P)
+        load_w1(2, 0, offset=AT_TABLE1)
+        load_w1(2, 1, offset=AT_TABLE1 + RAW_BYTES)
+        cast_w1(0, 1, nc.scalar, 0, HEAD_SHARE)
+        cast_w1(0, 1, nc.vector, HEAD_SHARE, P)
         quant_w1(0, 1, 0, 1)
         quant_w1(0, 1, 1, 2)
         quant_w1(0, 1, 2, 4)
-        load_w1(2, 1, offset=AT_TABLE)
-        make_h(0, nc.vector)
-        make_h(1)
-        take_bf(1, 0, "codes011")
-        cast_w1(1, 0, nc.scalar)
-        make_h(2)
-        take_bf(1, 1, "bf11")
+        for s in range(PACK):
+            for a in range(A_PASSES):
+                mul_h(s, a)
 
-        half = PAIRS // 2
-        diff = [
-            shared.tile([P, PACK, PAIRS], F32, name="diff0", offset=0, align_bytes=64),
-            keep.tile([P, PACK, PAIRS], F32, name="diff1"),
-        ]
+        diff = [keep.tile([P, PACK, PAIRS], F32, name="diff%d" % b) for b in range(2)]
+        second = [keep.tile([P, PAIRS], F32, name="second%d" % u) for u in range(2)]
         zplane = [keep.tile([P, PACK, PAIRS], BF16, name="zplane%d" % b) for b in range(2)]
-        zword = [keep.tile([P, PACK * PAIRS], BF16, name="zword%d" % b, align_bytes=64) for b in range(B_PASSES)]
+        long_run, short_run = slice(0, LONG), slice(LONG, PAIRS)
 
-        def pick_slice(s, second, between=None):
+        def words_of(tile, n):
+            return tile.bitcast(F32)[:, 0:n]
+
+        def pick_slice(s, long_last):
             b, t = divmod(s, PACK)
-            for u in range(2):
-                pick_second(s, second[u], half * u, half)
-            if between:
-                between()
-            for u in range(2):
-                pick_diff(s, diff[b][:, t, half * u : half * (u + 1)], second[u], half * u, half)
-            clamp(nc.gpsimd, diff[b][:, t, :], diff[b][:, t, :])
+            runs = (short_run, long_run) if long_last else (long_run, short_run)
+            for run in runs:
+                pick_second(s, second[s % 2][:, run], run.start, run.stop - run.start)
+            for run in runs:
+                pick_diff(s, diff[b][:, t, run], second[s % 2][:, run], run.start, run.stop - run.start)
+            clamp(nc.gpsimd, diff[b][:, t, long_run], diff[b][:, t, long_run])
 
-        def halves(words):
-            return words[:, 0:half], words[:, half:PAIRS]
+        def clamp_short_runs(b):
+            clamp(nc.vector, diff[b][:, :, short_run], diff[b][:, :, short_run])
 
         def weigh_slice(b, t):
             weigh(b, t, zplane[b][:, t, :], diff[b][:, t, :])
 
-        def finish_pass(b, t0):
-            for t in range(t0, PACK):
-                weigh_slice(b, t)
-            weave(nc.scalar, zword[b][:], zplane[b][:], 2)
-
-        spare = keep.tile([P, PAIRS], F32, name="spare")
-        pick_slice(0, (w1_bf[1, 1][:].bitcast(F32)[:, 0:half], spare[:, half:PAIRS]))
-        cast_w1(1, 1, nc.vector, LATER_SHARE, P)
-        cast_w1(1, 1, nc.scalar, 0, LATER_SHARE)
-        make_h(3)
-        take_bf(2, 0, "codes000")
-        cast_w1(2, 0, nc.scalar)
-        pick_slice(1, halves(spare[:]))
-        pick_slice(2, halves(w1_raw[1, 0][:, 0, :]), lambda: quant_w1(1, 0))
+        empty_h(0, nc.vector)
+        pick_slice(0, False)
+        empty_h(1)
+        pick_slice(1, True)
+        cast_w1(1, 0, nc.scalar)
+        quant_w1(1, 0)
+        empty_h(2)
+        pick_slice(2, True)
+        cast_w1(1, 1, nc.scalar)
         quant_w1(1, 1)
-        pick_slice(3, halves(spare[:]))
-        quant_w1(2, 0)
+        empty_h(3)
+        pick_slice(3, True)
+        clamp_short_runs(0)
+        cast_w1(2, 0, nc.scalar, 0, P // 2)
         make_h(4)
+        pick_slice(4, True)
+        cast_w1(2, 0, nc.scalar, P // 2, P)
+        quant_w1(2, 0)
         make_h(5)
-        take_bf(2, 1, "codes011")
+        pick_slice(5, True)
         cast_w1(2, 1, nc.scalar)
+        quant_w1(2, 1)
         make_h(6)
+        pick_slice(6, False)
         make_h(7)
-        pick_slice(4, halves(spare[:]))
-        pick_slice(5, halves(spare[:]))
-        pick_slice(6, halves(w1_raw[2, 1][:, 0, :]), lambda: quant_w1(2, 1))
-        pick_slice(7, halves(spare[:]))
-        for t in range(1, PACK):
+        pick_slice(7, True)
+        clamp_short_runs(1)
+
+        last = B_PASSES - 1
+        wide = keep.tile([P, PACK, HALF], F32, name="wide")
+        wide_plane = keep.tile([P, PACK, HALF], BF16, name="wide_plane")
+        late_second = keep.tile([P, PACK, HALF], F32, name="late_second")
+        third = keep.tile([P, PACK, PIECE_PITCH], F32, name="third")
+
+        def pick_last(t, wide_last):
+            s = PACK * last + t
+            spare = second[t % 2][:, 0:HALF]
+            picks = [
+                lambda: pick_second(s, spare, 0, HALF),
+                lambda: pick_second(s, late_second[:, t, :], HALF, HALF),
+                lambda: pick_diff(s, wide[:, t, :], spare, 0, HALF),
+                lambda: pick_diff(s, third[:, t, 0:PIECE], late_second[:, t, 0:PIECE], HALF, PIECE),
+            ]
+            for step in (1, 0, 3, 2) if wide_last else (0, 1, 2, 3):
+                picks[step]()
+            clamp(nc.gpsimd if t < PACK - 1 else nc.vector, wide[:, t, :], wide[:, t, :])
+
+        def weigh_woven(j0, src):
+            nc.vector.tensor_tensor(
+                out=zword[last][:, PACK * j0 : PACK * (j0 + PIECE)].rearrange("p (j t) -> p j t", t=PACK),
+                in0=src,
+                in1=gain_sb[:, last, :].unsqueeze(1).to_broadcast([P, PIECE, PACK]),
+                op=ALU.mult,
+            )
+
+        for t in range(PACK):
             weigh_slice(0, t)
         make_h(8)
-        make_h(9)
-        weigh_slice(0, 0)
-        make_h(10)
-        make_h(11)
+        pick_last(0, False)
         weigh_slice(1, 0)
+        make_h(9)
+        pick_last(1, False)
+        weigh_slice(1, 1)
+        make_h(10)
+        pick_last(2, True)
+        weave(nc.scalar, zword[0][:], zplane[0][:], 4)
+        quant_z(0, 0, PAIRS)
+        make_h(11)
         for b in range(B_PASSES):
             for r in range(4):
                 nc.sync.dma_start(
                     out=w2s[r:P:32, :, b, :].bitcast(I32),
                     in_=w2s_dealt[32 * b + 2 * r : 32 * (b + 1) : 8, :].rearrange("p (u c) -> p u c", c=2 * P).bitcast(I32),
                 )
-        finish_pass(0, PACK)
-        finish_pass(1, 1)
-
-        last = B_PASSES - 1
-        wide = keep.tile([P, PACK, half], F32, name="wide")
-        wide_plane = keep.tile([P, PACK, half], BF16, name="wide_plane")
-        for t0 in (0, 2):
-            second = diff[t0 // 2][:, 0, :]
-            for u in range(2):
-                pick_second(PACK * last + t0 + u, second[:, half * u : half * (u + 1)], 0, half)
-            for u in range(2):
-                pick_diff(PACK * last + t0 + u, wide[:, t0 + u, :], second[:, half * u : half * (u + 1)], 0, half)
-            clamp(nc.gpsimd, wide[:, t0 : t0 + 2, :], wide[:, t0 : t0 + 2, :])
+        mul_z(0)
+        pick_last(3, False)
+        weigh_slice(1, 2)
+        weigh_slice(1, 3)
+        weave(nc.scalar, zword[1][:], zplane[1][:], 4)
         for t in range(PACK):
             weigh(last, t, wide_plane[:, t, :], wide[:, t, :])
-        weave(nc.scalar, zword[last][:, 0 : PACK * half], wide_plane[:], 2)
+        weave(nc.scalar, zword[last][:, 0 : PACK * HALF], wide_plane[:], 4)
 
-        def pick_piece(b, j0):
-            narrow = zplane[b][:].bitcast(F32)[:, :, 0:PIECE]
-            for t in range(PACK):
-                pick_second(PACK * last + t, second[:, PIECE * t : PIECE * (t + 1)], j0, PIECE)
-            quant_z(b, 0, PAIRS, zword[b][:])
-            mul_z(b)
-            for t in range(PACK):
-                pick_diff(PACK * last + t, narrow[:, t, :], second[:, PIECE * t : PIECE * (t + 1)], j0, PIECE)
-            return narrow
-
-        narrow = pick_piece(0, half)
-        narrow_plane = keep.tile([P, PACK, PIECE], BF16, name="narrow_plane")
-        clamp(nc.gpsimd, narrow, narrow)
+        woven_third = second[0][:].rearrange("p (j t) -> p j t", t=PACK)
+        clamp(nc.vector, woven_third, third[:, :, 0:PIECE].rearrange("p t j -> p j t"))
+        weigh_woven(HALF, woven_third)
+        quant_z(1, 0, PAIRS)
+        mul_z(1)
+        fourth = words_of(zplane[1][:].rearrange("p t j -> p (t j)"), PACK * PIECE_PITCH).rearrange("p (t j) -> p t j", t=PACK)
         for t in range(PACK):
-            weigh(last, t, narrow_plane[:, t, :], narrow[:, t, :])
-        weave(nc.scalar, zword[last][:, PACK * half : PACK * (half + PIECE)], narrow_plane[:], 2)
-
-        narrow = pick_piece(1, half + PIECE)
-        woven = wide_plane[:].rearrange("p t j -> p (t j)").bitcast(F32).rearrange("p (j t) -> p j t", t=PACK)
-        quant_z(last, 0, half, zword[last][:, 0 : PACK * half])
-        clamp(nc.vector, woven, narrow.rearrange("p t j -> p j t"))
-        quant_z(last, half, PIECE, zword[last][:, PACK * half : PACK * (half + PIECE)])
-        nc.vector.tensor_tensor(
-            out=zword[last][:, PACK * (half + PIECE) :].rearrange("p (j t) -> p j t", t=PACK),
-            in0=woven,
-            in1=gain_sb[:, last, :].unsqueeze(1).to_broadcast([P, PIECE, PACK]),
-            op=ALU.mult,
-        )
-        quant_z(last, half + PIECE, PIECE, zword[last][:, PACK * (half + PIECE) :])
+            pick_diff(PACK * last + t, fourth[:, t, 0:PIECE], late_second[:, t, PIECE:HALF], HALF + PIECE, PIECE)
+        quant_z(last, 0, HALF)
+        woven = words_of(wide_plane[:].rearrange("p t j -> p (t j)"), PACK * PIECE).rearrange("p (j t) -> p j t", t=PACK)
+        clamp(nc.vector, woven, fourth[:, :, 0:PIECE].rearrange("p t j -> p j t"))
+        weigh_woven(HALF + PIECE, woven)
+        quant_z(last, HALF, HALF)
         mul_z(last)
 
-        y = [keep.tile([P, PACK, PAIRS], F32, name="y%d" % g) for g in range(GROUPS)]
-        yword = [keep.tile([P, PACK * PAIRS], BF16, name="yword%d" % g, align_bytes=64) for g in range(GROUPS)]
+        y = [
+            shared.tile([P, PACK, PAIRS], F32, name="y%d" % g, offset=AT_TABLE1 + RAW_BYTES * g, align_bytes=64)
+            for g in range(GROUPS)
+        ]
+        yword = [
+            shared.tile([P, PACK * PAIRS], BF16, name="yword%d" % g, offset=AT_TABLE0 + 512 + 2 * PACK * PAIRS * g, align_bytes=64)
+            for g in range(GROUPS)
+        ]
         yc = [keep.tile([P, PAIRS], U32, name="yc%d" % g, align_bytes=64) for g in range(GROUPS)]
 
         def add_bias(g, t, engine):
@@ -389,14 +418,14 @@ def tile_list_clamped_landmark_differences_kernel(
             if t != 2:
                 store_y(0, t if t < 2 else 2, t + 1)
         add_bias(1, 0, nc.vector)
-        weave(nc.vector, yword[0][:], y[0][:], 4)
+        weave(nc.vector, yword[0][:], y[0][:], 2)
         for t in range(1, PACK):
             add_bias(1, t, nc.scalar)
             if t % 2:
                 store_y(1, t - 1, t + 1)
         quant_y(0)
-        weave(nc.vector, yword[1][:, 0 : PACK * VECTOR_SHARE], y[1][:, :, 0:VECTOR_SHARE], 4)
-        weave(nc.scalar, yword[1][:, PACK * VECTOR_SHARE :], y[1][:, :, VECTOR_SHARE:], 4)
+        weave(nc.vector, yword[1][:, 0 : PACK * Y_SHARE], y[1][:, :, 0:Y_SHARE], 2)
+        weave(nc.scalar, yword[1][:, PACK * Y_SHARE :], y[1][:, :, Y_SHARE:], 2)
         quant_y(1)
         for quad in range(4):
             nc.scalar.dma_start(

@@ -25,13 +25,13 @@ GROUPS = N // KP
 BANK = 512
 HALF = PAIRS // 2
 PIECE = 128
-RAW_PITCH = KP + 9
+RAW_PITCH = KP
 LONG = 384
 PIECE_PITCH = PIECE + 1
 HEAD_SHARE = 48
 Y_SHARE = 256
-RAW_BYTES = 8384
-AT_SCALES = RAW_BYTES - 128
+RAW_BYTES = 4 * PACK * KP
+AT_SCALES = RAW_BYTES - 64
 AT_TABLE1 = AT_SCALES + T - 64
 AT_TABLE0 = AT_TABLE1 + 4 * T
 

@@ -275,10 +275,7 @@ def tile_list_clamped_landmark_differences_kernel(
                 pick_second(s, second[s % 2][:, run], run.start, run.stop - run.start)
             for run in runs:
                 pick_diff(s, diff[b][:, t, run], second[s % 2][:, run], run.start, run.stop - run.start)
-            clamp(nc.gpsimd, diff[b][:, t, long_run], diff[b][:, t, long_run])
-
-        def clamp_short_runs(b):
-            clamp(nc.vector, diff[b][:, :, short_run], diff[b][:, :, short_run])
+            clamp(nc.gpsimd, diff[b][:, t, :], diff[b][:, t, :])
 
         def weigh_slice(b, t):
             weigh(b, t, zplane[b][:, t, :], diff[b][:, t, :])
@@ -295,7 +292,6 @@ def tile_list_clamped_landmark_differences_kernel(
         quant_w1(1, 1)
         empty_h(3)
         pick_slice(3, True)
-        clamp_short_runs(0)
         cast_w1(2, 0, nc.scalar, 0, P // 2)
         make_h(4)
         pick_slice(4, True)
@@ -309,7 +305,6 @@ def tile_list_clamped_landmark_differences_kernel(
         pick_slice(6, False)
         make_h(7)
         pick_slice(7, True)
-        clamp_short_runs(1)
 
         last = B_PASSES - 1
         wide = keep.tile([P, PACK, HALF], F32, name="wide")

@@ -146,9 +146,15 @@ def tile_list_clamped_landmark_differences_kernel(
         def cast_w1(b, a, engine, m0=0, m1=P):
             if (b, a) not in w1_bf:
                 w1_bf[b, a] = keep.tile([P, PACK * KP], BF16, name="w1_bf", tag="bf%d%d" % (b, a), align_bytes=64)
-            dst = w1_bf[b, a][:].rearrange("p (t m j) -> p m t j", t=PACK, j=PACK)[:, m0:m1]
-            src = w1_raw[b, a][:, :, 0:KP].rearrange("p j (m t) -> p m t j", t=PACK)[:, m0:m1]
-            copy_on(engine, dst, src)
+            if engine is nc.vector:
+                dst = w1_bf[b, a][:].rearrange("p (t m j) -> p m t j", t=PACK, j=PACK)[:, m0:m1]
+                src = w1_raw[b, a][:, :, 0:KP].rearrange("p j (m t) -> p m t j", t=PACK)[:, m0:m1]
+                copy_on(engine, dst, src)
+                return
+            dst = w1_bf[b, a][:].rearrange("p (t m j) -> p m j t", t=PACK, j=PACK)[:, m0:m1]
+            src = w1_raw[b, a][:, :, 0:KP].rearrange("p j (m t) -> p m j t", t=PACK)[:, m0:m1]
+            for t0 in (0, 2):
+                copy_on(engine, dst[:, :, :, t0 : t0 + 2], src[:, :, :, t0 : t0 + 2])
 
         def quant_w1(b, a, t0=0, t1=PACK):
             if (b, a) not in w1s:

@@ -26,8 +26,7 @@ BANK = 512
 HALF = PAIRS // 2
 PIECE = 128
 RAW_PITCH = KP
-LONG = 384
-PIECE_PITCH = PIECE + 1
+PIECE_PITCH = PIECE
 HEAD_SHARE = 48
 Y_SHARE = 256
 RAW_BYTES = 4 * PACK * KP
@@ -143,7 +142,7 @@ def tile_list_clamped_landmark_differences_kernel(
             else:
                 engine.tensor_copy(out=dst, in_=src)
 
-        def cast_w1(b, a, engine, m0=0, m1=P):
+        def cast_w1(b, a, engine, m0=0, m1=P, pairs=(0, 2)):
             if (b, a) not in w1_bf:
                 w1_bf[b, a] = keep.tile([P, PACK * KP], BF16, name="w1_bf", tag="bf%d%d" % (b, a), align_bytes=64)
             if engine is nc.vector:
@@ -153,7 +152,7 @@ def tile_list_clamped_landmark_differences_kernel(
                 return
             dst = w1_bf[b, a][:].rearrange("p (t m j) -> p m j t", t=PACK, j=PACK)[:, m0:m1]
             src = w1_raw[b, a][:, :, 0:KP].rearrange("p j (m t) -> p m j t", t=PACK)[:, m0:m1]
-            for t0 in (0, 2):
+            for t0 in pairs:
                 copy_on(engine, dst[:, :, :, t0 : t0 + 2], src[:, :, :, t0 : t0 + 2])
 
         def quant_w1(b, a, t0=0, t1=PACK):
@@ -220,7 +219,7 @@ def tile_list_clamped_landmark_differences_kernel(
                 src.rearrange("p t (c i) -> p c t i", i=run),
             )
 
-        zc = [keep.tile([P, PAIRS], U32, name="zc%d" % b, align_bytes=64) for b in range(B_PASSES)]
+        zc = [keep.tile([P, PAIRS], U32, name="zc%d" % b, align_bytes=64) for b in range(B_PASSES - 1)]
         zs = [keep.tile([P, PAIRS], U8, name="zs%d" % b, align_bytes=64) for b in range(B_PASSES)]
         zword = [keep.tile([P, PACK * PAIRS], BF16, name="zword%d" % b, align_bytes=64) for b in range(B_PASSES)]
 
@@ -269,14 +268,13 @@ def tile_list_clamped_landmark_differences_kernel(
         diff = [keep.tile([P, PACK, PAIRS], F32, name="diff%d" % b) for b in range(2)]
         second = [keep.tile([P, PAIRS], F32, name="second%d" % u) for u in range(2)]
         zplane = [keep.tile([P, PACK, PAIRS], BF16, name="zplane%d" % b) for b in range(2)]
-        long_run, short_run = slice(0, LONG), slice(LONG, PAIRS)
 
         def words_of(tile, n):
             return tile.bitcast(F32)[:, 0:n]
 
-        def pick_slice(s, long_last):
+        def pick_slice(s):
             b, t = divmod(s, PACK)
-            runs = (short_run, long_run) if long_last else (long_run, short_run)
+            runs = (slice(0, HALF), slice(HALF, PAIRS))
             for run in runs:
                 pick_second(s, second[s % 2][:, run], run.start, run.stop - run.start)
             for run in runs:
@@ -287,40 +285,24 @@ def tile_list_clamped_landmark_differences_kernel(
             weigh(b, t, zplane[b][:, t, :], diff[b][:, t, :])
 
         empty_h(0, nc.vector)
-        pick_slice(0, False)
-        empty_h(1)
-        pick_slice(1, True)
-        cast_w1(1, 0, nc.scalar)
-        quant_w1(1, 0)
-        empty_h(2)
-        pick_slice(2, True)
-        cast_w1(1, 1, nc.scalar)
-        quant_w1(1, 1)
-        empty_h(3)
-        pick_slice(3, True)
-        cast_w1(2, 0, nc.scalar, 0, P // 2)
-        make_h(4)
-        pick_slice(4, True)
-        cast_w1(2, 0, nc.scalar, P // 2, P)
-        quant_w1(2, 0)
-        make_h(5)
-        pick_slice(5, True)
-        cast_w1(2, 1, nc.scalar)
-        quant_w1(2, 1)
-        make_h(6)
-        pick_slice(6, False)
-        make_h(7)
-        pick_slice(7, True)
+        later = [(b, a, t0) for b in range(1, B_PASSES) for t0 in (0, 2) for a in range(A_PASSES)]
+        for s, (b, a, t0) in enumerate(later):
+            pick_slice(s)
+            cast_w1(b, a, nc.scalar, pairs=(t0,))
+            quant_w1(b, a, t0, t0 + 2)
+            if s + 1 < PACK:
+                empty_h(s + 1)
+            else:
+                make_h(s + 1)
 
         last = B_PASSES - 1
         wide = keep.tile([P, PACK, HALF], F32, name="wide")
-        wide_plane = keep.tile([P, PACK, HALF], BF16, name="wide_plane")
+        wide_plane = keep.tile([P, PACK, HALF], BF16, name="wide_plane", tag="wide_plane", align_bytes=64)
         late_second = keep.tile([P, PACK, HALF], F32, name="late_second")
         third = keep.tile([P, PACK, PIECE_PITCH], F32, name="third")
 
-        def pick_last(t, wide_last):
+        def pick_last(t, wide_last, spare):
             s = PACK * last + t
-            spare = second[t % 2][:, 0:HALF]
             picks = [
                 lambda: pick_second(s, spare, 0, HALF),
                 lambda: pick_second(s, late_second[:, t, :], HALF, HALF),
@@ -329,7 +311,12 @@ def tile_list_clamped_landmark_differences_kernel(
             ]
             for step in (1, 0, 3, 2) if wide_last else (0, 1, 2, 3):
                 picks[step]()
-            clamp(nc.gpsimd if t < PACK - 1 else nc.vector, wide[:, t, :], wide[:, t, :])
+
+        def pick_last_and_weigh(t, wide_last, b, tb):
+            pick_last(t, wide_last, zplane[b][:, tb, :].bitcast(F32))
+            nc.gpsimd.tensor_scalar(
+                out=zplane[b][:, tb, :], in0=diff[b][:, tb, :], scalar1=gain_sb[:, b, tb : tb + 1], scalar2=1.0, op0=ALU.mult, op1=ALU.mult
+            )
 
         def weigh_woven(j0, src):
             nc.vector.tensor_tensor(
@@ -339,16 +326,13 @@ def tile_list_clamped_landmark_differences_kernel(
                 op=ALU.mult,
             )
 
-        for t in range(PACK):
-            weigh_slice(0, t)
-        make_h(8)
-        pick_last(0, False)
-        weigh_slice(1, 0)
+        pick_last_and_weigh(0, False, 0, 3)
         make_h(9)
-        pick_last(1, False)
-        weigh_slice(1, 1)
+        pick_last_and_weigh(1, False, 1, 2)
+        for t in range(PACK - 1):
+            weigh_slice(0, t)
         make_h(10)
-        pick_last(2, True)
+        pick_last_and_weigh(2, True, 1, 3)
         weave(nc.scalar, zword[0][:], zplane[0][:], 4)
         quant_z(0, 0, PAIRS)
         make_h(11)
@@ -359,26 +343,28 @@ def tile_list_clamped_landmark_differences_kernel(
                     in_=w2s_dealt[32 * b + 2 * r : 32 * (b + 1) : 8, :].rearrange("p (u c) -> p u c", c=2 * P).bitcast(I32),
                 )
         mul_z(0)
-        pick_last(3, False)
-        weigh_slice(1, 2)
-        weigh_slice(1, 3)
+        pick_last(3, True, second[1][:, 0:HALF])
+        for t in range(2):
+            weigh_slice(1, t)
         weave(nc.scalar, zword[1][:], zplane[1][:], 4)
-        for t in range(PACK):
-            weigh(last, t, wide_plane[:, t, :], wide[:, t, :])
-        weave(nc.scalar, zword[last][:, 0 : PACK * HALF], wide_plane[:], 4)
 
         woven_third = second[0][:].rearrange("p (j t) -> p j t", t=PACK)
         clamp(nc.vector, woven_third, third[:, :, 0:PIECE].rearrange("p t j -> p j t"))
+        clamp(nc.vector, wide[:], wide[:])
+        for t in range(PACK):
+            weigh(last, t, wide_plane[:, t, :], wide[:, t, :])
+        weave(nc.scalar, zword[last][:, 0 : PACK * HALF], wide_plane[:], 4)
         weigh_woven(HALF, woven_third)
         quant_z(1, 0, PAIRS)
         mul_z(1)
         fourth = words_of(zplane[1][:].rearrange("p t j -> p (t j)"), PACK * PIECE_PITCH).rearrange("p (t j) -> p t j", t=PACK)
         for t in range(PACK):
             pick_diff(PACK * last + t, fourth[:, t, 0:PIECE], late_second[:, t, PIECE:HALF], HALF + PIECE, PIECE)
-        quant_z(last, 0, HALF)
-        woven = words_of(wide_plane[:].rearrange("p t j -> p (t j)"), PACK * PIECE).rearrange("p (j t) -> p j t", t=PACK)
+        woven = second[1][:].rearrange("p (j t) -> p j t", t=PACK)
         clamp(nc.vector, woven, fourth[:, :, 0:PIECE].rearrange("p t j -> p j t"))
         weigh_woven(HALF + PIECE, woven)
+        zc.append(keep.tile([P, PAIRS], U32, name="zc_last", tag="wide_plane", align_bytes=64))
+        quant_z(last, 0, HALF)
         quant_z(last, HALF, HALF)
         mul_z(last)
 

@@ -25,10 +25,10 @@ GROUPS = N // KP
 BANK = 512
 HALF = PAIRS // 2
 PIECE = 128
-RAW_PITCH = KP
-PIECE_PITCH = PIECE
-HEAD_SHARE = 48
-Y_SHARE = 256
+HEAD_SHARE = 56
+GAP_SHARE = 88
+WIDE = 384
+Y_SHARE = 304
 RAW_BYTES = 4 * PACK * KP
 AT_SCALES = RAW_BYTES - 64
 AT_TABLE1 = AT_SCALES + T - 64
@@ -48,7 +48,8 @@ def tile_list_clamped_landmark_differences_kernel(
         pos1_sb = keep.tile([P, PAIRS // 16], U16, name="pos1_sb")
         pos2_sb = keep.tile([P, PAIRS // 16], U16, name="pos2_sb")
         tabs = shared.tile([P, T], U8, name="tabs", offset=AT_SCALES, align_bytes=64)
-        w2w_raw = keep.tile([P, B_PASSES * 2 * N], U8, name="w2w_raw", align_bytes=64)
+        w2w_raw = keep.tile([P, (B_PASSES - 1) * 2 * N], U8, name="w2w_raw", align_bytes=64)
+        w2w_last_raw = keep.tile([P, 2 * N], U8, name="w2w_last_raw", align_bytes=64)
         w2s_raw = keep.tile([P, N], U8, name="w2s_raw")
         planes = keep.tile([P, B_PASSES * N], U8, name="planes", align_bytes=64)
         w2s = planes[:].rearrange("p (u b c) -> p u b c", b=B_PASSES, c=2 * P)
@@ -69,11 +70,11 @@ def tile_list_clamped_landmark_differences_kernel(
 
         def load_w1(b, a, offset=None):
             if offset is None:
-                raw = keep.tile([P, PACK, RAW_PITCH], F32, name="w1_raw", tag="first_raw", align_bytes=64)
+                raw = keep.tile([P, PACK, KP], F32, name="w1_raw", tag="first_raw", align_bytes=64)
             else:
-                raw = shared.tile([P, PACK, RAW_PITCH], F32, name="w1_raw%d%d" % (b, a), offset=offset, align_bytes=64)
+                raw = shared.tile([P, PACK, KP], F32, name="w1_raw%d%d" % (b, a), offset=offset, align_bytes=64)
             nc.sync.dma_start(
-                out=raw[:, :, 0:KP],
+                out=raw[:],
                 in_=w1[KP * a : KP * (a + 1), KP * b : KP * (b + 1)].rearrange("(p j) c -> p j c", j=PACK),
             )
             w1_raw[b, a] = raw
@@ -87,8 +88,8 @@ def tile_list_clamped_landmark_differences_kernel(
         nc.sync.dma_start(pos2_sb[:], pos2)
         nc.sync.dma_start(pos1_sb[:], pos1)
         nc.sync.dma_start(
-            out=w2w_raw[:].bitcast(I32).rearrange("p (b c) -> p b c", b=B_PASSES),
-            in_=w2_words.bitcast(I32).rearrange("b p c -> p b c"),
+            out=w2w_raw[:].bitcast(I32).rearrange("p (b c) -> p b c", b=B_PASSES - 1),
+            in_=w2_words[0 : B_PASSES - 1].bitcast(I32).rearrange("b p c -> p b c"),
         )
         load_table(0, AT_TABLE0)
         load_w1(0, 0)
@@ -110,25 +111,25 @@ def tile_list_clamped_landmark_differences_kernel(
         load_table(1, AT_TABLE1)
         move_table_scales(1)
         load_w1(0, 1, offset=0)
+        nc.sync.dma_start(out=w2w_last_raw[:].bitcast(I32), in_=w2_words[B_PASSES - 1].bitcast(I32))
 
         w2w = {}
 
-        def deal_w2_words(b, dealt):
+        def deal_w2_words(b, dealt, raw):
             w2w[b] = dealt
             nc.vector.tensor_copy(
                 out=dealt.bitcast(U16).rearrange("p (r t c i) -> p r c t i", t=PACK, c=16, i=8),
-                in_=w2w_raw[:, 2 * N * b : 2 * N * (b + 1)].bitcast(U16).rearrange("p (r c i t) -> p r c t i", t=PACK, c=16, i=8),
+                in_=raw.bitcast(U16).rearrange("p (r c i t) -> p r c t i", t=PACK, c=16, i=8),
             )
 
         w2w_first = shared.tile([P, 2 * N], U8, name="w2w_first", offset=RAW_BYTES, align_bytes=64)
-        deal_w2_words(0, w2w_first[:])
+        deal_w2_words(0, w2w_first[:], w2w_raw[:, 0 : 2 * N])
         w2s_dealt = shared.tile([P, N], U8, name="w2s_dealt", offset=RAW_BYTES + 2 * N, align_bytes=64)
         nc.vector.tensor_copy(
             out=w2s_dealt[:].rearrange("p (r t c i) -> p r c t i", t=PACK, c=8, i=16),
             in_=w2s_raw[:].rearrange("p (r c i t) -> p r c t i", t=PACK, c=8, i=16),
         )
-        for b in range(1, B_PASSES):
-            deal_w2_words(b, w2w_raw[:, 2 * N * (b - 1) : 2 * N * b])
+        deal_w2_words(1, w2w_raw[:, 0 : 2 * N], w2w_raw[:, 2 * N :])
         vw = [keep.tile([P, S], U32, name="vw0", align_bytes=64)]
         nc.vector.tensor_copy(out=vw[0][:], in_=tabw[0][:].bitcast(U32).indirect(offs_sb[:]))
 
@@ -142,20 +143,15 @@ def tile_list_clamped_landmark_differences_kernel(
             else:
                 engine.tensor_copy(out=dst, in_=src)
 
-        def cast_w1(b, a, engine, m0=0, m1=P, pairs=(0, 2)):
-            if (b, a) not in w1_bf:
-                w1_bf[b, a] = keep.tile([P, PACK * KP], BF16, name="w1_bf", tag="bf%d%d" % (b, a), align_bytes=64)
-            if engine is nc.vector:
-                dst = w1_bf[b, a][:].rearrange("p (t m j) -> p m t j", t=PACK, j=PACK)[:, m0:m1]
-                src = w1_raw[b, a][:, :, 0:KP].rearrange("p j (m t) -> p m t j", t=PACK)[:, m0:m1]
-                copy_on(engine, dst, src)
-                return
-            dst = w1_bf[b, a][:].rearrange("p (t m j) -> p m j t", t=PACK, j=PACK)[:, m0:m1]
-            src = w1_raw[b, a][:, :, 0:KP].rearrange("p j (m t) -> p m j t", t=PACK)[:, m0:m1]
-            for t0 in pairs:
-                copy_on(engine, dst[:, :, :, t0 : t0 + 2], src[:, :, :, t0 : t0 + 2])
+        def cast_w1(b, a, t0, engine, m0=0, m1=P):
+            if (b, a, t0) not in w1_bf:
+                w1_bf[b, a, t0] = keep.tile([P, 2 * KP], BF16, name="w1_bf", tag="bf%d%d%d" % (b, a, t0), align_bytes=64)
+            order = "m t j" if engine is nc.vector else "m j t"
+            dst = w1_bf[b, a, t0][:].rearrange("p (t m j) -> p " + order, t=2, j=PACK)
+            src = w1_raw[b, a][:].rearrange("p j (m t) -> p j m t", t=PACK)[:, :, :, t0 : t0 + 2].rearrange("p j m t -> p " + order)
+            copy_on(engine, dst[:, m0:m1], src[:, m0:m1])
 
-        def quant_w1(b, a, t0=0, t1=PACK):
+        def quant_w1(b, a, t0, t1):
             if (b, a) not in w1s:
                 w1s[b, a] = keep.tile([P, KP], U8, name="w1s%d%d" % (b, a), align_bytes=64)
             codes = keep.tile([P, P * (t1 - t0)], U32, name="w1c%d%d%d" % (b, a, t0), align_bytes=64)
@@ -164,7 +160,7 @@ def tile_list_clamped_landmark_differences_kernel(
             nc.vector.quantize_mx(
                 out=codes[:].bitcast(FP8X4),
                 scales=w1s[b, a][:, P * t0 : P * t1],
-                in_=w1_bf[b, a][:, KP * t0 : KP * t1],
+                in_=w1_bf[b, a, t0 - t0 % 2][:, KP * (t0 % 2) : KP * (t0 % 2 + t1 - t0)],
             )
 
         h = {}
@@ -248,19 +244,24 @@ def tile_list_clamped_landmark_differences_kernel(
                         stop=(b == B_PASSES - 1),
                     )
 
-        cast_w1(0, 0, nc.scalar)
+        for t0 in (0, 2):
+            cast_w1(0, 0, t0, nc.scalar)
         load_w1(1, 0, offset=AT_TABLE0 + 512)
         load_w1(1, 1)
-        quant_w1(0, 0)
-        vw.append(keep.tile([P, S], U32, name="vw1", tag="bf00", align_bytes=64))
+        for t0 in (0, 2):
+            quant_w1(0, 0, t0, t0 + 2)
+        vw.append(keep.tile([P, S], U32, name="vw1", tag="bf002", align_bytes=64))
         nc.vector.tensor_copy(out=vw[1][:], in_=tabw[1][:].bitcast(U32).indirect(offs_sb[:]))
         load_w1(2, 0, offset=AT_TABLE1)
         load_w1(2, 1, offset=AT_TABLE1 + RAW_BYTES)
-        cast_w1(0, 1, nc.scalar, 0, HEAD_SHARE)
-        cast_w1(0, 1, nc.vector, HEAD_SHARE, P)
+        for t0, share in ((0, HEAD_SHARE), (2, GAP_SHARE)):
+            cast_w1(0, 1, t0, nc.scalar, 0, share)
+            cast_w1(0, 1, t0, nc.vector, share, P)
         quant_w1(0, 1, 0, 1)
         quant_w1(0, 1, 1, 2)
         quant_w1(0, 1, 2, 4)
+        w2w_last = keep.tile([P, 2 * N], U8, name="w2w_last", tag="bf010", align_bytes=64)
+        deal_w2_words(2, w2w_last[:], w2w_last_raw[:])
         for s in range(PACK):
             for a in range(A_PASSES):
                 mul_h(s, a)
@@ -288,53 +289,36 @@ def tile_list_clamped_landmark_differences_kernel(
         later = [(b, a, t0) for b in range(1, B_PASSES) for t0 in (0, 2) for a in range(A_PASSES)]
         for s, (b, a, t0) in enumerate(later):
             pick_slice(s)
-            cast_w1(b, a, nc.scalar, pairs=(t0,))
+            cast_w1(b, a, t0, nc.scalar)
             quant_w1(b, a, t0, t0 + 2)
+            if s + 1 == 2 * PACK:
+                for t in range(PACK):
+                    weigh_slice(0, t)
             if s + 1 < PACK:
                 empty_h(s + 1)
             else:
                 make_h(s + 1)
 
         last = B_PASSES - 1
-        wide = keep.tile([P, PACK, HALF], F32, name="wide")
-        wide_plane = keep.tile([P, PACK, HALF], BF16, name="wide_plane", tag="wide_plane", align_bytes=64)
-        late_second = keep.tile([P, PACK, HALF], F32, name="late_second")
-        third = keep.tile([P, PACK, PIECE_PITCH], F32, name="third")
+        wide = keep.tile([P, PACK, WIDE], F32, name="wide")
+        wide_plane = keep.tile([P, PACK, WIDE], BF16, name="wide_plane", tag="wide_plane", align_bytes=64)
 
-        def pick_last(t, wide_last, spare):
+        def pick_wide(t):
             s = PACK * last + t
-            picks = [
-                lambda: pick_second(s, spare, 0, HALF),
-                lambda: pick_second(s, late_second[:, t, :], HALF, HALF),
-                lambda: pick_diff(s, wide[:, t, :], spare, 0, HALF),
-                lambda: pick_diff(s, third[:, t, 0:PIECE], late_second[:, t, 0:PIECE], HALF, PIECE),
-            ]
-            for step in (1, 0, 3, 2) if wide_last else (0, 1, 2, 3):
-                picks[step]()
+            runs = (slice(0, PIECE), slice(PIECE, WIDE))
+            for run in runs:
+                pick_second(s, second[s % 2][:, run], run.start, run.stop - run.start)
+            for run in runs:
+                pick_diff(s, wide[:, t, run], second[s % 2][:, run], run.start, run.stop - run.start)
+            clamp(nc.gpsimd, wide[:, t, :], wide[:, t, :])
 
-        def pick_last_and_weigh(t, wide_last, b, tb):
-            pick_last(t, wide_last, zplane[b][:, tb, :].bitcast(F32))
-            nc.gpsimd.tensor_scalar(
-                out=zplane[b][:, tb, :], in0=diff[b][:, tb, :], scalar1=gain_sb[:, b, tb : tb + 1], scalar2=1.0, op0=ALU.mult, op1=ALU.mult
-            )
-
-        def weigh_woven(j0, src):
-            nc.vector.tensor_tensor(
-                out=zword[last][:, PACK * j0 : PACK * (j0 + PIECE)].rearrange("p (j t) -> p j t", t=PACK),
-                in0=src,
-                in1=gain_sb[:, last, :].unsqueeze(1).to_broadcast([P, PIECE, PACK]),
-                op=ALU.mult,
-            )
-
-        pick_last_and_weigh(0, False, 0, 3)
+        pick_wide(0)
         make_h(9)
-        pick_last_and_weigh(1, False, 1, 2)
-        for t in range(PACK - 1):
-            weigh_slice(0, t)
-        make_h(10)
-        pick_last_and_weigh(2, True, 1, 3)
+        pick_wide(1)
         weave(nc.scalar, zword[0][:], zplane[0][:], 4)
         quant_z(0, 0, PAIRS)
+        make_h(10)
+        pick_wide(2)
         make_h(11)
         for b in range(B_PASSES):
             for r in range(4):
@@ -343,26 +327,34 @@ def tile_list_clamped_landmark_differences_kernel(
                     in_=w2s_dealt[32 * b + 2 * r : 32 * (b + 1) : 8, :].rearrange("p (u c) -> p u c", c=2 * P).bitcast(I32),
                 )
         mul_z(0)
-        pick_last(3, True, second[1][:, 0:HALF])
-        for t in range(2):
+        pick_wide(3)
+        for t in range(PACK):
             weigh_slice(1, t)
         weave(nc.scalar, zword[1][:], zplane[1][:], 4)
-
-        woven_third = second[0][:].rearrange("p (j t) -> p j t", t=PACK)
-        clamp(nc.vector, woven_third, third[:, :, 0:PIECE].rearrange("p t j -> p j t"))
-        clamp(nc.vector, wide[:], wide[:])
         for t in range(PACK):
             weigh(last, t, wide_plane[:, t, :], wide[:, t, :])
-        weave(nc.scalar, zword[last][:, 0 : PACK * HALF], wide_plane[:], 4)
-        weigh_woven(HALF, woven_third)
+        weave(nc.scalar, zword[last][:, 0 : PACK * WIDE], wide_plane[:], 4)
+
+        late_second = second[1][:].rearrange("p (t j) -> p t j", t=PACK)
+        for t in range(PACK):
+            pick_second(PACK * last + t, late_second[:, t, :], WIDE, PIECE)
         quant_z(1, 0, PAIRS)
         mul_z(1)
-        fourth = words_of(zplane[1][:].rearrange("p t j -> p (t j)"), PACK * PIECE_PITCH).rearrange("p (t j) -> p t j", t=PACK)
+        late = words_of(zplane[1][:].rearrange("p t j -> p (t j)"), PACK * PIECE).rearrange("p (t j) -> p t j", t=PACK)
         for t in range(PACK):
-            pick_diff(PACK * last + t, fourth[:, t, 0:PIECE], late_second[:, t, PIECE:HALF], HALF + PIECE, PIECE)
-        woven = second[1][:].rearrange("p (j t) -> p j t", t=PACK)
-        clamp(nc.vector, woven, fourth[:, :, 0:PIECE].rearrange("p t j -> p j t"))
-        weigh_woven(HALF + PIECE, woven)
+            pick_diff(PACK * last + t, late[:, t, :], late_second[:, t, :], WIDE, PIECE)
+        woven = second[0][:].rearrange("p (j t) -> p j t", t=PACK)
+        late_words = zword[last][:, PACK * WIDE :].rearrange("p (j t) -> p j t", t=PACK)
+        late_halves = (slice(0, PIECE // 2), slice(PIECE // 2, PIECE))
+        for run in late_halves:
+            clamp(nc.vector, woven[:, run], late.rearrange("p t j -> p j t")[:, run])
+        for run in late_halves:
+            nc.vector.tensor_tensor(
+                out=late_words[:, run],
+                in0=woven[:, run],
+                in1=gain_sb[:, last, :].unsqueeze(1).to_broadcast([P, PIECE // 2, PACK]),
+                op=ALU.mult,
+            )
         zc.append(keep.tile([P, PAIRS], U32, name="zc_last", tag="wide_plane", align_bytes=64))
         quant_z(last, 0, HALF)
         quant_z(last, HALF, HALF)
@@ -394,26 +386,41 @@ def tile_list_clamped_landmark_differences_kernel(
                 in_=y[g][:, t0:t1, :],
             )
 
-        def quant_y(g):
+        def weave_y(engine, g, j0, j1):
+            weave(engine, yword[g][:, PACK * j0 : PACK * j1], y[g][:, :, j0:j1], 2)
+
+        def quant_y(g, j0):
             nc.vector.quantize_mx(
-                out=yc[g][:].bitcast(FP8X4), scales=ys[:, PAIRS * g : PAIRS * (g + 1)], in_=yword[g][:]
+                out=yc[g][:, j0 : j0 + HALF].bitcast(FP8X4),
+                scales=ys[:, PAIRS * g + j0 : PAIRS * g + j0 + HALF],
+                in_=yword[g][:, PACK * j0 : PACK * (j0 + HALF)],
             )
-            nc.sync.dma_start(out=out_1[g].rearrange("p m t -> p (m t)").bitcast(I32), in_=yc[g][:].bitcast(I32))
+
+        def store_codes(g, j0, j1):
+            nc.sync.dma_start(
+                out=out_1[g].rearrange("p m t -> p (m t)").bitcast(I32)[:, j0:j1], in_=yc[g][:, j0:j1].bitcast(I32)
+            )
 
         for t in range(PACK):
             add_bias(0, t, nc.scalar if t % 2 else nc.vector)
             if t != 2:
                 store_y(0, t if t < 2 else 2, t + 1)
         add_bias(1, 0, nc.vector)
-        weave(nc.vector, yword[0][:], y[0][:], 2)
+        for j0 in (0, HALF):
+            weave_y(nc.vector, 0, j0, j0 + HALF)
         for t in range(1, PACK):
             add_bias(1, t, nc.scalar)
             if t % 2:
                 store_y(1, t - 1, t + 1)
-        quant_y(0)
-        weave(nc.vector, yword[1][:, 0 : PACK * Y_SHARE], y[1][:, :, 0:Y_SHARE], 2)
-        weave(nc.scalar, yword[1][:, PACK * Y_SHARE :], y[1][:, :, Y_SHARE:], 2)
-        quant_y(1)
+        for j0 in (0, HALF):
+            quant_y(0, j0)
+        store_codes(0, 0, PAIRS)
+        weave_y(nc.vector, 1, 0, HALF)
+        weave_y(nc.vector, 1, HALF, Y_SHARE)
+        weave_y(nc.scalar, 1, Y_SHARE, PAIRS)
+        for j0 in (0, HALF):
+            quant_y(1, j0)
+            store_codes(1, j0, j0 + HALF)
         for quad in range(4):
             nc.scalar.dma_start(
                 out=out_2[:, 4 * quad : 4 * quad + 4, :].bitcast(I32).rearrange("g r m -> r g m"),

@@ -25,8 +25,7 @@ GROUPS = N // KP
 BANK = 512
 HALF = PAIRS // 2
 PIECE = 128
-HEAD_SHARE = 56
-GAP_SHARE = 88
+GAP_SHARE = 104
 WIDE = 384
 Y_SHARE = 304
 RAW_BYTES = 4 * PACK * KP
@@ -68,15 +67,14 @@ def tile_list_clamped_landmark_differences_kernel(
         w1_raw = {}
         tabw = {}
 
-        def load_w1(b, a, offset=None):
+        def load_w1(b, a, offset=None, pieces=1):
             if offset is None:
                 raw = keep.tile([P, PACK, KP], F32, name="w1_raw", tag="first_raw", align_bytes=64)
             else:
                 raw = shared.tile([P, PACK, KP], F32, name="w1_raw%d%d" % (b, a), offset=offset, align_bytes=64)
-            nc.sync.dma_start(
-                out=raw[:],
-                in_=w1[KP * a : KP * (a + 1), KP * b : KP * (b + 1)].rearrange("(p j) c -> p j c", j=PACK),
-            )
+            rows = w1[KP * a : KP * (a + 1), KP * b : KP * (b + 1)].rearrange("(p j) c -> p j c", j=PACK)
+            for c0 in range(0, KP, KP // pieces):
+                nc.sync.dma_start(out=raw[:, :, c0 : c0 + KP // pieces], in_=rows[:, :, c0 : c0 + KP // pieces])
             w1_raw[b, a] = raw
 
         def load_table(a, offset):
@@ -110,7 +108,7 @@ def tile_list_clamped_landmark_differences_kernel(
         move_table_scales(0)
         load_table(1, AT_TABLE1)
         move_table_scales(1)
-        load_w1(0, 1, offset=0)
+        load_w1(0, 1, offset=0, pieces=2)
         nc.sync.dma_start(out=w2w_last_raw[:].bitcast(I32), in_=w2_words[B_PASSES - 1].bitcast(I32))
 
         w2w = {}
@@ -215,7 +213,7 @@ def tile_list_clamped_landmark_differences_kernel(
                 src.rearrange("p t (c i) -> p c t i", i=run),
             )
 
-        zc = [keep.tile([P, PAIRS], U32, name="zc%d" % b, align_bytes=64) for b in range(B_PASSES - 1)]
+        zc = {1: keep.tile([P, PAIRS], U32, name="zc1", align_bytes=64)}
         zs = [keep.tile([P, PAIRS], U8, name="zs%d" % b, align_bytes=64) for b in range(B_PASSES)]
         zword = [keep.tile([P, PACK * PAIRS], BF16, name="zword%d" % b, align_bytes=64) for b in range(B_PASSES)]
 
@@ -254,9 +252,11 @@ def tile_list_clamped_landmark_differences_kernel(
         nc.vector.tensor_copy(out=vw[1][:], in_=tabw[1][:].bitcast(U32).indirect(offs_sb[:]))
         load_w1(2, 0, offset=AT_TABLE1)
         load_w1(2, 1, offset=AT_TABLE1 + RAW_BYTES)
-        for t0, share in ((0, HEAD_SHARE), (2, GAP_SHARE)):
-            cast_w1(0, 1, t0, nc.scalar, 0, share)
-            cast_w1(0, 1, t0, nc.vector, share, P)
+        for t0 in (0, 2):
+            cast_w1(0, 1, t0, nc.scalar, 0, P // 2)
+        cast_w1(0, 1, 0, nc.vector, P // 2, P)
+        cast_w1(0, 1, 2, nc.vector, GAP_SHARE, P)
+        cast_w1(0, 1, 2, nc.scalar, P // 2, GAP_SHARE)
         quant_w1(0, 1, 0, 1)
         quant_w1(0, 1, 1, 2)
         quant_w1(0, 1, 2, 4)
@@ -267,7 +267,7 @@ def tile_list_clamped_landmark_differences_kernel(
                 mul_h(s, a)
 
         diff = [keep.tile([P, PACK, PAIRS], F32, name="diff%d" % b) for b in range(2)]
-        second = [keep.tile([P, PAIRS], F32, name="second%d" % u) for u in range(2)]
+        second = [keep.tile([P, PAIRS], F32, name="second", tag="second%d" % u, align_bytes=64) for u in range(2)]
         zplane = [keep.tile([P, PACK, PAIRS], BF16, name="zplane%d" % b) for b in range(2)]
 
         def words_of(tile, n):
@@ -286,7 +286,7 @@ def tile_list_clamped_landmark_differences_kernel(
             weigh(b, t, zplane[b][:, t, :], diff[b][:, t, :])
 
         empty_h(0, nc.vector)
-        later = [(b, a, t0) for b in range(1, B_PASSES) for t0 in (0, 2) for a in range(A_PASSES)]
+        later = [(1, a, t0) for a in range(A_PASSES) for t0 in (0, 2)] + [(2, a, t0) for t0 in (0, 2) for a in range(A_PASSES)]
         for s, (b, a, t0) in enumerate(later):
             pick_slice(s)
             cast_w1(b, a, t0, nc.scalar)
@@ -303,22 +303,30 @@ def tile_list_clamped_landmark_differences_kernel(
         wide = keep.tile([P, PACK, WIDE], F32, name="wide")
         wide_plane = keep.tile([P, PACK, WIDE], BF16, name="wide_plane", tag="wide_plane", align_bytes=64)
 
+        late_second = keep.tile([P, PACK, HALF], F32, name="late_second")
+
         def pick_wide(t):
             s = PACK * last + t
-            runs = (slice(0, PIECE), slice(PIECE, WIDE))
-            for run in runs:
-                pick_second(s, second[s % 2][:, run], run.start, run.stop - run.start)
-            for run in runs:
-                pick_diff(s, wide[:, t, run], second[s % 2][:, run], run.start, run.stop - run.start)
-            clamp(nc.gpsimd, wide[:, t, :], wide[:, t, :])
+            spare = second[s % 2][:, 0:HALF]
+            first, third = wide[:, t, 0:HALF], wide[:, t, HALF:WIDE]
+            pick_second(s, spare, 0, HALF)
+            pick_second(s, late_second[:, t, :], HALF, HALF)
+            pick_diff(s, first, spare, 0, HALF)
+            pick_diff(s, third, late_second[:, t, 0:PIECE], HALF, PIECE)
+            if t < PACK - 1:
+                clamp(nc.gpsimd, wide[:, t, :], wide[:, t, :])
+            else:
+                clamp(nc.vector, first, first)
+                clamp(nc.vector, third, third)
 
         pick_wide(0)
         make_h(9)
         pick_wide(1)
         weave(nc.scalar, zword[0][:], zplane[0][:], 4)
-        quant_z(0, 0, PAIRS)
         make_h(10)
         pick_wide(2)
+        zc[0] = keep.tile([P, PAIRS], U32, name="zc0", tag="second0", align_bytes=64)
+        quant_z(0, 0, PAIRS)
         make_h(11)
         for b in range(B_PASSES):
             for r in range(4):
@@ -335,15 +343,12 @@ def tile_list_clamped_landmark_differences_kernel(
             weigh(last, t, wide_plane[:, t, :], wide[:, t, :])
         weave(nc.scalar, zword[last][:, 0 : PACK * WIDE], wide_plane[:], 4)
 
-        late_second = second[1][:].rearrange("p (t j) -> p t j", t=PACK)
-        for t in range(PACK):
-            pick_second(PACK * last + t, late_second[:, t, :], WIDE, PIECE)
         quant_z(1, 0, PAIRS)
         mul_z(1)
         late = words_of(zplane[1][:].rearrange("p t j -> p (t j)"), PACK * PIECE).rearrange("p (t j) -> p t j", t=PACK)
         for t in range(PACK):
-            pick_diff(PACK * last + t, late[:, t, :], late_second[:, t, :], WIDE, PIECE)
-        woven = second[0][:].rearrange("p (j t) -> p j t", t=PACK)
+            pick_diff(PACK * last + t, late[:, t, :], late_second[:, t, PIECE:HALF], WIDE, PIECE)
+        woven = second[1][:].rearrange("p (j t) -> p j t", t=PACK)
         late_words = zword[last][:, PACK * WIDE :].rearrange("p (j t) -> p j t", t=PACK)
         late_halves = (slice(0, PIECE // 2), slice(PIECE // 2, PIECE))
         for run in late_halves:
@@ -355,7 +360,7 @@ def tile_list_clamped_landmark_differences_kernel(
                 in1=gain_sb[:, last, :].unsqueeze(1).to_broadcast([P, PIECE // 2, PACK]),
                 op=ALU.mult,
             )
-        zc.append(keep.tile([P, PAIRS], U32, name="zc_last", tag="wide_plane", align_bytes=64))
+        zc[last] = keep.tile([P, PAIRS], U32, name="zc_last", tag="wide_plane", align_bytes=64)
         quant_z(last, 0, HALF)
         quant_z(last, HALF, HALF)
         mul_z(last)

@@ -32,6 +32,7 @@ RAW_BYTES = 4 * PACK * KP
 AT_SCALES = RAW_BYTES - 64
 AT_TABLE1 = AT_SCALES + T - 64
 AT_TABLE0 = AT_TABLE1 + 4 * T
+AT_FIRST_BF = AT_TABLE0 + 512 + RAW_BYTES
 
 
 def tile_list_clamped_landmark_differences_kernel(
@@ -58,6 +59,9 @@ def tile_list_clamped_landmark_differences_kernel(
         gain_sb = keep.tile([P, B_PASSES, PACK], F32, name="gain_sb")
         bias_sb = keep.tile([P, GROUPS, PACK], F32, name="bias_sb")
 
+        warm = keep.tile([P, 2], F32, name="warm")
+        nc.vector.memset(warm[:, 0:1], 0.0)
+        nc.scalar.copy(out=warm[:, 1:2], in_=warm[:, 0:1])
         nc.vector.memset(w2s_raw[:].bitcast(I32), 0)
         nc.vector.memset(tabs[32:64, :].bitcast(I32), 0)
         nc.vector.memset(tabs[64:P, :].bitcast(I32), 0)
@@ -131,6 +135,7 @@ def tile_list_clamped_landmark_differences_kernel(
         vw = [keep.tile([P, S], U32, name="vw0", align_bytes=64)]
         nc.vector.tensor_copy(out=vw[0][:], in_=tabw[0][:].bitcast(U32).indirect(offs_sb[:]))
 
+        first_bf = shared.tile([P, PACK * KP], BF16, name="first_bf", offset=AT_FIRST_BF, align_bytes=64)
         w1_bf = {}
         w1c = {}
         w1s = {}
@@ -143,9 +148,12 @@ def tile_list_clamped_landmark_differences_kernel(
 
         def cast_w1(b, a, t0, engine, m0=0, m1=P):
             if (b, a, t0) not in w1_bf:
-                w1_bf[b, a, t0] = keep.tile([P, 2 * KP], BF16, name="w1_bf", tag="bf%d%d%d" % (b, a, t0), align_bytes=64)
+                if (b, a) == (0, 0):
+                    w1_bf[b, a, t0] = first_bf[:, KP * t0 : KP * (t0 + 2)]
+                else:
+                    w1_bf[b, a, t0] = keep.tile([P, 2 * KP], BF16, name="w1_bf", tag="bf%d%d%d" % (b, a, t0), align_bytes=64)[:]
             order = "m t j" if engine is nc.vector else "m j t"
-            dst = w1_bf[b, a, t0][:].rearrange("p (t m j) -> p " + order, t=2, j=PACK)
+            dst = w1_bf[b, a, t0].rearrange("p (t m j) -> p " + order, t=2, j=PACK)
             src = w1_raw[b, a][:].rearrange("p j (m t) -> p j m t", t=PACK)[:, :, :, t0 : t0 + 2].rearrange("p j m t -> p " + order)
             copy_on(engine, dst[:, m0:m1], src[:, m0:m1])
 
@@ -158,7 +166,7 @@ def tile_list_clamped_landmark_differences_kernel(
             nc.vector.quantize_mx(
                 out=codes[:].bitcast(FP8X4),
                 scales=w1s[b, a][:, P * t0 : P * t1],
-                in_=w1_bf[b, a, t0 - t0 % 2][:, KP * (t0 % 2) : KP * (t0 % 2 + t1 - t0)],
+                in_=first_bf[:] if t1 - t0 == PACK else w1_bf[b, a, t0 - t0 % 2][:, KP * (t0 % 2) : KP * (t0 % 2 + t1 - t0)],
             )
 
         h = {}
@@ -213,7 +221,7 @@ def tile_list_clamped_landmark_differences_kernel(
                 src.rearrange("p t (c i) -> p c t i", i=run),
             )
 
-        zc = {1: keep.tile([P, PAIRS], U32, name="zc1", align_bytes=64)}
+        zc = {b: keep.tile([P, PAIRS], U32, name="zc%d" % b, align_bytes=64) for b in range(1, B_PASSES)}
         zs = [keep.tile([P, PAIRS], U8, name="zs%d" % b, align_bytes=64) for b in range(B_PASSES)]
         zword = [keep.tile([P, PACK * PAIRS], BF16, name="zword%d" % b, align_bytes=64) for b in range(B_PASSES)]
 
@@ -246,9 +254,8 @@ def tile_list_clamped_landmark_differences_kernel(
             cast_w1(0, 0, t0, nc.scalar)
         load_w1(1, 0, offset=AT_TABLE0 + 512)
         load_w1(1, 1)
-        for t0 in (0, 2):
-            quant_w1(0, 0, t0, t0 + 2)
-        vw.append(keep.tile([P, S], U32, name="vw1", tag="bf002", align_bytes=64))
+        quant_w1(0, 0, 0, PACK)
+        vw.append(shared.tile([P, S], U32, name="vw1", offset=AT_FIRST_BF, align_bytes=64))
         nc.vector.tensor_copy(out=vw[1][:], in_=tabw[1][:].bitcast(U32).indirect(offs_sb[:]))
         load_w1(2, 0, offset=AT_TABLE1)
         load_w1(2, 1, offset=AT_TABLE1 + RAW_BYTES)
@@ -268,10 +275,9 @@ def tile_list_clamped_landmark_differences_kernel(
 
         diff = [keep.tile([P, PACK, PAIRS], F32, name="diff%d" % b) for b in range(2)]
         second = [keep.tile([P, PAIRS], F32, name="second", tag="second%d" % u, align_bytes=64) for u in range(2)]
-        zplane = [keep.tile([P, PACK, PAIRS], BF16, name="zplane%d" % b) for b in range(2)]
-
-        def words_of(tile, n):
-            return tile.bitcast(F32)[:, 0:n]
+        first_planes = keep.tile([P, PACK, PAIRS], BF16, name="first_planes")
+        spare_and_planes = keep.tile([P, (1 + PACK) * PAIRS], BF16, name="spare_and_planes")
+        zplane = [first_planes[:], spare_and_planes[:, PAIRS:].rearrange("p (t j) -> p t j", t=PACK)]
 
         def pick_slice(s):
             b, t = divmod(s, PACK)
@@ -289,11 +295,10 @@ def tile_list_clamped_landmark_differences_kernel(
         later = [(1, a, t0) for a in range(A_PASSES) for t0 in (0, 2)] + [(2, a, t0) for t0 in (0, 2) for a in range(A_PASSES)]
         for s, (b, a, t0) in enumerate(later):
             pick_slice(s)
-            cast_w1(b, a, t0, nc.scalar)
+            cast_w1(b, a, t0, nc.scalar, P // 2 if s == PACK else 0, P)
             quant_w1(b, a, t0, t0 + 2)
-            if s + 1 == 2 * PACK:
-                for t in range(PACK):
-                    weigh_slice(0, t)
+            if s + 1 == PACK:
+                cast_w1(*later[PACK], nc.scalar, 0, P // 2)
             if s + 1 < PACK:
                 empty_h(s + 1)
             else:
@@ -301,13 +306,13 @@ def tile_list_clamped_landmark_differences_kernel(
 
         last = B_PASSES - 1
         wide = keep.tile([P, PACK, WIDE], F32, name="wide")
-        wide_plane = keep.tile([P, PACK, WIDE], BF16, name="wide_plane", tag="wide_plane", align_bytes=64)
+        wide_plane = keep.tile([P, PACK, WIDE], BF16, name="wide_plane")
 
         late_second = keep.tile([P, PACK, HALF], F32, name="late_second")
 
         def pick_wide(t):
             s = PACK * last + t
-            spare = second[s % 2][:, 0:HALF]
+            spare = second[s % 2][:, 0:HALF] if t < PACK - 1 else spare_and_planes[:].bitcast(F32)[:, 0:HALF]
             first, third = wide[:, t, 0:HALF], wide[:, t, HALF:WIDE]
             pick_second(s, spare, 0, HALF)
             pick_second(s, late_second[:, t, :], HALF, HALF)
@@ -322,9 +327,13 @@ def tile_list_clamped_landmark_differences_kernel(
         pick_wide(0)
         make_h(9)
         pick_wide(1)
-        weave(nc.scalar, zword[0][:], zplane[0][:], 4)
+        for t in range(PACK):
+            weigh_slice(0, t)
+        for t in range(2):
+            weigh_slice(1, t)
         make_h(10)
         pick_wide(2)
+        weave(nc.scalar, zword[0][:], zplane[0], 4)
         zc[0] = keep.tile([P, PAIRS], U32, name="zc0", tag="second0", align_bytes=64)
         quant_z(0, 0, PAIRS)
         make_h(11)
@@ -336,17 +345,19 @@ def tile_list_clamped_landmark_differences_kernel(
                 )
         mul_z(0)
         pick_wide(3)
-        for t in range(PACK):
+        for t in range(2, PACK):
             weigh_slice(1, t)
-        weave(nc.scalar, zword[1][:], zplane[1][:], 4)
+        weave(nc.scalar, zword[1][:], zplane[1], 4)
         for t in range(PACK):
             weigh(last, t, wide_plane[:, t, :], wide[:, t, :])
-        weave(nc.scalar, zword[last][:, 0 : PACK * WIDE], wide_plane[:], 4)
+        for j0, j1 in ((0, HALF), (HALF, WIDE)):
+            weave(nc.scalar, zword[last][:, PACK * j0 : PACK * j1], wide_plane[:, :, j0:j1], 4)
 
-        quant_z(1, 0, PAIRS)
-        mul_z(1)
-        late = words_of(zplane[1][:].rearrange("p t j -> p (t j)"), PACK * PIECE).rearrange("p (t j) -> p t j", t=PACK)
+        late = spare_and_planes[:].bitcast(F32)[:, 0:PAIRS].rearrange("p (t j) -> p t j", t=PACK)
         for t in range(PACK):
+            if t == 2:
+                quant_z(1, 0, PAIRS)
+                mul_z(1)
             pick_diff(PACK * last + t, late[:, t, :], late_second[:, t, PIECE:HALF], WIDE, PIECE)
         woven = second[1][:].rearrange("p (j t) -> p j t", t=PACK)
         late_words = zword[last][:, PACK * WIDE :].rearrange("p (j t) -> p j t", t=PACK)
@@ -360,7 +371,6 @@ def tile_list_clamped_landmark_differences_kernel(
                 in1=gain_sb[:, last, :].unsqueeze(1).to_broadcast([P, PIECE // 2, PACK]),
                 op=ALU.mult,
             )
-        zc[last] = keep.tile([P, PAIRS], U32, name="zc_last", tag="wide_plane", align_bytes=64)
         quant_z(last, 0, HALF)
         quant_z(last, HALF, HALF)
         mul_z(last)

@@ -402,7 +402,7 @@ def tile_list_clamped_landmark_differences_kernel(
             )
 
         def weave_y(engine, g, j0, j1):
-            weave(engine, yword[g][:, PACK * j0 : PACK * j1], y[g][:, :, j0:j1], 2)
+            weave(engine, yword[g][:, PACK * j0 : PACK * j1], y[g][:, :, j0:j1], 1 if engine is nc.vector else 2)
 
         def quant_y(g, j0):
             nc.vector.quantize_mx(
@@ -435,7 +435,7 @@ def tile_list_clamped_landmark_differences_kernel(
         weave_y(nc.scalar, 1, Y_SHARE, PAIRS)
         for j0 in (0, HALF):
             quant_y(1, j0)
-            store_codes(1, j0, j0 + HALF)
+        store_codes(1, 0, PAIRS)
         for quad in range(4):
             nc.scalar.dma_start(
                 out=out_2[:, 4 * quad : 4 * quad + 4, :].bitcast(I32).rearrange("g r m -> r g m"),

@@ -25,7 +25,8 @@ GROUPS = N // KP
 BANK = 512
 HALF = PAIRS // 2
 PIECE = 128
-GAP_SHARE = 104
+HEAD_SHARE = 76
+GAP_SHARE = 96
 WIDE = 384
 Y_SHARE = 304
 RAW_BYTES = 4 * PACK * KP
@@ -71,14 +72,14 @@ def tile_list_clamped_landmark_differences_kernel(
         w1_raw = {}
         tabw = {}
 
-        def load_w1(b, a, offset=None, pieces=1):
+        def load_w1(b, a, offset=None, cuts=(0, KP)):
             if offset is None:
                 raw = keep.tile([P, PACK, KP], F32, name="w1_raw", tag="first_raw", align_bytes=64)
             else:
                 raw = shared.tile([P, PACK, KP], F32, name="w1_raw%d%d" % (b, a), offset=offset, align_bytes=64)
             rows = w1[KP * a : KP * (a + 1), KP * b : KP * (b + 1)].rearrange("(p j) c -> p j c", j=PACK)
-            for c0 in range(0, KP, KP // pieces):
-                nc.sync.dma_start(out=raw[:, :, c0 : c0 + KP // pieces], in_=rows[:, :, c0 : c0 + KP // pieces])
+            for c0, c1 in zip(cuts, cuts[1:]):
+                nc.sync.dma_start(out=raw[:, :, c0:c1], in_=rows[:, :, c0:c1])
             w1_raw[b, a] = raw
 
         def load_table(a, offset):
@@ -112,7 +113,7 @@ def tile_list_clamped_landmark_differences_kernel(
         move_table_scales(0)
         load_table(1, AT_TABLE1)
         move_table_scales(1)
-        load_w1(0, 1, offset=0, pieces=2)
+        load_w1(0, 1, offset=0, cuts=(0, KP - P, KP))
         nc.sync.dma_start(out=w2w_last_raw[:].bitcast(I32), in_=w2_words[B_PASSES - 1].bitcast(I32))
 
         w2w = {}
@@ -259,11 +260,9 @@ def tile_list_clamped_landmark_differences_kernel(
         nc.vector.tensor_copy(out=vw[1][:], in_=tabw[1][:].bitcast(U32).indirect(offs_sb[:]))
         load_w1(2, 0, offset=AT_TABLE1)
         load_w1(2, 1, offset=AT_TABLE1 + RAW_BYTES)
-        for t0 in (0, 2):
-            cast_w1(0, 1, t0, nc.scalar, 0, P // 2)
-        cast_w1(0, 1, 0, nc.vector, P // 2, P)
-        cast_w1(0, 1, 2, nc.vector, GAP_SHARE, P)
-        cast_w1(0, 1, 2, nc.scalar, P // 2, GAP_SHARE)
+        for t0, share in ((0, HEAD_SHARE), (2, GAP_SHARE)):
+            cast_w1(0, 1, t0, nc.scalar, 0, share)
+            cast_w1(0, 1, t0, nc.vector, share, P)
         quant_w1(0, 1, 0, 1)
         quant_w1(0, 1, 1, 2)
         quant_w1(0, 1, 2, 4)

@@ -33,7 +33,6 @@ RAW_BYTES = 4 * PACK * KP
 AT_SCALES = RAW_BYTES - 64
 AT_TABLE1 = AT_SCALES + T - 64
 AT_TABLE0 = AT_TABLE1 + 4 * T
-AT_FIRST_BF = AT_TABLE0 + 512 + RAW_BYTES
 
 
 def tile_list_clamped_landmark_differences_kernel(
@@ -60,9 +59,6 @@ def tile_list_clamped_landmark_differences_kernel(
         gain_sb = keep.tile([P, B_PASSES, PACK], F32, name="gain_sb")
         bias_sb = keep.tile([P, GROUPS, PACK], F32, name="bias_sb")
 
-        warm = keep.tile([P, 2], F32, name="warm")
-        nc.vector.memset(warm[:, 0:1], 0.0)
-        nc.scalar.copy(out=warm[:, 1:2], in_=warm[:, 0:1])
         nc.vector.memset(w2s_raw[:].bitcast(I32), 0)
         nc.vector.memset(tabs[32:64, :].bitcast(I32), 0)
         nc.vector.memset(tabs[64:P, :].bitcast(I32), 0)
@@ -136,7 +132,7 @@ def tile_list_clamped_landmark_differences_kernel(
         vw = [keep.tile([P, S], U32, name="vw0", align_bytes=64)]
         nc.vector.tensor_copy(out=vw[0][:], in_=tabw[0][:].bitcast(U32).indirect(offs_sb[:]))
 
-        first_bf = shared.tile([P, PACK * KP], BF16, name="first_bf", offset=AT_FIRST_BF, align_bytes=64)
+        first_bf = keep.tile([P, PACK * KP], BF16, name="first_bf", tag="first_bf", align_bytes=64)
         w1_bf = {}
         w1c = {}
         w1s = {}
@@ -256,7 +252,7 @@ def tile_list_clamped_landmark_differences_kernel(
         load_w1(1, 0, offset=AT_TABLE0 + 512)
         load_w1(1, 1)
         quant_w1(0, 0, 0, PACK)
-        vw.append(shared.tile([P, S], U32, name="vw1", offset=AT_FIRST_BF, align_bytes=64))
+        vw.append(keep.tile([P, S], U32, name="vw1", tag="first_bf", align_bytes=64))
         nc.vector.tensor_copy(out=vw[1][:], in_=tabw[1][:].bitcast(U32).indirect(offs_sb[:]))
         load_w1(2, 0, offset=AT_TABLE1)
         load_w1(2, 1, offset=AT_TABLE1 + RAW_BYTES)

@@ -25,14 +25,18 @@ GROUPS = N // KP
 BANK = 512
 HALF = PAIRS // 2
 PIECE = 128
-HEAD_SHARE = 76
-GAP_SHARE = 96
 WIDE = 384
 Y_SHARE = 304
+Z_SHARE = 352
+PLAIN = 2 * PACK
 RAW_BYTES = 4 * PACK * KP
-AT_SCALES = RAW_BYTES - 64
-AT_TABLE1 = AT_SCALES + T - 64
-AT_TABLE0 = AT_TABLE1 + 4 * T
+AT_TABLE0 = 0
+AT_TABLE1 = 4 * T
+AT_RAW0 = 8 * T
+AT_RAW1 = AT_RAW0 + 2 * RAW_BYTES
+AT_W2 = AT_RAW1 + 2 * RAW_BYTES
+AT_W2_SCALES = AT_W2 + B_PASSES * 2 * N
+AT_SCALES = AT_W2_SCALES + 64 - T
 
 
 def tile_list_clamped_landmark_differences_kernel(
@@ -48,8 +52,7 @@ def tile_list_clamped_landmark_differences_kernel(
         pos1_sb = keep.tile([P, PAIRS // 16], U16, name="pos1_sb")
         pos2_sb = keep.tile([P, PAIRS // 16], U16, name="pos2_sb")
         tabs = shared.tile([P, T], U8, name="tabs", offset=AT_SCALES, align_bytes=64)
-        w2w_raw = keep.tile([P, (B_PASSES - 1) * 2 * N], U8, name="w2w_raw", align_bytes=64)
-        w2w_last_raw = keep.tile([P, 2 * N], U8, name="w2w_last_raw", align_bytes=64)
+        w2w_raw = keep.tile([P, B_PASSES * 2 * N], U8, name="w2w_raw", align_bytes=64)
         w2s_raw = keep.tile([P, N], U8, name="w2s_raw")
         planes = keep.tile([P, B_PASSES * N], U8, name="planes", align_bytes=64)
         w2s = planes[:].rearrange("p (u b c) -> p u b c", b=B_PASSES, c=2 * P)
@@ -68,15 +71,17 @@ def tile_list_clamped_landmark_differences_kernel(
         w1_raw = {}
         tabw = {}
 
-        def load_w1(b, a, offset=None, cuts=(0, KP)):
-            if offset is None:
-                raw = keep.tile([P, PACK, KP], F32, name="w1_raw", tag="first_raw", align_bytes=64)
-            else:
-                raw = shared.tile([P, PACK, KP], F32, name="w1_raw%d%d" % (b, a), offset=offset, align_bytes=64)
-            rows = w1[KP * a : KP * (a + 1), KP * b : KP * (b + 1)].rearrange("(p j) c -> p j c", j=PACK)
-            for c0, c1 in zip(cuts, cuts[1:]):
-                nc.sync.dma_start(out=raw[:, :, c0:c1], in_=rows[:, :, c0:c1])
-            w1_raw[b, a] = raw
+        def load_w1(c0, c1, a, offset):
+            raw = shared.tile([P, PACK, c1 - c0], F32, name="w1_raw%d_%d" % (c0, a), offset=offset, align_bytes=64)
+            rows = w1[KP * a : KP * (a + 1), c0:c1].rearrange("(p j) c -> p j c", j=PACK)
+            nc.sync.dma_start(out=raw[:], in_=rows)
+            for c in range(c0, c1, P):
+                w1_raw[c // P, a] = raw[:, :, c - c0 : c - c0 + P]
+            return raw
+
+        def load_plain(s0, s1, base):
+            for a in range(A_PASSES):
+                load_w1(P * s0, P * s1, a, base + 4 * PACK * P * (A_PASSES * (s0 % PACK) + a * (s1 - s0)))
 
         def load_table(a, offset):
             tabw[a] = shared.tile([P, T], I32, name="tabw%d" % a, offset=offset, align_bytes=64)
@@ -84,17 +89,12 @@ def tile_list_clamped_landmark_differences_kernel(
 
         nc.sync.dma_start(offs_sb[:], offs)
         nc.sync.dma_start(out=tabs[0:32, :].bitcast(I32), in_=tab_scales.rearrange("a q t -> (a q) t").bitcast(I32))
-        nc.sync.dma_start(pos2_sb[:], pos2)
-        nc.sync.dma_start(pos1_sb[:], pos1)
         nc.sync.dma_start(
-            out=w2w_raw[:].bitcast(I32).rearrange("p (b c) -> p b c", b=B_PASSES - 1),
-            in_=w2_words[0 : B_PASSES - 1].bitcast(I32).rearrange("b p c -> p b c"),
+            out=w2w_raw[:].bitcast(I32).rearrange("p (b c) -> p b c", b=B_PASSES),
+            in_=w2_words.bitcast(I32).rearrange("b p c -> p b c"),
         )
+        nc.sync.dma_start(out=w2s_raw[0:96:2, :].bitcast(I32), in_=w2_scales.rearrange("b q c -> (b q) c").bitcast(I32))
         load_table(0, AT_TABLE0)
-        load_w1(0, 0)
-        nc.scalar.dma_start(out=gain_sb[:], in_=gain.rearrange("(b p t) -> p b t", b=B_PASSES, t=PACK))
-        nc.scalar.dma_start(out=bias_sb[:], in_=bias.rearrange("(g p t) -> p g t", g=GROUPS, t=PACK))
-        nc.scalar.dma_start(out=w2s_raw[0:96:2, :].bitcast(I32), in_=w2_scales.rearrange("b q c -> (b q) c").bitcast(I32))
 
         vs_picked = keep.tile([P, S], U8, name="vs_picked")
         nc.vector.tensor_copy(out=vs_picked[:], in_=tabs[:].indirect(offs_sb[:]))
@@ -106,36 +106,40 @@ def tile_list_clamped_landmark_differences_kernel(
                     in_=vs_picked[16 * a + r : 16 * (a + 1) : 4, :].bitcast(I32),
                 )
 
-        move_table_scales(0)
-        load_table(1, AT_TABLE1)
         move_table_scales(1)
-        load_w1(0, 1, offset=0, cuts=(0, KP - P, KP))
-        nc.sync.dma_start(out=w2w_last_raw[:].bitcast(I32), in_=w2_words[B_PASSES - 1].bitcast(I32))
+        load_plain(0, 1, AT_RAW0)
+        load_table(1, AT_TABLE1)
+        move_table_scales(0)
+        load_plain(1, 2, AT_RAW0)
+        nc.sync.dma_start(pos2_sb[:], pos2)
+        nc.sync.dma_start(pos1_sb[:], pos1)
+        load_plain(2, 3, AT_RAW0)
+        load_plain(3, 4, AT_RAW0)
+        load_plain(4, 6, AT_RAW1)
+        load_plain(6, 8, AT_RAW1)
+        dealt_raw = [load_w1(2 * KP, 3 * KP, a, AT_TABLE0 + RAW_BYTES * a) for a in range(A_PASSES)]
+        nc.sync.dma_start(out=gain_sb[:], in_=gain.rearrange("(b p t) -> p b t", b=B_PASSES, t=PACK))
+        nc.sync.dma_start(out=bias_sb[:], in_=bias.rearrange("(g p t) -> p g t", g=GROUPS, t=PACK))
 
-        w2w = {}
+        w2w = shared.tile([P, B_PASSES * 2 * N], U8, name="w2w", offset=AT_W2, align_bytes=64)
 
-        def deal_w2_words(b, dealt, raw):
-            w2w[b] = dealt
+        def deal_w2_words(b):
+            run = slice(2 * N * b, 2 * N * (b + 1))
             nc.vector.tensor_copy(
-                out=dealt.bitcast(U16).rearrange("p (r t c i) -> p r c t i", t=PACK, c=16, i=8),
-                in_=raw.bitcast(U16).rearrange("p (r c i t) -> p r c t i", t=PACK, c=16, i=8),
+                out=w2w[:, run].bitcast(U16).rearrange("p (r t c i) -> p r c t i", t=PACK, c=16, i=8),
+                in_=w2w_raw[:, run].bitcast(U16).rearrange("p (r c i t) -> p r c t i", t=PACK, c=16, i=8),
             )
 
-        w2w_first = shared.tile([P, 2 * N], U8, name="w2w_first", offset=RAW_BYTES, align_bytes=64)
-        deal_w2_words(0, w2w_first[:], w2w_raw[:, 0 : 2 * N])
-        w2s_dealt = shared.tile([P, N], U8, name="w2s_dealt", offset=RAW_BYTES + 2 * N, align_bytes=64)
+        deal_w2_words(0)
+        w2s_dealt = shared.tile([P, N], U8, name="w2s_dealt", offset=AT_W2_SCALES, align_bytes=64)
         nc.vector.tensor_copy(
             out=w2s_dealt[:].rearrange("p (r t c i) -> p r c t i", t=PACK, c=8, i=16),
             in_=w2s_raw[:].rearrange("p (r c i t) -> p r c t i", t=PACK, c=8, i=16),
         )
-        deal_w2_words(1, w2w_raw[:, 0 : 2 * N], w2w_raw[:, 2 * N :])
-        vw = [keep.tile([P, S], U32, name="vw0", align_bytes=64)]
+        vw = [keep.tile([P, S], U32, name="vw%d" % a, align_bytes=64) for a in range(A_PASSES)]
         nc.vector.tensor_copy(out=vw[0][:], in_=tabw[0][:].bitcast(U32).indirect(offs_sb[:]))
-
-        first_bf = keep.tile([P, PACK * KP], BF16, name="first_bf", tag="first_bf", align_bytes=64)
-        w1_bf = {}
-        w1c = {}
-        w1s = {}
+        deal_w2_words(1)
+        deal_w2_words(2)
 
         def copy_on(engine, dst, src):
             if engine is nc.scalar:
@@ -143,56 +147,68 @@ def tile_list_clamped_landmark_differences_kernel(
             else:
                 engine.tensor_copy(out=dst, in_=src)
 
-        def cast_w1(b, a, t0, engine, m0=0, m1=P):
-            if (b, a, t0) not in w1_bf:
-                if (b, a) == (0, 0):
-                    w1_bf[b, a, t0] = first_bf[:, KP * t0 : KP * (t0 + 2)]
-                else:
-                    w1_bf[b, a, t0] = keep.tile([P, 2 * KP], BF16, name="w1_bf", tag="bf%d%d%d" % (b, a, t0), align_bytes=64)[:]
-            order = "m t j" if engine is nc.vector else "m j t"
-            dst = w1_bf[b, a, t0].rearrange("p (t m j) -> p " + order, t=2, j=PACK)
-            src = w1_raw[b, a][:].rearrange("p j (m t) -> p j m t", t=PACK)[:, :, :, t0 : t0 + 2].rearrange("p j m t -> p " + order)
-            copy_on(engine, dst[:, m0:m1], src[:, m0:m1])
+        w1c = {}
+        w1s = {}
 
-        def quant_w1(b, a, t0, t1):
-            if (b, a) not in w1s:
-                w1s[b, a] = keep.tile([P, KP], U8, name="w1s%d%d" % (b, a), align_bytes=64)
-            codes = keep.tile([P, P * (t1 - t0)], U32, name="w1c%d%d%d" % (b, a, t0), align_bytes=64)
-            for t in range(t0, t1):
-                w1c[b, a, t] = codes[:, P * (t - t0) : P * (t - t0 + 1)]
-            nc.vector.quantize_mx(
-                out=codes[:].bitcast(FP8X4),
-                scales=w1s[b, a][:, P * t0 : P * t1],
-                in_=first_bf[:] if t1 - t0 == PACK else w1_bf[b, a, t0 - t0 % 2][:, KP * (t0 % 2) : KP * (t0 % 2 + t1 - t0)],
+        def cast_plain(s, a, dst):
+            nc.scalar.copy(
+                out=dst.rearrange("p (c i j) -> p c j i", i=2, j=PACK),
+                in_=w1_raw[s, a].rearrange("p j (c i) -> p c j i", i=2),
             )
+
+        def cast_dealt(s, a, dst):
+            nc.scalar.copy(
+                out=dst.rearrange("p (t m j) -> p m j t", t=2, j=PACK),
+                in_=dealt_raw[a][:].rearrange("p j (m t) -> p m j t", t=PACK)[:, :, :, s - PLAIN : s - PLAIN + 2],
+            )
+
+        quantised = []
+
+        def ready_w1(holds, behind=None):
+            tag = "bf%d" % (len(quantised) % 3) if behind is None else "w1c%d_%d" % behind
+            src = keep.tile([P, KP * len(holds)], BF16, name="w1_bf", tag=tag, align_bytes=64)
+            codes = keep.tile([P, P * len(holds)], U32, name="w1c%d_%d" % holds[0], align_bytes=64)
+            scales = keep.tile([P, P * len(holds)], U8, name="w1s%d_%d" % holds[0], align_bytes=64)
+            for n, (s, a) in enumerate(holds):
+                if s < PLAIN:
+                    cast_plain(s, a, src[:, KP * n : KP * (n + 1)])
+                elif s % 2 == 0:
+                    cast_dealt(s, a, src[:, KP * n : KP * (n + 2)])
+                w1c[s, a] = codes[:, P * n : P * (n + 1)]
+                w1s[s, a] = scales[:, P * n : P * (n + 1)]
+            nc.vector.quantize_mx(out=codes[:].bitcast(FP8X4), scales=scales[:], in_=src[:])
+            quantised.append(holds)
 
         h = {}
         hacc = {}
 
-        def mul_h(s, a):
-            b, t = divmod(s, PACK)
-            for half in range(2):
-                if a == 0:
-                    hacc[s, half] = psum.tile([P, BANK], F32, name="hacc", tag="bank%d" % (2 * t + half))
-                nc.tensor.matmul_mx(
-                    out=hacc[s, half][:],
-                    lhsT=w1c[b, a, t].bitcast(FP8X4),
-                    lhsT_scale=w1s[b, a][:, P * t : P * (t + 1)],
-                    rhs=vw[a][:, BANK * half : BANK * (half + 1)].bitcast(FP8X4),
-                    rhs_scale=vs[a][:, BANK * half : BANK * (half + 1)],
-                    start=(a == 0),
-                    stop=(a == A_PASSES - 1),
-                )
+        def mul_h(s, a, bank, c0, c1):
+            if a == 0:
+                hacc[s, c0] = psum.tile([P, c1 - c0], F32, name="hacc", tag="bank%d" % bank)
+            nc.tensor.matmul_mx(
+                out=hacc[s, c0][:],
+                lhsT=w1c[s, a].bitcast(FP8X4),
+                lhsT_scale=w1s[s, a],
+                rhs=vw[a][:, c0:c1].bitcast(FP8X4),
+                rhs_scale=vs[a][:, c0:c1],
+                start=(a == 0),
+                stop=(a == A_PASSES - 1),
+            )
 
-        def empty_h(s, second_engine=nc.scalar):
-            h[s] = keep.tile([P, S], F32, name="h%d" % s)
-            for half in range(2):
-                copy_on(second_engine if half else nc.scalar, h[s][:, BANK * half : BANK * (half + 1)], hacc[s, half][:])
+        def mul_w1(holds):
+            for s in sorted(set(s for s, a in holds)):
+                for half in range(2):
+                    for a in range(A_PASSES):
+                        if (s, a) in holds:
+                            mul_h(s, a, 2 * (s % PACK) + half, BANK * half, BANK * (half + 1))
 
-        def make_h(s):
-            for a in range(A_PASSES):
-                mul_h(s, a)
-            empty_h(s)
+        def empty_h(s, offset=None):
+            if offset is None:
+                h[s] = keep.tile([P, S], F32, name="h", tag="h%d" % (s % PLAIN))
+            else:
+                h[s] = shared.tile([P, S], F32, name="h%d" % s, offset=offset, align_bytes=64)
+            for c0 in (0, BANK):
+                nc.scalar.copy(out=h[s][:, c0 : c0 + BANK], in_=hacc[s, c0][:])
 
         def pick_second(s, dst, j0, n):
             nc.vector.tensor_copy(out=dst, in_=h[s][:].indirect(pos2_sb[:, j0 // 16 : (j0 + n) // 16]))
@@ -208,8 +224,8 @@ def tile_list_clamped_landmark_differences_kernel(
         def clamp(engine, dst, src):
             engine.tensor_scalar(out=dst, in0=src, scalar1=1.0, scalar2=-1.0, op0=ALU.min, op1=ALU.max)
 
-        def weigh(b, t, dst, src):
-            nc.scalar.activation(out=dst, in_=src, func=ACT.Copy, scale=gain_sb[:, b, t : t + 1])
+        def weigh(scale, dst, src):
+            nc.scalar.activation(out=dst, in_=src, func=ACT.Copy, scale=scale)
 
         def weave(engine, dst, src, run):
             copy_on(
@@ -218,9 +234,9 @@ def tile_list_clamped_landmark_differences_kernel(
                 src.rearrange("p t (c i) -> p c t i", i=run),
             )
 
-        zc = {b: keep.tile([P, PAIRS], U32, name="zc%d" % b, align_bytes=64) for b in range(1, B_PASSES)}
+        zc = {}
         zs = [keep.tile([P, PAIRS], U8, name="zs%d" % b, align_bytes=64) for b in range(B_PASSES)]
-        zword = [keep.tile([P, PACK * PAIRS], BF16, name="zword%d" % b, align_bytes=64) for b in range(B_PASSES)]
+        zword = {}
 
         def quant_z(b, j0, n):
             nc.vector.quantize_mx(
@@ -236,10 +252,10 @@ def tile_list_clamped_landmark_differences_kernel(
                 for t in range(PACK):
                     if b == 0:
                         yacc[g, t] = psum.tile([P, PAIRS], F32, name="yacc", tag="bank%d" % (PACK * g + t))
-                    col = g * KP + t * P
+                    col = N * b + g * KP + t * P
                     nc.tensor.matmul_mx(
                         out=yacc[g, t][:],
-                        lhsT=w2w[b][:, 2 * col : 2 * (col + P)].bitcast(FP4X4),
+                        lhsT=w2w[:, 2 * col : 2 * (col + P)].bitcast(FP4X4),
                         lhsT_scale=w2s[:, 2 * g + t // 2, b, P * (t % 2) : P * (t % 2 + 1)],
                         rhs=zc[b][:].bitcast(FP8X4),
                         rhs_scale=zs[b][:],
@@ -247,67 +263,62 @@ def tile_list_clamped_landmark_differences_kernel(
                         stop=(b == B_PASSES - 1),
                     )
 
-        for t0 in (0, 2):
-            cast_w1(0, 0, t0, nc.scalar)
-        load_w1(1, 0, offset=AT_TABLE0 + 512)
-        load_w1(1, 1)
-        quant_w1(0, 0, 0, PACK)
-        vw.append(keep.tile([P, S], U32, name="vw1", tag="first_bf", align_bytes=64))
-        nc.vector.tensor_copy(out=vw[1][:], in_=tabw[1][:].bitcast(U32).indirect(offs_sb[:]))
-        load_w1(2, 0, offset=AT_TABLE1)
-        load_w1(2, 1, offset=AT_TABLE1 + RAW_BYTES)
-        for t0, share in ((0, HEAD_SHARE), (2, GAP_SHARE)):
-            cast_w1(0, 1, t0, nc.scalar, 0, share)
-            cast_w1(0, 1, t0, nc.vector, share, P)
-        quant_w1(0, 1, 0, 1)
-        quant_w1(0, 1, 1, 2)
-        quant_w1(0, 1, 2, 4)
-        w2w_last = keep.tile([P, 2 * N], U8, name="w2w_last", tag="bf010", align_bytes=64)
-        deal_w2_words(2, w2w_last[:], w2w_last_raw[:])
-        for s in range(PACK):
-            for a in range(A_PASSES):
-                mul_h(s, a)
+        ready_w1([(0, 0), (0, 1)])
+        first_cuts = ((0, 0, BANK), (1, BANK, BANK + HALF), (7, BANK + HALF, S))
+        for bank, c0, c1 in first_cuts:
+            mul_h(0, 0, bank, c0, c1)
+        for bank, c0, c1 in first_cuts:
+            nc.vector.tensor_copy(
+                out=vw[1][:, c0:c1], in_=tabw[1][:].bitcast(U32).indirect(offs_sb[:, c0 // 16 : c1 // 16])
+            )
+            mul_h(0, 1, bank, c0, c1)
+        h[0] = keep.tile([P, S], F32, name="h", tag="h0")
+        for bank, c0, c1 in first_cuts:
+            nc.vector.tensor_copy(out=h[0][:, c0:c1], in_=hacc[0, c0][:])
+        ready_w1([(1, 0), (1, 1)])
+        mul_w1([(1, 0), (1, 1)])
 
-        diff = [keep.tile([P, PACK, PAIRS], F32, name="diff%d" % b) for b in range(2)]
+        def eplane_at(b, t):
+            return AT_TABLE1 + RAW_BYTES * b + 4 * PAIRS * t
+
+        eplane = {
+            (b, t): shared.tile([P, PAIRS], F32, name="eplane%d%d" % (b, t), offset=eplane_at(b, t), align_bytes=64)
+            for b in range(2)
+            for t in range(PACK)
+        }
+        zplane = [keep.tile([P, PACK, PAIRS], BF16, name="zplane%d" % b, align_bytes=64) for b in range(2)]
         second = [keep.tile([P, PAIRS], F32, name="second", tag="second%d" % u, align_bytes=64) for u in range(2)]
-        first_planes = keep.tile([P, PACK, PAIRS], BF16, name="first_planes")
-        spare_and_planes = keep.tile([P, (1 + PACK) * PAIRS], BF16, name="spare_and_planes")
-        zplane = [first_planes[:], spare_and_planes[:, PAIRS:].rearrange("p (t j) -> p t j", t=PACK)]
+        runs = (slice(0, HALF), slice(HALF, PAIRS))
 
         def pick_slice(s):
-            b, t = divmod(s, PACK)
-            runs = (slice(0, HALF), slice(HALF, PAIRS))
-            for run in runs:
-                pick_second(s, second[s % 2][:, run], run.start, run.stop - run.start)
-            for run in runs:
-                pick_diff(s, diff[b][:, t, run], second[s % 2][:, run], run.start, run.stop - run.start)
-            clamp(nc.gpsimd, diff[b][:, t, :], diff[b][:, t, :])
-
-        def weigh_slice(b, t):
-            weigh(b, t, zplane[b][:, t, :], diff[b][:, t, :])
-
-        empty_h(0, nc.vector)
-        later = [(1, a, t0) for a in range(A_PASSES) for t0 in (0, 2)] + [(2, a, t0) for t0 in (0, 2) for a in range(A_PASSES)]
-        for s, (b, a, t0) in enumerate(later):
-            pick_slice(s)
-            cast_w1(b, a, t0, nc.scalar, P // 2 if s == PACK else 0, P)
-            quant_w1(b, a, t0, t0 + 2)
-            if s + 1 == PACK:
-                cast_w1(*later[PACK], nc.scalar, 0, P // 2)
-            if s + 1 < PACK:
-                empty_h(s + 1)
+            b, u = divmod(s, PACK)
+            if b == 0:
+                diff = keep.tile([P, PAIRS], F32, name="diff%d" % s)
             else:
-                make_h(s + 1)
+                diff = shared.tile([P, PAIRS], F32, name="diff%d" % s, offset=AT_RAW0 + 8 * PAIRS * u, align_bytes=64)
+            if s < 3:
+                at = AT_RAW0 + 4 * PAIRS * (A_PASSES * (s + 1) + 1)
+                picked = shared.tile([P, PAIRS], F32, name="picked%d" % s, offset=at, align_bytes=64)
+            else:
+                picked = second[s % 2]
+            for run in runs:
+                pick_second(s, picked[:, run], run.start, HALF)
+            for run in runs:
+                pick_diff(s, diff[:, run], picked[:, run], run.start, HALF)
+            clamp(nc.gpsimd, diff[:], diff[:])
+            for t in range(PACK):
+                nc.sync.dma_start(out=eplane[b, t][32 * u : 32 * (u + 1), :], in_=diff[t:P:PACK, :])
+
+        def weigh_plane(b, t):
+            weigh(gain_sb[:, b, t : t + 1], zplane[b][:, t, :], eplane[b, t][:])
 
         last = B_PASSES - 1
         wide = keep.tile([P, PACK, WIDE], F32, name="wide")
-        wide_plane = keep.tile([P, PACK, WIDE], BF16, name="wide_plane")
-
         late_second = keep.tile([P, PACK, HALF], F32, name="late_second")
 
         def pick_wide(t):
             s = PACK * last + t
-            spare = second[s % 2][:, 0:HALF] if t < PACK - 1 else spare_and_planes[:].bitcast(F32)[:, 0:HALF]
+            spare = second[s % 2][:, 0:HALF]
             first, third = wide[:, t, 0:HALF], wide[:, t, HALF:WIDE]
             pick_second(s, spare, 0, HALF)
             pick_second(s, late_second[:, t, :], HALF, HALF)
@@ -319,46 +330,60 @@ def tile_list_clamped_landmark_differences_kernel(
                 clamp(nc.vector, first, first)
                 clamp(nc.vector, third, third)
 
+        steps = [[(2, 0), (2, 1)], [(3, 0), (3, 1), (4, 0)]]
+        steps.extend([[(s, 1), (s + 1, 0)] for s in range(4, 7)])
+        steps.extend([[(7, 1), (8, 0), (9, 0)], [(8, 1), (9, 1)], [(10, 0), (11, 0)], [(10, 1), (11, 1)]])
+        for s in range(PLAIN):
+            pick_slice(s)
+            ready_w1(steps[s], (s, 0) if s in (1, 2) else None)
+            empty_h(s + 1)
+            mul_w1(steps[s])
         pick_wide(0)
-        make_h(9)
-        pick_wide(1)
-        for t in range(PACK):
-            weigh_slice(0, t)
-        for t in range(2):
-            weigh_slice(1, t)
-        make_h(10)
-        pick_wide(2)
-        weave(nc.scalar, zword[0][:], zplane[0], 4)
-        zc[0] = keep.tile([P, PAIRS], U32, name="zc0", tag="second0", align_bytes=64)
-        quant_z(0, 0, PAIRS)
-        make_h(11)
+        ready_w1(steps[PLAIN])
+        empty_h(9)
+        mul_w1(steps[PLAIN])
         for b in range(B_PASSES):
             for r in range(4):
                 nc.sync.dma_start(
                     out=w2s[r:P:32, :, b, :].bitcast(I32),
                     in_=w2s_dealt[32 * b + 2 * r : 32 * (b + 1) : 8, :].rearrange("p (u c) -> p u c", c=2 * P).bitcast(I32),
                 )
+        pick_wide(1)
+        for t in range(PACK):
+            weigh_plane(0, t)
+        empty_h(10, eplane_at(0, 0))
+        zword[0] = keep.tile([P, PACK * PAIRS], BF16, name="zword0", align_bytes=64)
+        weave(nc.vector, zword[0][:, 0 : PACK * Z_SHARE], zplane[0][:, :, 0:Z_SHARE], 1)
+        weave(nc.scalar, zword[0][:, PACK * Z_SHARE :], zplane[0][:, :, Z_SHARE:], 4)
+        empty_h(11, eplane_at(0, 2))
+        pick_wide(2)
+        zc[0] = keep.tile([P, PAIRS], U32, name="zc0", align_bytes=64)
+        quant_z(0, 0, PAIRS)
         mul_z(0)
+        for t in range(PACK):
+            weigh_plane(1, t)
+        zword[1] = keep.tile([P, PACK * PAIRS], BF16, name="zword1", align_bytes=64)
+        weave(nc.scalar, zword[1][:], zplane[1][:], 4)
         pick_wide(3)
-        for t in range(2, PACK):
-            weigh_slice(1, t)
-        weave(nc.scalar, zword[1][:], zplane[1], 4)
+        zword[last] = keep.tile([P, PACK * PAIRS], BF16, name="zword2", align_bytes=64)
+        zc[last] = keep.tile([P, PAIRS], U32, name="zc2", align_bytes=64)
+        wide_plane = shared.tile([P, PACK, WIDE], BF16, name="wide_plane", offset=eplane_at(1, 1), align_bytes=64)
         for t in range(PACK):
-            weigh(last, t, wide_plane[:, t, :], wide[:, t, :])
-        for j0, j1 in ((0, HALF), (HALF, WIDE)):
-            weave(nc.scalar, zword[last][:, PACK * j0 : PACK * j1], wide_plane[:, :, j0:j1], 4)
+            weigh(gain_sb[:, last, t : t + 1], wide_plane[:, t, :], wide[:, t, :])
+        weave(nc.scalar, zword[last][:, 0 : PACK * HALF], wide_plane[:, :, 0:HALF], 4)
 
-        late = spare_and_planes[:].bitcast(F32)[:, 0:PAIRS].rearrange("p (t j) -> p t j", t=PACK)
+        late = keep.tile([P, PACK, PIECE], F32, name="late", tag="second1", align_bytes=64)
         for t in range(PACK):
-            if t == 2:
-                quant_z(1, 0, PAIRS)
-                mul_z(1)
             pick_diff(PACK * last + t, late[:, t, :], late_second[:, t, PIECE:HALF], WIDE, PIECE)
-        woven = second[1][:].rearrange("p (j t) -> p j t", t=PACK)
+        zc[1] = keep.tile([P, PAIRS], U32, name="zc1", align_bytes=64)
+        quant_z(1, 0, PAIRS)
+        mul_z(1)
+        woven_tile = keep.tile([P, PACK * PIECE], F32, name="woven", tag="zplane1", align_bytes=64)
+        woven = woven_tile[:].rearrange("p (j t) -> p j t", t=PACK)
         late_words = zword[last][:, PACK * WIDE :].rearrange("p (j t) -> p j t", t=PACK)
         late_halves = (slice(0, PIECE // 2), slice(PIECE // 2, PIECE))
         for run in late_halves:
-            clamp(nc.vector, woven[:, run], late.rearrange("p t j -> p j t")[:, run])
+            clamp(nc.vector, woven[:, run], late[:].rearrange("p t j -> p j t")[:, run])
         for run in late_halves:
             nc.vector.tensor_tensor(
                 out=late_words[:, run],
@@ -366,16 +391,17 @@ def tile_list_clamped_landmark_differences_kernel(
                 in1=gain_sb[:, last, :].unsqueeze(1).to_broadcast([P, PIECE // 2, PACK]),
                 op=ALU.mult,
             )
+        weave(nc.vector, zword[last][:, PACK * HALF : PACK * WIDE], wide_plane[:, :, HALF:WIDE], 1)
         quant_z(last, 0, HALF)
         quant_z(last, HALF, HALF)
         mul_z(last)
 
         y = [
-            shared.tile([P, PACK, PAIRS], F32, name="y%d" % g, offset=AT_TABLE1 + RAW_BYTES * g, align_bytes=64)
+            shared.tile([P, PACK, PAIRS], F32, name="y%d" % g, offset=AT_TABLE0 + RAW_BYTES * g, align_bytes=64)
             for g in range(GROUPS)
         ]
         yword = [
-            shared.tile([P, PACK * PAIRS], BF16, name="yword%d" % g, offset=AT_TABLE0 + 512 + 2 * PACK * PAIRS * g, align_bytes=64)
+            shared.tile([P, PACK * PAIRS], BF16, name="yword%d" % g, offset=AT_RAW1 + 2 * PACK * PAIRS * g, align_bytes=64)
             for g in range(GROUPS)
         ]
         yc = [keep.tile([P, PAIRS], U32, name="yc%d" % g, align_bytes=64) for g in range(GROUPS)]

@@ -27,16 +27,16 @@ HALF = PAIRS // 2
 PIECE = 128
 WIDE = 384
 Y_SHARE = 304
-Z_SHARE = 352
 PLAIN = 2 * PACK
 RAW_BYTES = 4 * PACK * KP
 AT_TABLE0 = 0
 AT_TABLE1 = 4 * T
 AT_RAW0 = 8 * T
-AT_RAW1 = AT_RAW0 + 2 * RAW_BYTES
-AT_W2 = AT_RAW1 + 2 * RAW_BYTES
+AT_W2 = AT_RAW0 + 4 * RAW_BYTES
 AT_W2_SCALES = AT_W2 + B_PASSES * 2 * N
 AT_SCALES = AT_W2_SCALES + 64 - T
+AT_PLANES = AT_W2_SCALES + N
+ROW = 4 * PAIRS
 
 
 def tile_list_clamped_landmark_differences_kernel(
@@ -79,9 +79,12 @@ def tile_list_clamped_landmark_differences_kernel(
                 w1_raw[c // P, a] = raw[:, :, c - c0 : c - c0 + P]
             return raw
 
-        def load_plain(s0, s1, base):
+        def raw_at(s, a):
+            return AT_RAW0 + ROW * (A_PASSES * s + a)
+
+        def load_plain(s):
             for a in range(A_PASSES):
-                load_w1(P * s0, P * s1, a, base + 4 * PACK * P * (A_PASSES * (s0 % PACK) + a * (s1 - s0)))
+                load_w1(P * s, P * (s + 1), a, raw_at(s, a))
 
         def load_table(a, offset):
             tabw[a] = shared.tile([P, T], I32, name="tabw%d" % a, offset=offset, align_bytes=64)
@@ -107,16 +110,14 @@ def tile_list_clamped_landmark_differences_kernel(
                 )
 
         move_table_scales(1)
-        load_plain(0, 1, AT_RAW0)
+        load_plain(0)
         load_table(1, AT_TABLE1)
         move_table_scales(0)
-        load_plain(1, 2, AT_RAW0)
+        load_plain(1)
         nc.sync.dma_start(pos2_sb[:], pos2)
         nc.sync.dma_start(pos1_sb[:], pos1)
-        load_plain(2, 3, AT_RAW0)
-        load_plain(3, 4, AT_RAW0)
-        load_plain(4, 6, AT_RAW1)
-        load_plain(6, 8, AT_RAW1)
+        for s in range(2, PLAIN):
+            load_plain(s)
         dealt_raw = [load_w1(2 * KP, 3 * KP, a, AT_TABLE0 + RAW_BYTES * a) for a in range(A_PASSES)]
         nc.sync.dma_start(out=gain_sb[:], in_=gain.rearrange("(b p t) -> p b t", b=B_PASSES, t=PACK))
         nc.sync.dma_start(out=bias_sb[:], in_=bias.rearrange("(g p t) -> p g t", g=GROUPS, t=PACK))
@@ -164,9 +165,8 @@ def tile_list_clamped_landmark_differences_kernel(
 
         quantised = []
 
-        def ready_w1(holds, behind=None):
-            tag = "bf%d" % (len(quantised) % 3) if behind is None else "w1c%d_%d" % behind
-            src = keep.tile([P, KP * len(holds)], BF16, name="w1_bf", tag=tag, align_bytes=64)
+        def ready_w1(holds):
+            src = keep.tile([P, KP * len(holds)], BF16, name="w1_bf", tag="bf%d" % (len(quantised) % 4), align_bytes=64)
             codes = keep.tile([P, P * len(holds)], U32, name="w1c%d_%d" % holds[0], align_bytes=64)
             scales = keep.tile([P, P * len(holds)], U8, name="w1s%d_%d" % holds[0], align_bytes=64)
             for n, (s, a) in enumerate(holds):
@@ -202,13 +202,16 @@ def tile_list_clamped_landmark_differences_kernel(
                         if (s, a) in holds:
                             mul_h(s, a, 2 * (s % PACK) + half, BANK * half, BANK * (half + 1))
 
-        def empty_h(s, offset=None):
-            if offset is None:
-                h[s] = keep.tile([P, S], F32, name="h", tag="h%d" % (s % PLAIN))
-            else:
-                h[s] = shared.tile([P, S], F32, name="h%d" % s, offset=offset, align_bytes=64)
+        def empty_bank(s, c0, engine):
+            if c0 == 0 and s < PLAIN:
+                h[s] = keep.tile([P, S], F32, name="h%d" % s)
+            elif c0 == 0:
+                h[s] = shared.tile([P, S], F32, name="h%d" % s, offset=AT_TABLE1 + 4 * S * (s - PLAIN), align_bytes=64)
+            copy_on(engine, h[s][:, c0 : c0 + BANK], hacc[s, c0][:])
+
+        def empty_h(s):
             for c0 in (0, BANK):
-                nc.scalar.copy(out=h[s][:, c0 : c0 + BANK], in_=hacc[s, c0][:])
+                empty_bank(s, c0, nc.scalar)
 
         def pick_second(s, dst, j0, n):
             nc.vector.tensor_copy(out=dst, in_=h[s][:].indirect(pos2_sb[:, j0 // 16 : (j0 + n) // 16]))
@@ -272,14 +275,18 @@ def tile_list_clamped_landmark_differences_kernel(
                 out=vw[1][:, c0:c1], in_=tabw[1][:].bitcast(U32).indirect(offs_sb[:, c0 // 16 : c1 // 16])
             )
             mul_h(0, 1, bank, c0, c1)
-        h[0] = keep.tile([P, S], F32, name="h", tag="h0")
+        ready_w1([(1, 0)])
+        mul_w1([(1, 0)])
+        h[0] = shared.tile([P, S], F32, name="h0", offset=raw_at(0, 1), align_bytes=64)
         for bank, c0, c1 in first_cuts:
             nc.vector.tensor_copy(out=h[0][:, c0:c1], in_=hacc[0, c0][:])
-        ready_w1([(1, 0), (1, 1)])
-        mul_w1([(1, 0), (1, 1)])
+        ready_w1([(1, 1)])
+        mul_w1([(1, 1)])
 
         def eplane_at(b, t):
-            return AT_TABLE1 + RAW_BYTES * b + 4 * PAIRS * t
+            if b:
+                return AT_PLANES + ROW * t
+            return AT_TABLE1 + ROW * (t + 1) if t < PACK - 1 else AT_TABLE1 + 3 * (4 * S) - ROW // 2
 
         eplane = {
             (b, t): shared.tile([P, PAIRS], F32, name="eplane%d%d" % (b, t), offset=eplane_at(b, t), align_bytes=64)
@@ -292,17 +299,17 @@ def tile_list_clamped_landmark_differences_kernel(
 
         def pick_slice(s):
             b, u = divmod(s, PACK)
-            if b == 0:
-                diff = keep.tile([P, PAIRS], F32, name="diff%d" % s)
-            else:
-                diff = shared.tile([P, PAIRS], F32, name="diff%d" % s, offset=AT_RAW0 + 8 * PAIRS * u, align_bytes=64)
-            if s < 3:
-                at = AT_RAW0 + 4 * PAIRS * (A_PASSES * (s + 1) + 1)
-                picked = shared.tile([P, PAIRS], F32, name="picked%d" % s, offset=at, align_bytes=64)
+            if s + 2 < PLAIN:
+                picked = shared.tile([P, PAIRS], F32, name="picked%d" % s, offset=raw_at(s + 2 if s else 1, 1), align_bytes=64)
             else:
                 picked = second[s % 2]
             for run in runs:
                 pick_second(s, picked[:, run], run.start, HALF)
+            if s == 0:
+                ready_w1([(2, 0), (2, 1)])
+                mul_w1([(2, 0), (2, 1)])
+                empty_bank(1, 0, nc.vector)
+            diff = shared.tile([P, PAIRS], F32, name="diff%d" % s, offset=raw_at(s, 0) if s else raw_at(2, 1), align_bytes=64)
             for run in runs:
                 pick_diff(s, diff[:, run], picked[:, run], run.start, HALF)
             clamp(nc.gpsimd, diff[:], diff[:])
@@ -330,32 +337,35 @@ def tile_list_clamped_landmark_differences_kernel(
                 clamp(nc.vector, first, first)
                 clamp(nc.vector, third, third)
 
-        steps = [[(2, 0), (2, 1)], [(3, 0), (3, 1), (4, 0)]]
-        steps.extend([[(s, 1), (s + 1, 0)] for s in range(4, 7)])
-        steps.extend([[(7, 1), (8, 0), (9, 0)], [(8, 1), (9, 1)], [(10, 0), (11, 0)], [(10, 1), (11, 1)]])
+        steps = [[(s, 0), (s, 1)] for s in range(3, PLAIN)]
+        steps[-1].extend([(PLAIN, 0), (PLAIN + 1, 0)])
+        steps.extend([[(s, a), (s + 1, a)] for s, a in ((PLAIN, 1), (PLAIN + 2, 0), (PLAIN + 2, 1))])
         for s in range(PLAIN):
             pick_slice(s)
-            ready_w1(steps[s], (s, 0) if s in (1, 2) else None)
-            empty_h(s + 1)
+            ready_w1(steps[s])
+            if s == PLAIN - 1:
+                weigh_plane(0, 0)
+                weigh_plane(0, 1)
+            if s:
+                empty_h(s + 1)
+            else:
+                empty_bank(1, BANK, nc.scalar)
             mul_w1(steps[s])
-        pick_wide(0)
-        ready_w1(steps[PLAIN])
-        empty_h(9)
-        mul_w1(steps[PLAIN])
         for b in range(B_PASSES):
             for r in range(4):
                 nc.sync.dma_start(
                     out=w2s[r:P:32, :, b, :].bitcast(I32),
                     in_=w2s_dealt[32 * b + 2 * r : 32 * (b + 1) : 8, :].rearrange("p (u c) -> p u c", c=2 * P).bitcast(I32),
                 )
+        pick_wide(0)
+        weigh_plane(0, 2)
+        weigh_plane(0, 3)
+        empty_h(9)
         pick_wide(1)
-        for t in range(PACK):
-            weigh_plane(0, t)
-        empty_h(10, eplane_at(0, 0))
+        empty_h(10)
         zword[0] = keep.tile([P, PACK * PAIRS], BF16, name="zword0", align_bytes=64)
-        weave(nc.vector, zword[0][:, 0 : PACK * Z_SHARE], zplane[0][:, :, 0:Z_SHARE], 1)
-        weave(nc.scalar, zword[0][:, PACK * Z_SHARE :], zplane[0][:, :, Z_SHARE:], 4)
-        empty_h(11, eplane_at(0, 2))
+        weave(nc.scalar, zword[0][:], zplane[0][:], 4)
+        empty_h(11)
         pick_wide(2)
         zc[0] = keep.tile([P, PAIRS], U32, name="zc0", align_bytes=64)
         quant_z(0, 0, PAIRS)
@@ -401,7 +411,7 @@ def tile_list_clamped_landmark_differences_kernel(
             for g in range(GROUPS)
         ]
         yword = [
-            shared.tile([P, PACK * PAIRS], BF16, name="yword%d" % g, offset=AT_RAW1 + 2 * PACK * PAIRS * g, align_bytes=64)
+            shared.tile([P, PACK * PAIRS], BF16, name="yword%d" % g, offset=AT_RAW0 + 2 * PACK * PAIRS * g, align_bytes=64)
             for g in range(GROUPS)
         ]
         yc = [keep.tile([P, PAIRS], U32, name="yc%d" % g, align_bytes=64) for g in range(GROUPS)]

@@ -92,6 +92,8 @@ def tile_list_clamped_landmark_differences_kernel(
 
         nc.sync.dma_start(offs_sb[:], offs)
         nc.sync.dma_start(out=tabs[0:32, :].bitcast(I32), in_=tab_scales.rearrange("a q t -> (a q) t").bitcast(I32))
+        nc.sync.dma_start(pos2_sb[:], pos2)
+        nc.sync.dma_start(pos1_sb[:], pos1)
         nc.sync.dma_start(
             out=w2w_raw[:].bitcast(I32).rearrange("p (b c) -> p b c", b=B_PASSES),
             in_=w2_words.bitcast(I32).rearrange("b p c -> p b c"),
@@ -114,8 +116,6 @@ def tile_list_clamped_landmark_differences_kernel(
         load_table(1, AT_TABLE1)
         move_table_scales(0)
         load_plain(1)
-        nc.sync.dma_start(pos2_sb[:], pos2)
-        nc.sync.dma_start(pos1_sb[:], pos1)
         for s in range(2, PLAIN):
             load_plain(s)
         dealt_raw = [load_w1(2 * KP, 3 * KP, a, AT_TABLE0 + RAW_BYTES * a) for a in range(A_PASSES)]
@@ -299,7 +299,7 @@ def tile_list_clamped_landmark_differences_kernel(
 
         def pick_slice(s):
             b, u = divmod(s, PACK)
-            if s + 2 < PLAIN:
+            if s < 3:
                 picked = shared.tile([P, PAIRS], F32, name="picked%d" % s, offset=raw_at(s + 2 if s else 1, 1), align_bytes=64)
             else:
                 picked = second[s % 2]
@@ -309,7 +309,10 @@ def tile_list_clamped_landmark_differences_kernel(
                 ready_w1([(2, 0), (2, 1)])
                 mul_w1([(2, 0), (2, 1)])
                 empty_bank(1, 0, nc.vector)
-            diff = shared.tile([P, PAIRS], F32, name="diff%d" % s, offset=raw_at(s, 0) if s else raw_at(2, 1), align_bytes=64)
+            if s == 0:
+                diff = shared.tile([P, PAIRS], F32, name="diff0", offset=raw_at(2, 1), align_bytes=64)
+            else:
+                diff = keep.tile([P, PAIRS], F32, name="diff%d" % s)
             for run in runs:
                 pick_diff(s, diff[:, run], picked[:, run], run.start, HALF)
             clamp(nc.gpsimd, diff[:], diff[:])

@@ -250,21 +250,22 @@ def tile_list_clamped_landmark_differences_kernel(
 
         yacc = {}
 
-        def mul_z(b):
-            for g in range(GROUPS):
-                for t in range(PACK):
-                    if b == 0:
-                        yacc[g, t] = psum.tile([P, PAIRS], F32, name="yacc", tag="bank%d" % (PACK * g + t))
-                    col = N * b + g * KP + t * P
-                    nc.tensor.matmul_mx(
-                        out=yacc[g, t][:],
-                        lhsT=w2w[:, 2 * col : 2 * (col + P)].bitcast(FP4X4),
-                        lhsT_scale=w2s[:, 2 * g + t // 2, b, P * (t % 2) : P * (t % 2 + 1)],
-                        rhs=zc[b][:].bitcast(FP8X4),
-                        rhs_scale=zs[b][:],
-                        start=(b == 0),
-                        stop=(b == B_PASSES - 1),
-                    )
+        tiles = [(g, t) for g in range(GROUPS) for t in range(PACK)]
+
+        def mul_z(b, some, start=False, stop=False):
+            for g, t in some:
+                if start:
+                    yacc[g, t] = psum.tile([P, PAIRS], F32, name="yacc", tag="bank%d" % (PACK * g + t))
+                col = N * b + g * KP + t * P
+                nc.tensor.matmul_mx(
+                    out=yacc[g, t][:],
+                    lhsT=w2w[:, 2 * col : 2 * (col + P)].bitcast(FP4X4),
+                    lhsT_scale=w2s[:, 2 * g + t // 2, b, P * (t % 2) : P * (t % 2 + 1)],
+                    rhs=zc[b][:].bitcast(FP8X4),
+                    rhs_scale=zs[b][:],
+                    start=start,
+                    stop=stop,
+                )
 
         ready_w1([(0, 0), (0, 1)])
         first_cuts = ((0, 0, BANK), (1, BANK, BANK + HALF), (7, BANK + HALF, S))
@@ -278,9 +279,10 @@ def tile_list_clamped_landmark_differences_kernel(
         ready_w1([(1, 0)])
         mul_w1([(1, 0)])
         h[0] = shared.tile([P, S], F32, name="h0", offset=raw_at(0, 1), align_bytes=64)
-        for bank, c0, c1 in first_cuts:
+        for bank, c0, c1 in first_cuts[1:]:
             nc.vector.tensor_copy(out=h[0][:, c0:c1], in_=hacc[0, c0][:])
         ready_w1([(1, 1)])
+        nc.scalar.copy(out=h[0][:, 0:BANK], in_=hacc[0, 0][:])
         mul_w1([(1, 1)])
 
         def eplane_at(b, t):
@@ -308,7 +310,6 @@ def tile_list_clamped_landmark_differences_kernel(
             if s == 0:
                 ready_w1([(2, 0), (2, 1)])
                 mul_w1([(2, 0), (2, 1)])
-                empty_bank(1, 0, nc.vector)
             if s == 0:
                 diff = shared.tile([P, PAIRS], F32, name="diff0", offset=raw_at(2, 1), align_bytes=64)
             else:
@@ -349,10 +350,7 @@ def tile_list_clamped_landmark_differences_kernel(
             if s == PLAIN - 1:
                 weigh_plane(0, 0)
                 weigh_plane(0, 1)
-            if s:
-                empty_h(s + 1)
-            else:
-                empty_bank(1, BANK, nc.scalar)
+            empty_h(s + 1)
             mul_w1(steps[s])
         for b in range(B_PASSES):
             for r in range(4):
@@ -372,7 +370,7 @@ def tile_list_clamped_landmark_differences_kernel(
         pick_wide(2)
         zc[0] = keep.tile([P, PAIRS], U32, name="zc0", align_bytes=64)
         quant_z(0, 0, PAIRS)
-        mul_z(0)
+        mul_z(0, tiles, start=True)
         for t in range(PACK):
             weigh_plane(1, t)
         zword[1] = keep.tile([P, PACK * PAIRS], BF16, name="zword1", align_bytes=64)
@@ -390,7 +388,7 @@ def tile_list_clamped_landmark_differences_kernel(
             pick_diff(PACK * last + t, late[:, t, :], late_second[:, t, PIECE:HALF], WIDE, PIECE)
         zc[1] = keep.tile([P, PAIRS], U32, name="zc1", align_bytes=64)
         quant_z(1, 0, PAIRS)
-        mul_z(1)
+        mul_z(1, tiles[:-1])
         woven_tile = keep.tile([P, PACK * PIECE], F32, name="woven", tag="zplane1", align_bytes=64)
         woven = woven_tile[:].rearrange("p (j t) -> p j t", t=PACK)
         late_words = zword[last][:, PACK * WIDE :].rearrange("p (j t) -> p j t", t=PACK)
@@ -407,7 +405,9 @@ def tile_list_clamped_landmark_differences_kernel(
         weave(nc.vector, zword[last][:, PACK * HALF : PACK * WIDE], wide_plane[:, :, HALF:WIDE], 1)
         quant_z(last, 0, HALF)
         quant_z(last, HALF, HALF)
-        mul_z(last)
+        mul_z(last, tiles[:-1], stop=True)
+        mul_z(last, tiles[-1:])
+        mul_z(1, tiles[-1:], stop=True)
 
         y = [
             shared.tile([P, PACK, PAIRS], F32, name="y%d" % g, offset=AT_TABLE0 + RAW_BYTES * g, align_bytes=64)
@@ -419,20 +419,20 @@ def tile_list_clamped_landmark_differences_kernel(
         ]
         yc = [keep.tile([P, PAIRS], U32, name="yc%d" % g, align_bytes=64) for g in range(GROUPS)]
 
-        def add_bias(g, t, engine):
+        def add_bias(g, t, engine, run=slice(0, PAIRS)):
             if engine is nc.vector:
                 nc.vector.tensor_scalar(
-                    out=y[g][:, t, :], in0=yacc[g, t][:], scalar1=bias_sb[:, g, t : t + 1], scalar2=None, op0=ALU.add
+                    out=y[g][:, t, run], in0=yacc[g, t][:, run], scalar1=bias_sb[:, g, t : t + 1], scalar2=None, op0=ALU.add
                 )
             else:
                 nc.scalar.activation(
-                    out=y[g][:, t, :], in_=yacc[g, t][:], func=ACT.Identity, bias=bias_sb[:, g, t : t + 1]
+                    out=y[g][:, t, run], in_=yacc[g, t][:, run], func=ACT.Identity, bias=bias_sb[:, g, t : t + 1]
                 )
 
-        def store_y(g, t0, t1):
+        def store_y(g, t0, t1, run=slice(0, PAIRS)):
             nc.sync.dma_start(
-                out=out_0[KP * g : KP * (g + 1), :].rearrange("(p t) j -> p t j", t=PACK)[:, t0:t1, :],
-                in_=y[g][:, t0:t1, :],
+                out=out_0[KP * g : KP * (g + 1), :].rearrange("(p t) j -> p t j", t=PACK)[:, t0:t1, run],
+                in_=y[g][:, t0:t1, run],
             )
 
         def weave_y(engine, g, j0, j1):
@@ -450,7 +450,10 @@ def tile_list_clamped_landmark_differences_kernel(
                 out=out_1[g].rearrange("p m t -> p (m t)").bitcast(I32)[:, j0:j1], in_=yc[g][:, j0:j1].bitcast(I32)
             )
 
-        for t in range(PACK):
+        for run in runs:
+            add_bias(0, 0, nc.vector, run)
+            store_y(0, 0, 1, run)
+        for t in range(1, PACK):
             add_bias(0, t, nc.scalar if t % 2 else nc.vector)
             if t != 2:
                 store_y(0, t if t < 2 else 2, t + 1)

@@ -252,17 +252,17 @@ def tile_list_clamped_landmark_differences_kernel(
 
         tiles = [(g, t) for g in range(GROUPS) for t in range(PACK)]
 
-        def mul_z(b, some, start=False, stop=False):
+        def mul_z(b, some, start=False, stop=False, run=slice(0, PAIRS)):
             for g, t in some:
                 if start:
                     yacc[g, t] = psum.tile([P, PAIRS], F32, name="yacc", tag="bank%d" % (PACK * g + t))
                 col = N * b + g * KP + t * P
                 nc.tensor.matmul_mx(
-                    out=yacc[g, t][:],
+                    out=yacc[g, t][:, run],
                     lhsT=w2w[:, 2 * col : 2 * (col + P)].bitcast(FP4X4),
                     lhsT_scale=w2s[:, 2 * g + t // 2, b, P * (t % 2) : P * (t % 2 + 1)],
-                    rhs=zc[b][:].bitcast(FP8X4),
-                    rhs_scale=zs[b][:],
+                    rhs=zc[b][:, run].bitcast(FP8X4),
+                    rhs_scale=zs[b][:, run],
                     start=start,
                     stop=stop,
                 )
@@ -381,7 +381,8 @@ def tile_list_clamped_landmark_differences_kernel(
         wide_plane = shared.tile([P, PACK, WIDE], BF16, name="wide_plane", offset=eplane_at(1, 1), align_bytes=64)
         for t in range(PACK):
             weigh(gain_sb[:, last, t : t + 1], wide_plane[:, t, :], wide[:, t, :])
-        weave(nc.scalar, zword[last][:, 0 : PACK * HALF], wide_plane[:, :, 0:HALF], 4)
+        for j0, j1 in ((0, HALF), (HALF, WIDE)):
+            weave(nc.scalar, zword[last][:, PACK * j0 : PACK * j1], wide_plane[:, :, j0:j1], 4)
 
         late = keep.tile([P, PACK, PIECE], F32, name="late", tag="second1", align_bytes=64)
         for t in range(PACK):
@@ -402,10 +403,11 @@ def tile_list_clamped_landmark_differences_kernel(
                 in1=gain_sb[:, last, :].unsqueeze(1).to_broadcast([P, PIECE // 2, PACK]),
                 op=ALU.mult,
             )
-        weave(nc.vector, zword[last][:, PACK * HALF : PACK * WIDE], wide_plane[:, :, HALF:WIDE], 1)
         quant_z(last, 0, HALF)
         quant_z(last, HALF, HALF)
-        mul_z(last, tiles[:-1], stop=True)
+        mul_z(last, tiles[:1], run=runs[0])
+        mul_z(last, tiles[:1], stop=True, run=runs[1])
+        mul_z(last, tiles[1:-1], stop=True)
         mul_z(last, tiles[-1:])
         mul_z(1, tiles[-1:], stop=True)
 

@@ -153,8 +153,8 @@ def tile_list_clamped_landmark_differences_kernel(
 
         def cast_plain(s, a, dst):
             nc.scalar.copy(
-                out=dst.rearrange("p (c i j) -> p c j i", i=2, j=PACK),
-                in_=w1_raw[s, a].rearrange("p j (c i) -> p c j i", i=2),
+                out=dst.rearrange("p (c i j) -> p c j i", i=4, j=PACK),
+                in_=w1_raw[s, a].rearrange("p j (c i) -> p c j i", i=4),
             )
 
         def cast_dealt(s, a, dst):

from contextlib import ExitStack

import concourse.mybir as mybir

K, T, S, PAIRS, H, N = 1024, 4096, 1024, 512, 1536, 1024
FLOPS = 2 * K * H * S + 2 * H * N * PAIRS

F32 = mybir.dt.float32
BF16 = mybir.dt.bfloat16
I32 = mybir.dt.int32
U32 = mybir.dt.uint32
U16 = mybir.dt.uint16
U8 = mybir.dt.uint8
FP8X4 = mybir.dt.float8_e4m3fn_x4
FP4X4 = mybir.dt.float4_e2m1fn_x4
ALU = mybir.AluOpType
ACT = mybir.ActivationFunctionType

P = 128
PACK = 4
KP = P * PACK
A_PASSES = K // KP
B_PASSES = H // KP
GROUPS = N // KP
BANK = 512
HALF = PAIRS // 2
PIECE = 128
WIDE = 384
Y_SHARE = 304
PLAIN = 2 * PACK
RAW_BYTES = 4 * PACK * KP
AT_TABLE0 = 0
AT_TABLE1 = 4 * T
AT_RAW0 = 8 * T
AT_W2 = AT_RAW0 + 4 * RAW_BYTES
AT_W2_SCALES = AT_W2 + B_PASSES * 2 * N
AT_SCALES = AT_W2_SCALES + 64 - T
AT_PLANES = AT_W2_SCALES + N
ROW = 4 * PAIRS


def tile_list_clamped_landmark_differences_kernel(
    tc, tab_words, tab_scales, offs, pos1, pos2, w1, gain, w2_words, w2_scales, bias, out_0, out_1, out_2
):
    nc = tc.nc
    with ExitStack() as ctx:
        keep = ctx.enter_context(tc.tile_pool(name="keep", bufs=1))
        shared = ctx.enter_context(tc.tile_pool(name="shared", bufs=1))
        psum = ctx.enter_context(tc.psum_pool(name="psum", bufs=1))

        offs_sb = keep.tile([P, S // 16], U16, name="offs_sb")
        pos1_sb = keep.tile([P, PAIRS // 16], U16, name="pos1_sb")
        pos2_sb = keep.tile([P, PAIRS // 16], U16, name="pos2_sb")
        tabs = shared.tile([P, T], U8, name="tabs", offset=AT_SCALES, align_bytes=64)
        w2w_raw = keep.tile([P, B_PASSES * 2 * N], U8, name="w2w_raw", align_bytes=64)
        w2s_raw = keep.tile([P, N], U8, name="w2s_raw")
        planes = keep.tile([P, B_PASSES * N], U8, name="planes", align_bytes=64)
        w2s = planes[:].rearrange("p (u b c) -> p u b c", b=B_PASSES, c=2 * P)
        first_plane = keep.tile([P, S], U8, name="first_plane", align_bytes=64)
        vs = [first_plane[:], planes[:, 0:S]]
        ys = keep.tile([P, GROUPS * PAIRS], U8, name="ys", align_bytes=64)
        gain_sb = keep.tile([P, B_PASSES, PACK], F32, name="gain_sb")
        bias_sb = keep.tile([P, GROUPS, PACK], F32, name="bias_sb")

        nc.vector.memset(w2s_raw[:].bitcast(I32), 0)
        nc.vector.memset(tabs[32:64, :].bitcast(I32), 0)
        nc.vector.memset(tabs[64:P, :].bitcast(I32), 0)
        nc.vector.memset(first_plane[:].bitcast(I32), 0)
        nc.vector.memset(planes[:].bitcast(I32), 0)

        w1_raw = {}
        tabw = {}

        def load_w1(c0, c1, a, offset):
            raw = shared.tile([P, PACK, c1 - c0], F32, name="w1_raw%d_%d" % (c0, a), offset=offset, align_bytes=64)
            rows = w1[KP * a : KP * (a + 1), c0:c1].rearrange("(p j) c -> p j c", j=PACK)
            nc.sync.dma_start(out=raw[:], in_=rows)
            for c in range(c0, c1, P):
                w1_raw[c // P, a] = raw[:, :, c - c0 : c - c0 + P]
            return raw

        def raw_at(s, a):
            return AT_RAW0 + ROW * (A_PASSES * s + a)

        def load_plain(s):
            for a in range(A_PASSES):
                load_w1(P * s, P * (s + 1), a, raw_at(s, a))

        def load_table(a, offset):
            tabw[a] = shared.tile([P, T], I32, name="tabw%d" % a, offset=offset, align_bytes=64)
            nc.sync.dma_start(out=tabw[a][:], in_=tab_words[a].rearrange("p t i -> p (t i)").bitcast(I32))

        nc.sync.dma_start(offs_sb[:], offs)
        nc.sync.dma_start(out=tabs[0:32, :].bitcast(I32), in_=tab_scales.rearrange("a q t -> (a q) t").bitcast(I32))
        nc.sync.dma_start(pos2_sb[:], pos2)
        nc.sync.dma_start(pos1_sb[:], pos1)
        nc.sync.dma_start(
            out=w2w_raw[:].bitcast(I32).rearrange("p (b c) -> p b c", b=B_PASSES),
            in_=w2_words.bitcast(I32).rearrange("b p c -> p b c"),
        )
        nc.sync.dma_start(out=w2s_raw[0:96:2, :].bitcast(I32), in_=w2_scales.rearrange("b q c -> (b q) c").bitcast(I32))
        load_table(0, AT_TABLE0)

        vs_picked = keep.tile([P, S], U8, name="vs_picked")
        nc.vector.tensor_copy(out=vs_picked[:], in_=tabs[:].indirect(offs_sb[:]))

        def move_table_scales(a):
            for r in range(4):
                nc.sync.dma_start(
                    out=vs[a][r:P:32, :].bitcast(I32),
                    in_=vs_picked[16 * a + r : 16 * (a + 1) : 4, :].bitcast(I32),
                )

        move_table_scales(1)
        load_plain(0)
        load_table(1, AT_TABLE1)
        move_table_scales(0)
        load_plain(1)
        for s in range(2, PLAIN):
            load_plain(s)
        dealt_raw = [load_w1(2 * KP, 3 * KP, a, AT_TABLE0 + RAW_BYTES * a) for a in range(A_PASSES)]
        nc.sync.dma_start(out=gain_sb[:], in_=gain.rearrange("(b p t) -> p b t", b=B_PASSES, t=PACK))
        nc.sync.dma_start(out=bias_sb[:], in_=bias.rearrange("(g p t) -> p g t", g=GROUPS, t=PACK))

        w2w = shared.tile([P, B_PASSES * 2 * N], U8, name="w2w", offset=AT_W2, align_bytes=64)

        def deal_w2_words(b):
            run = slice(2 * N * b, 2 * N * (b + 1))
            nc.vector.tensor_copy(
                out=w2w[:, run].bitcast(U16).rearrange("p (r t c i) -> p r c t i", t=PACK, c=16, i=8),
                in_=w2w_raw[:, run].bitcast(U16).rearrange("p (r c i t) -> p r c t i", t=PACK, c=16, i=8),
            )

        deal_w2_words(0)
        w2s_dealt = shared.tile([P, N], U8, name="w2s_dealt", offset=AT_W2_SCALES, align_bytes=64)
        nc.vector.tensor_copy(
            out=w2s_dealt[:].rearrange("p (r t c i) -> p r c t i", t=PACK, c=8, i=16),
            in_=w2s_raw[:].rearrange("p (r c i t) -> p r c t i", t=PACK, c=8, i=16),
        )
        vw = [keep.tile([P, S], U32, name="vw%d" % a, align_bytes=64) for a in range(A_PASSES)]
        nc.vector.tensor_copy(out=vw[0][:], in_=tabw[0][:].bitcast(U32).indirect(offs_sb[:]))
        deal_w2_words(1)
        deal_w2_words(2)

        def copy_on(engine, dst, src):
            if engine is nc.scalar:
                nc.scalar.copy(out=dst, in_=src)
            else:
                engine.tensor_copy(out=dst, in_=src)

        w1c = {}
        w1s = {}

        def cast_plain(s, a, dst):
            nc.scalar.copy(
                out=dst.rearrange("p (c i j) -> p c j i", i=4, j=PACK),
                in_=w1_raw[s, a].rearrange("p j (c i) -> p c j i", i=4),
            )

        def cast_dealt(s, a, dst):
            nc.scalar.copy(
                out=dst.rearrange("p (t m j) -> p m j t", t=2, j=PACK),
                in_=dealt_raw[a][:].rearrange("p j (m t) -> p m j t", t=PACK)[:, :, :, s - PLAIN : s - PLAIN + 2],
            )

        quantised = []

        def ready_w1(holds):
            src = keep.tile([P, KP * len(holds)], BF16, name="w1_bf", tag="bf%d" % (len(quantised) % 4), align_bytes=64)
            codes = keep.tile([P, P * len(holds)], U32, name="w1c%d_%d" % holds[0], align_bytes=64)
            scales = keep.tile([P, P * len(holds)], U8, name="w1s%d_%d" % holds[0], align_bytes=64)
            for n, (s, a) in enumerate(holds):
                if s < PLAIN:
                    cast_plain(s, a, src[:, KP * n : KP * (n + 1)])
                elif s % 2 == 0:
                    cast_dealt(s, a, src[:, KP * n : KP * (n + 2)])
                w1c[s, a] = codes[:, P * n : P * (n + 1)]
                w1s[s, a] = scales[:, P * n : P * (n + 1)]
            nc.vector.quantize_mx(out=codes[:].bitcast(FP8X4), scales=scales[:], in_=src[:])
            quantised.append(holds)

        h = {}
        hacc = {}

        def mul_h(s, a, bank, c0, c1):
            if a == 0:
                hacc[s, c0] = psum.tile([P, c1 - c0], F32, name="hacc", tag="bank%d" % bank)
            nc.tensor.matmul_mx(
                out=hacc[s, c0][:],
                lhsT=w1c[s, a].bitcast(FP8X4),
                lhsT_scale=w1s[s, a],
                rhs=vw[a][:, c0:c1].bitcast(FP8X4),
                rhs_scale=vs[a][:, c0:c1],
                start=(a == 0),
                stop=(a == A_PASSES - 1),
            )

        def mul_w1(holds):
            for s in sorted(set(s for s, a in holds)):
                for half in range(2):
                    for a in range(A_PASSES):
                        if (s, a) in holds:
                            mul_h(s, a, 2 * (s % PACK) + half, BANK * half, BANK * (half + 1))

        def empty_bank(s, c0, engine):
            if c0 == 0 and s < PLAIN:
                h[s] = keep.tile([P, S], F32, name="h%d" % s)
            elif c0 == 0:
                h[s] = shared.tile([P, S], F32, name="h%d" % s, offset=AT_TABLE1 + 4 * S * (s - PLAIN), align_bytes=64)
            copy_on(engine, h[s][:, c0 : c0 + BANK], hacc[s, c0][:])

        def empty_h(s):
            for c0 in (0, BANK):
                empty_bank(s, c0, nc.scalar)

        def pick_second(s, dst, j0, n):
            nc.vector.tensor_copy(out=dst, in_=h[s][:].indirect(pos2_sb[:, j0 // 16 : (j0 + n) // 16]))

        def pick_diff(s, dst, second, j0, n):
            nc.vector.tensor_tensor(
                out=dst,
                in0=h[s][:].indirect(pos1_sb[:, j0 // 16 : (j0 + n) // 16]),
                in1=second,
                op=ALU.subtract,
            )

        def clamp(engine, dst, src):
            engine.tensor_scalar(out=dst, in0=src, scalar1=1.0, scalar2=-1.0, op0=ALU.min, op1=ALU.max)

        def weigh(scale, dst, src):
            nc.scalar.activation(out=dst, in_=src, func=ACT.Copy, scale=scale)

        def weave(engine, dst, src, run):
            copy_on(
                engine,
                dst.rearrange("p (c i t) -> p c t i", i=run, t=PACK),
                src.rearrange("p t (c i) -> p c t i", i=run),
            )

        zc = {}
        zs = [keep.tile([P, PAIRS], U8, name="zs%d" % b, align_bytes=64) for b in range(B_PASSES)]
        zword = {}

        def quant_z(b, j0, n):
            nc.vector.quantize_mx(
                out=zc[b][:, j0 : j0 + n].bitcast(FP8X4),
                scales=zs[b][:, j0 : j0 + n],
                in_=zword[b][:, PACK * j0 : PACK * (j0 + n)],
            )

        yacc = {}

        tiles = [(g, t) for g in range(GROUPS) for t in range(PACK)]

        def mul_z(b, some, start=False, stop=False, run=slice(0, PAIRS)):
            for g, t in some:
                if start:
                    yacc[g, t] = psum.tile([P, PAIRS], F32, name="yacc", tag="bank%d" % (PACK * g + t))
                col = N * b + g * KP + t * P
                nc.tensor.matmul_mx(
                    out=yacc[g, t][:, run],
                    lhsT=w2w[:, 2 * col : 2 * (col + P)].bitcast(FP4X4),
                    lhsT_scale=w2s[:, 2 * g + t // 2, b, P * (t % 2) : P * (t % 2 + 1)],
                    rhs=zc[b][:, run].bitcast(FP8X4),
                    rhs_scale=zs[b][:, run],
                    start=start,
                    stop=stop,
                )

        ready_w1([(0, 0), (0, 1)])
        first_cuts = ((0, 0, BANK), (1, BANK, BANK + HALF), (7, BANK + HALF, S))
        for bank, c0, c1 in first_cuts:
            mul_h(0, 0, bank, c0, c1)
        for bank, c0, c1 in first_cuts:
            nc.vector.tensor_copy(
                out=vw[1][:, c0:c1], in_=tabw[1][:].bitcast(U32).indirect(offs_sb[:, c0 // 16 : c1 // 16])
            )
            mul_h(0, 1, bank, c0, c1)
        ready_w1([(1, 0)])
        mul_w1([(1, 0)])
        h[0] = shared.tile([P, S], F32, name="h0", offset=raw_at(0, 1), align_bytes=64)
        for bank, c0, c1 in first_cuts[1:]:
            nc.vector.tensor_copy(out=h[0][:, c0:c1], in_=hacc[0, c0][:])
        ready_w1([(1, 1)])
        nc.scalar.copy(out=h[0][:, 0:BANK], in_=hacc[0, 0][:])
        mul_w1([(1, 1)])

        def eplane_at(b, t):
            if b:
                return AT_PLANES + ROW * t
            return AT_TABLE1 + ROW * (t + 1) if t < PACK - 1 else AT_TABLE1 + 3 * (4 * S) - ROW // 2

        eplane = {
            (b, t): shared.tile([P, PAIRS], F32, name="eplane%d%d" % (b, t), offset=eplane_at(b, t), align_bytes=64)
            for b in range(2)
            for t in range(PACK)
        }
        zplane = [keep.tile([P, PACK, PAIRS], BF16, name="zplane%d" % b, align_bytes=64) for b in range(2)]
        second = [keep.tile([P, PAIRS], F32, name="second", tag="second%d" % u, align_bytes=64) for u in range(2)]
        runs = (slice(0, HALF), slice(HALF, PAIRS))

        def pick_slice(s):
            b, u = divmod(s, PACK)
            if s < 3:
                picked = shared.tile([P, PAIRS], F32, name="picked%d" % s, offset=raw_at(s + 2 if s else 1, 1), align_bytes=64)
            else:
                picked = second[s % 2]
            for run in runs:
                pick_second(s, picked[:, run], run.start, HALF)
            if s == 0:
                ready_w1([(2, 0), (2, 1)])
                mul_w1([(2, 0), (2, 1)])
            if s == 0:
                diff = shared.tile([P, PAIRS], F32, name="diff0", offset=raw_at(2, 1), align_bytes=64)
            else:
                diff = keep.tile([P, PAIRS], F32, name="diff%d" % s)
            for run in runs:
                pick_diff(s, diff[:, run], picked[:, run], run.start, HALF)
            clamp(nc.gpsimd, diff[:], diff[:])
            for t in range(PACK):
                nc.sync.dma_start(out=eplane[b, t][32 * u : 32 * (u + 1), :], in_=diff[t:P:PACK, :])

        def weigh_plane(b, t):
            weigh(gain_sb[:, b, t : t + 1], zplane[b][:, t, :], eplane[b, t][:])

        last = B_PASSES - 1
        wide = keep.tile([P, PACK, WIDE], F32, name="wide")
        late_second = keep.tile([P, PACK, HALF], F32, name="late_second")

        def pick_wide(t):
            s = PACK * last + t
            spare = second[s % 2][:, 0:HALF]
            first, third = wide[:, t, 0:HALF], wide[:, t, HALF:WIDE]
            pick_second(s, spare, 0, HALF)
            pick_second(s, late_second[:, t, :], HALF, HALF)
            pick_diff(s, first, spare, 0, HALF)
            pick_diff(s, third, late_second[:, t, 0:PIECE], HALF, PIECE)
            if t < PACK - 1:
                clamp(nc.gpsimd, wide[:, t, :], wide[:, t, :])
            else:
                clamp(nc.vector, first, first)
                clamp(nc.vector, third, third)

        steps = [[(s, 0), (s, 1)] for s in range(3, PLAIN)]
        steps[-1].extend([(PLAIN, 0), (PLAIN + 1, 0)])
        steps.extend([[(s, a), (s + 1, a)] for s, a in ((PLAIN, 1), (PLAIN + 2, 0), (PLAIN + 2, 1))])
        for s in range(PLAIN):
            pick_slice(s)
            ready_w1(steps[s])
            if s == PLAIN - 1:
                weigh_plane(0, 0)
                weigh_plane(0, 1)
            empty_h(s + 1)
            mul_w1(steps[s])
        for b in range(B_PASSES):
            for r in range(4):
                nc.sync.dma_start(
                    out=w2s[r:P:32, :, b, :].bitcast(I32),
                    in_=w2s_dealt[32 * b + 2 * r : 32 * (b + 1) : 8, :].rearrange("p (u c) -> p u c", c=2 * P).bitcast(I32),
                )
        pick_wide(0)
        weigh_plane(0, 2)
        weigh_plane(0, 3)
        empty_h(9)
        pick_wide(1)
        empty_h(10)
        zword[0] = keep.tile([P, PACK * PAIRS], BF16, name="zword0", align_bytes=64)
        weave(nc.scalar, zword[0][:], zplane[0][:], 4)
        empty_h(11)
        pick_wide(2)
        zc[0] = keep.tile([P, PAIRS], U32, name="zc0", align_bytes=64)
        quant_z(0, 0, PAIRS)
        mul_z(0, tiles, start=True)
        for t in range(PACK):
            weigh_plane(1, t)
        zword[1] = keep.tile([P, PACK * PAIRS], BF16, name="zword1", align_bytes=64)
        weave(nc.scalar, zword[1][:], zplane[1][:], 4)
        pick_wide(3)
        zword[last] = keep.tile([P, PACK * PAIRS], BF16, name="zword2", align_bytes=64)
        zc[last] = keep.tile([P, PAIRS], U32, name="zc2", align_bytes=64)
        wide_plane = shared.tile([P, PACK, WIDE], BF16, name="wide_plane", offset=eplane_at(1, 1), align_bytes=64)
        for t in range(PACK):
            weigh(gain_sb[:, last, t : t + 1], wide_plane[:, t, :], wide[:, t, :])
        for j0, j1 in ((0, HALF), (HALF, WIDE)):
            weave(nc.scalar, zword[last][:, PACK * j0 : PACK * j1], wide_plane[:, :, j0:j1], 4)

        late = keep.tile([P, PACK, PIECE], F32, name="late", tag="second1", align_bytes=64)
        for t in range(PACK):
            pick_diff(PACK * last + t, late[:, t, :], late_second[:, t, PIECE:HALF], WIDE, PIECE)
        zc[1] = keep.tile([P, PAIRS], U32, name="zc1", align_bytes=64)
        quant_z(1, 0, PAIRS)
        mul_z(1, tiles[:-1])
        woven_tile = keep.tile([P, PACK * PIECE], F32, name="woven", tag="zplane1", align_bytes=64)
        woven = woven_tile[:].rearrange("p (j t) -> p j t", t=PACK)
        late_words = zword[last][:, PACK * WIDE :].rearrange("p (j t) -> p j t", t=PACK)
        late_halves = (slice(0, PIECE // 2), slice(PIECE // 2, PIECE))
        for run in late_halves:
            clamp(nc.vector, woven[:, run], late[:].rearrange("p t j -> p j t")[:, run])
        for run in late_halves:
            nc.vector.tensor_tensor(
                out=late_words[:, run],
                in0=woven[:, run],
                in1=gain_sb[:, last, :].unsqueeze(1).to_broadcast([P, PIECE // 2, PACK]),
                op=ALU.mult,
            )
        quant_z(last, 0, HALF)
        quant_z(last, HALF, HALF)
        mul_z(last, tiles[:1], run=runs[0])
        mul_z(last, tiles[:1], stop=True, run=runs[1])
        mul_z(last, tiles[1:-1], stop=True)
        mul_z(last, tiles[-1:])
        mul_z(1, tiles[-1:], stop=True)

        y = [
            shared.tile([P, PACK, PAIRS], F32, name="y%d" % g, offset=AT_TABLE0 + RAW_BYTES * g, align_bytes=64)
            for g in range(GROUPS)
        ]
        yword = [
            shared.tile([P, PACK * PAIRS], BF16, name="yword%d" % g, offset=AT_RAW0 + 2 * PACK * PAIRS * g, align_bytes=64)
            for g in range(GROUPS)
        ]
        yc = [keep.tile([P, PAIRS], U32, name="yc%d" % g, align_bytes=64) for g in range(GROUPS)]

        def add_bias(g, t, engine, run=slice(0, PAIRS)):
            if engine is nc.vector:
                nc.vector.tensor_scalar(
                    out=y[g][:, t, run], in0=yacc[g, t][:, run], scalar1=bias_sb[:, g, t : t + 1], scalar2=None, op0=ALU.add
                )
            else:
                nc.scalar.activation(
                    out=y[g][:, t, run], in_=yacc[g, t][:, run], func=ACT.Identity, bias=bias_sb[:, g, t : t + 1]
                )

        def store_y(g, t0, t1, run=slice(0, PAIRS)):
            nc.sync.dma_start(
                out=out_0[KP * g : KP * (g + 1), :].rearrange("(p t) j -> p t j", t=PACK)[:, t0:t1, run],
                in_=y[g][:, t0:t1, run],
            )

        def weave_y(engine, g, j0, j1):
            weave(engine, yword[g][:, PACK * j0 : PACK * j1], y[g][:, :, j0:j1], 1 if engine is nc.vector else 2)

        def quant_y(g, j0):
            nc.vector.quantize_mx(
                out=yc[g][:, j0 : j0 + HALF].bitcast(FP8X4),
                scales=ys[:, PAIRS * g + j0 : PAIRS * g + j0 + HALF],
                in_=yword[g][:, PACK * j0 : PACK * (j0 + HALF)],
            )

        def store_codes(g, j0, j1):
            nc.sync.dma_start(
                out=out_1[g].rearrange("p m t -> p (m t)").bitcast(I32)[:, j0:j1], in_=yc[g][:, j0:j1].bitcast(I32)
            )

        for run in runs:
            add_bias(0, 0, nc.vector, run)
            store_y(0, 0, 1, run)
        for t in range(1, PACK):
            add_bias(0, t, nc.scalar if t % 2 else nc.vector)
            if t != 2:
                store_y(0, t if t < 2 else 2, t + 1)
        add_bias(1, 0, nc.vector)
        for j0 in (0, HALF):
            weave_y(nc.vector, 0, j0, j0 + HALF)
        for t in range(1, PACK):
            add_bias(1, t, nc.scalar)
            if t % 2:
                store_y(1, t - 1, t + 1)
        for j0 in (0, HALF):
            quant_y(0, j0)
        store_codes(0, 0, PAIRS)
        weave_y(nc.vector, 1, 0, HALF)
        weave_y(nc.vector, 1, HALF, Y_SHARE)
        weave_y(nc.scalar, 1, Y_SHARE, PAIRS)
        for j0 in (0, HALF):
            quant_y(1, j0)
        store_codes(1, 0, PAIRS)
        for quad in range(4):
            nc.scalar.dma_start(
                out=out_2[:, 4 * quad : 4 * quad + 4, :].bitcast(I32).rearrange("g r m -> r g m"),
                in_=ys[32 * quad : 32 * quad + 4, :].bitcast(I32).rearrange("p (g m) -> p g m", g=GROUPS),
            )
